import numpy as np
import ml_dtypes


def mxq(x, axis, fmt="e4m3"):
    dtype, down = {"e4m3": (ml_dtypes.float8_e4m3fn, 7), "e5m2": (ml_dtypes.float8_e5m2, 14)}[fmt]
    v = np.moveaxis(np.asarray(x, np.float32).astype(ml_dtypes.bfloat16).astype(np.float64), axis, -1)
    blocks = v.reshape(v.shape[:-1] + (-1, 32))
    amax = np.abs(blocks).max(-1, keepdims=True)
    byte = np.maximum(np.where(amax > 0, np.frexp(amax)[1] - 1 + 127, 0) - down, 1)
    scale = np.exp2(byte - 127.0)
    codes = (blocks / scale).astype(np.float32).astype(dtype).astype(np.float64)
    return np.moveaxis((codes * scale).reshape(v.shape), -1, axis)


WIDE = False


def mx_kscale(k):
    if not WIDE:
        return np.ones(k)
    levels = np.array([10, -10, 5, -5, 0])
    if k % 512:
        return np.exp2(np.random.permutation(np.resize(levels, k // 32))).repeat(32)
    a = np.empty((k // 512, 16))
    for p in range(k // 512):
        a[p, :8] = np.random.permutation(np.resize(levels, 8))
        for g in range(8):
            far = levels[np.abs(levels - a[p, g]) >= 10]
            a[p, g + 8] = far[np.random.randint(len(far))]
    return np.exp2(a.ravel()).repeat(32)


def f64(x):
    return np.asarray(x).astype(np.float64)


def striped(idx):
    return np.tile(idx.reshape(-1, 16).T, (8, 1)).astype(np.uint16)


def unstriped(offs):
    return offs[:16].T.reshape(-1).astype(np.int64)


E2M1 = np.array([0.0, 0.5, 1.0, 1.5, 2.0, 3.0, 4.0, 6.0, -0.0, -0.5, -1.0, -1.5, -2.0, -3.0, -4.0, -6.0])


def pack_weight(w, fmt):
    k, n = w.shape
    w = f64(np.asarray(w, np.float32).astype(ml_dtypes.bfloat16)).reshape(k // 32, 32, n)
    amax = np.abs(w).max(1)
    if fmt == "e4m3":
        byte = np.frexp(amax)[1] - 1 + 127 - 7
    else:
        mant, ex = np.frexp(amax / 6.0)
        byte = np.where(mant > 0.5, ex, ex - 1) + 127
    byte = np.clip(np.where(amax > 0, byte, 1), 1, 254)
    scaled = (w * np.exp2(127.0 - byte)[:, None, :]).reshape(k, n).astype(np.float32)
    by_word = np.ascontiguousarray(scaled.reshape(k // 512, 128, 4, n).transpose(0, 1, 3, 2))
    if fmt == "e4m3":
        words = by_word.astype(ml_dtypes.float8_e4m3fn).view(np.uint8)
    else:
        c = by_word.astype(ml_dtypes.float4_e2m1fn).view(np.uint8) & 0xF
        words = (c[..., 0::2] | (c[..., 1::2] << 4)).reshape(k // 512, 128, 2 * n)
    return np.ascontiguousarray(words), np.ascontiguousarray(byte.astype(np.uint8).reshape(k // 512, 16, n))


def unpack_weight(words, scales, fmt):
    g, _, n = scales.shape
    words = np.ascontiguousarray(words).reshape(g, 128, n, -1)
    if fmt == "e4m3":
        vals = words.view(ml_dtypes.float8_e4m3fn).astype(np.float64)
    else:
        nib = np.empty((g, 128, n, 4), np.uint8)
        nib[..., 0::2] = words & 0xF
        nib[..., 1::2] = words >> 4
        vals = E2M1[nib]
    vals = vals * np.repeat(np.exp2(scales.astype(np.float64) - 127.0), 8, axis=1)[..., None]
    return vals.transpose(0, 1, 3, 2).reshape(g * 512, n)


def gelu(v):
    return 0.5 * v * (1.0 + np.tanh(np.sqrt(2.0 / np.pi) * (v + 0.044715 * v**3)))


K, H, N, T, S = 1024, 1024, 512, 2048, 1024

def setup_inputs():
    n = np.random.standard_normal
    s = mx_kscale(K)[:, None]
    u = mx_kscale(H)[:, None]
    tab_words, tab_scales = pack_weight(n((K, T)) * s, "e4m3")
    w2_words, w2_scales = pack_weight(n((H, N)) / np.sqrt(H) / u, "e2m1")
    return {
        "tab_words": tab_words,
        "tab_scales": tab_scales,
        "offs": striped(np.random.permutation(T)[:S]),
        "w1": (n((K, H)) / np.sqrt(K) / s).astype(np.float32),
        "opp": (np.exp(0.5 * n((H, S))) * u).astype(np.float32),
        "w2_words": w2_words,
        "w2_scales": w2_scales,
        "gT": np.exp(0.5 * n((N, T))).astype(np.float32),
        "plan": np.exp(0.5 * n(N)).astype(np.float32),
    }

def reference(tab_words, tab_scales, offs, w1, opp, w2_words, w2_scales, gT, plan):
    v = unpack_weight(tab_words, tab_scales, "e4m3")[:, unstriped(offs)]
    h = mxq(f64(w1), 0, "e4m3").T @ v
    z = np.exp(-np.abs(h)) * f64(opp)
    w2 = unpack_weight(w2_words, w2_scales, "e2m1")
    y = w2.T @ mxq(z, 0, "e4m3")
    g = f64(gT)[:, unstriped(offs)]
    new = g + y * (f64(plan)[:, None] - g)
    out = f64(gT).copy()
    out[:, unstriped(offs)] = new
    return out

@@ -1,0 +1,214 @@
+from contextlib import ExitStack
+
+import concourse.mybir as mybir
+
+K, H, N, T, S = 1024, 1024, 512, 2048, 1024
+FLOPS = 2 * K * H * S + 2 * H * N * S
+
+F32 = mybir.dt.float32
+BF16 = mybir.dt.bfloat16
+I32 = mybir.dt.int32
+U32 = mybir.dt.uint32
+U16 = mybir.dt.uint16
+U8 = mybir.dt.uint8
+FP8X4 = mybir.dt.float8_e4m3fn_x4
+FP4X4 = mybir.dt.float4_e2m1fn_x4
+ACT = mybir.ActivationFunctionType
+ALU = mybir.AluOpType
+
+P = 128
+PACK = 4
+PASS = P * PACK
+HALF = 512
+
+
+def tile_list_zoning_accessibility_step_kernel(
+    tc, tab_words, tab_scales, offs, w1, opp, w2_words, w2_scales, gT, plan, out
+):
+    nc = tc.nc
+    k_passes = K // PASS
+    r_passes = H // PASS
+    halves = S // HALF
+    n_tiles = N // P
+    list_cols = HALF // 16
+
+    with ExitStack() as ctx:
+        keep = ctx.enter_context(tc.tile_pool(name="keep", bufs=1))
+        ring = ctx.enter_context(tc.tile_pool(name="ring", bufs=2))
+        psum = ctx.enter_context(tc.psum_pool(name="psum", bufs=4))
+
+        offsets = keep.tile([P, S // 16], U16, name="offsets")
+        tab_w = [keep.tile([P, T], I32, name=f"tab_w{a}") for a in range(k_passes)]
+        tab_s = keep.tile([P, T], U8, name="tab_s")
+        w1_raw = {
+            (a, b): keep.tile([P, PACK, PASS], F32, name=f"w1_raw{a}{b}")
+            for a in range(k_passes)
+            for b in range(r_passes)
+        }
+        opp_sb = {
+            (b, h): keep.tile([P, PACK, HALF], F32, name=f"opp{b}{h}")
+            for b in range(r_passes)
+            for h in range(halves)
+        }
+        state = [keep.tile([P, T], F32, name=f"state{n}") for n in range(n_tiles)]
+        w2_w = keep.tile([P, r_passes, 2 * N], U8, name="w2_w", align_bytes=64)
+        w2_s = keep.tile([P, r_passes, N], U8, name="w2_s", align_bytes=64)
+        plan_sb = keep.tile([P, n_tiles], F32, name="plan_sb")
+
+        nc.vector.memset(tab_s[:].bitcast(I32), 0)
+        nc.vector.memset(w2_s[:].bitcast(I32), 0)
+
+        def load_tab(a):
+            nc.sync.dma_start(tab_w[a][:], tab_words[a].rearrange("p t i -> p (t i)").bitcast(I32))
+
+        def load_w1(a, b):
+            rows = w1[a * PASS : (a + 1) * PASS, b * PASS : (b + 1) * PASS]
+            nc.sync.dma_start(w1_raw[a, b][:], rows.rearrange("(p i) c -> p i c", i=PACK))
+
+        def load_opp(b, h):
+            rows = opp[b * PASS : (b + 1) * PASS, h * HALF : (h + 1) * HALF]
+            nc.sync.dma_start(opp_sb[b, h][:], rows.rearrange("(p i) j -> p i j", i=PACK))
+
+        def load_state(n):
+            nc.sync.dma_start(state[n][:], gT[n * P : (n + 1) * P, :])
+
+        load_tab(0)
+        nc.sync.dma_start(offsets[:], offs)
+        for q in range(4):
+            nc.sync.dma_start(
+                tab_s[32 * q : 32 * q + 4 * k_passes, :].bitcast(I32),
+                tab_scales[:, 4 * q : 4 * q + 4, :].bitcast(I32),
+            )
+        load_tab(1)
+        load_w1(0, 0)
+        load_w1(1, 0)
+        load_state(0)
+        with nc.allow_non_contiguous_dma(reason="one plan value a partition and row tile"):
+            nc.sync.dma_start(plan_sb[:], plan.rearrange("(n p) -> p n", p=P))
+        load_w1(0, 1)
+        load_w1(1, 1)
+        load_opp(0, 0)
+        load_state(1)
+        load_opp(1, 0)
+        nc.sync.dma_start(w2_w[:].bitcast(I32), w2_words.rearrange("a p c -> p a c").bitcast(I32))
+        for q in range(4):
+            nc.sync.dma_start(
+                w2_s[32 * q : 32 * q + 4, :, :].bitcast(I32),
+                w2_scales[:, 4 * q : 4 * q + 4, :].rearrange("a r n -> r a n").bitcast(I32),
+            )
+        load_state(2)
+        load_opp(0, 1)
+        load_opp(1, 1)
+        load_state(3)
+
+        v_w = [keep.tile([P, S], U32, name=f"v_w{a}", align_bytes=64) for a in range(k_passes)]
+        v_s = keep.tile([P, S], U8, name="v_s", align_bytes=64)
+        nc.vector.tensor_copy(v_w[0][:], tab_w[0][:].bitcast(U32).indirect(offsets[:]))
+        nc.vector.tensor_copy(v_s[:], tab_s[:].indirect(offsets[:]))
+        nc.vector.tensor_copy(v_w[1][:], tab_w[1][:].bitcast(U32).indirect(offsets[:]))
+
+        w1_w, w1_s = {}, {}
+
+        def prepare_w1(a, b, copy):
+            grouped = ring.tile([P, PASS * PACK], BF16, name="w1_grouped", align_bytes=64)
+            copy(
+                grouped[:].rearrange("p (u e m i) -> p u m i e", u=2, e=2, i=PACK),
+                w1_raw[a, b][:].rearrange("p i (m u e) -> p u m i e", u=2, e=2),
+            )
+            w1_w[a, b] = keep.tile([P, PASS], U32, name=f"w1_w{a}{b}", align_bytes=64)
+            w1_s[a, b] = keep.tile([P, PASS], U8, name=f"w1_s{a}{b}", align_bytes=64)
+            nc.vector.quantize_mx(out=w1_w[a, b][:].bitcast(FP8X4), scales=w1_s[a, b][:], in_=grouped[:])
+
+        decay = {}
+
+        def first_product(b, h):
+            decay[b, h] = keep.tile([P, PACK, HALF], F32, name=f"decay{b}{h}")
+            cols = slice(h * HALF, (h + 1) * HALF)
+            for i in range(PACK):
+                sep = psum.tile([P, HALF], F32, name="sep")
+                m = slice(i * P, (i + 1) * P)
+                for a in range(k_passes):
+                    nc.tensor.matmul_mx(
+                        out=sep[:],
+                        lhsT=w1_w[a, b][:, m].bitcast(FP8X4),
+                        lhsT_scale=w1_s[a, b][:, m],
+                        rhs=v_w[a][:, cols].bitcast(FP8X4),
+                        rhs_scale=v_s[4 * a : P, cols],
+                        start=(a == 0),
+                        stop=(a == k_passes - 1),
+                    )
+                size = ring.tile([P, HALF], F32, name="size")
+                nc.scalar.activation(size[:], sep[:], ACT.Abs)
+                nc.scalar.activation(decay[b, h][:, i, :], size[:], ACT.Exp, scale=-1.0)
+
+        z_w, z_s = {}, {}
+
+        def make_z(b, h):
+            grouped = ring.tile([P, HALF * PACK], BF16, name="z_grouped", align_bytes=64)
+            nc.vector.tensor_tensor(
+                grouped[:].rearrange("p (c e i) -> p c i e", e=2, i=PACK),
+                decay[b, h][:].rearrange("p i (c e) -> p c i e", e=2),
+                opp_sb[b, h][:].rearrange("p i (c e) -> p c i e", e=2),
+                ALU.mult,
+            )
+            z_w[b, h] = keep.tile([P, HALF], U32, name=f"z_w{b}{h}", align_bytes=64)
+            z_s[b, h] = keep.tile([P, HALF], U8, name=f"z_s{b}{h}", align_bytes=64)
+            nc.vector.quantize_mx(out=z_w[b, h][:].bitcast(FP8X4), scales=z_s[b, h][:], in_=grouped[:])
+
+        picked, gap = {}, {}
+
+        def pick_state(n):
+            picked[n] = keep.tile([P, S], F32, name=f"picked{n}")
+            nc.vector.tensor_copy(picked[n][:], state[n][:].indirect(offsets[:]))
+            gap[n] = keep.tile([P, S], F32, name=f"gap{n}")
+            nc.scalar.activation(gap[n][:], picked[n][:], ACT.Identity, bias=plan_sb[:, n : n + 1], scale=-1.0)
+
+        def second_product(h, pair):
+            steps = {n: psum.tile([P, HALF], F32, name="step") for n in pair}
+            for b in range(r_passes):
+                for n in pair:
+                    nc.tensor.matmul_mx(
+                        out=steps[n][:],
+                        lhsT=w2_w[:, b, 2 * n * P : 2 * (n + 1) * P].bitcast(FP4X4),
+                        lhsT_scale=w2_s[:, b, n * P : (n + 1) * P],
+                        rhs=z_w[b, h][:].bitcast(FP8X4),
+                        rhs_scale=z_s[b, h][:],
+                        start=(b == 0),
+                        stop=(b == r_passes - 1),
+                    )
+            return steps
+
+        def update(h, steps):
+            cols = slice(h * HALF, (h + 1) * HALF)
+            for n, step in steps.items():
+                nc.vector.tensor_tensor(gap[n][:, cols], step[:], gap[n][:, cols], ALU.mult)
+            for n in steps:
+                nc.vector.tensor_tensor(
+                    state[n][:].indirect(offsets[:, h * list_cols : (h + 1) * list_cols]),
+                    picked[n][:, cols],
+                    gap[n][:, cols],
+                    ALU.add,
+                )
+                if h == halves - 1:
+                    nc.sync.dma_start(out[n * P : (n + 1) * P, :], state[n][:])
+
+        prepare_w1(0, 0, nc.scalar.copy)
+        prepare_w1(1, 0, nc.vector.tensor_copy)
+        first_product(0, 0)
+        pick_state(0)
+        prepare_w1(0, 1, nc.vector.tensor_copy)
+        prepare_w1(1, 1, nc.vector.tensor_copy)
+        first_product(1, 0)
+        make_z(0, 0)
+        pick_state(1)
+        make_z(1, 0)
+        first_product(0, 1)
+        first_product(1, 1)
+        pick_state(2)
+        update(0, second_product(0, (0, 1)))
+        make_z(0, 1)
+        make_z(1, 1)
+        pick_state(3)
+        update(0, second_product(0, (2, 3)))
+        update(1, second_product(1, (0, 1)))
+        update(1, second_product(1, (2, 3)))

@@ -35,13 +35,16 @@ def tile_list_zoning_accessibility_step_kernel(
     with ExitStack() as ctx:
         keep = ctx.enter_context(tc.tile_pool(name="keep", bufs=1))
         ring = ctx.enter_context(tc.tile_pool(name="ring", bufs=2))
-        psum = ctx.enter_context(tc.psum_pool(name="psum", bufs=4))
+        psum = ctx.enter_context(tc.psum_pool(name="psum", bufs=1))
+
+        def held(shape, dtype, name, slot=None):
+            return keep.tile(shape, dtype, name=name, tag=slot or name, align_bytes=64)
 
         offsets = keep.tile([P, S // 16], U16, name="offsets")
-        tab_w = [keep.tile([P, T], I32, name=f"tab_w{a}") for a in range(k_passes)]
+        tab_w = [held([P, T], I32, f"tab_w{a}") for a in range(k_passes)]
         tab_s = keep.tile([P, T], U8, name="tab_s")
         w1_raw = {
-            (a, b): keep.tile([P, PACK, PASS], F32, name=f"w1_raw{a}{b}")
+            (a, b): held([P, PACK, PASS], F32, f"w1_raw{a}{b}")
             for a in range(k_passes)
             for b in range(r_passes)
         }
@@ -97,9 +100,9 @@ def tile_list_zoning_accessibility_step_kernel(
                 w2_scales[:, 4 * q : 4 * q + 4, :].rearrange("a r n -> r a n").bitcast(I32),
             )
         load_state(2)
+        load_state(3)
         load_opp(0, 1)
         load_opp(1, 1)
-        load_state(3)
 
         v_w = [keep.tile([P, S], U32, name=f"v_w{a}", align_bytes=64) for a in range(k_passes)]
         v_s = keep.tile([P, S], U8, name="v_s", align_bytes=64)
@@ -109,42 +112,50 @@ def tile_list_zoning_accessibility_step_kernel(
 
         w1_w, w1_s = {}, {}
 
-        def prepare_w1(a, b, copy):
-            grouped = ring.tile([P, PASS * PACK], BF16, name="w1_grouped", align_bytes=64)
+        def prepare_w1(a, b, copy, grouped):
             copy(
-                grouped[:].rearrange("p (u e m i) -> p u m i e", u=2, e=2, i=PACK),
+                grouped.rearrange("p (u e m i) -> p u m i e", u=2, e=2, i=PACK),
                 w1_raw[a, b][:].rearrange("p i (m u e) -> p u m i e", u=2, e=2),
             )
-            w1_w[a, b] = keep.tile([P, PASS], U32, name=f"w1_w{a}{b}", align_bytes=64)
-            w1_s[a, b] = keep.tile([P, PASS], U8, name=f"w1_s{a}{b}", align_bytes=64)
-            nc.vector.quantize_mx(out=w1_w[a, b][:].bitcast(FP8X4), scales=w1_s[a, b][:], in_=grouped[:])
+            w1_w[a, b] = held([P, PASS], U32, f"w1_w{a}{b}")
+            w1_s[a, b] = held([P, PASS], U8, f"w1_s{a}{b}")
+            nc.vector.quantize_mx(out=w1_w[a, b][:].bitcast(FP8X4), scales=w1_s[a, b][:], in_=grouped)
 
         decay = {}
 
-        def first_product(b, h):
-            decay[b, h] = keep.tile([P, PACK, HALF], F32, name=f"decay{b}{h}")
+        def first_product(b, h, banks, by_pass):
+            decay[b, h] = held([P, PACK, HALF], F32, f"decay{b}{h}")
             cols = slice(h * HALF, (h + 1) * HALF)
-            for i in range(PACK):
-                sep = psum.tile([P, HALF], F32, name="sep")
+            sep = {}
+
+            def one_pass(i, a):
+                if a == 0:
+                    sep[i] = psum.tile([P, HALF], F32, name="sep", tag=f"bank{banks[i]}")
                 m = slice(i * P, (i + 1) * P)
-                for a in range(k_passes):
-                    nc.tensor.matmul_mx(
-                        out=sep[:],
-                        lhsT=w1_w[a, b][:, m].bitcast(FP8X4),
-                        lhsT_scale=w1_s[a, b][:, m],
-                        rhs=v_w[a][:, cols].bitcast(FP8X4),
-                        rhs_scale=v_s[4 * a : P, cols],
-                        start=(a == 0),
-                        stop=(a == k_passes - 1),
-                    )
-                size = ring.tile([P, HALF], F32, name="size")
-                nc.scalar.activation(size[:], sep[:], ACT.Abs)
-                nc.scalar.activation(decay[b, h][:, i, :], size[:], ACT.Exp, scale=-1.0)
+                nc.tensor.matmul_mx(
+                    out=sep[i][:],
+                    lhsT=w1_w[a, b][:, m].bitcast(FP8X4),
+                    lhsT_scale=w1_s[a, b][:, m],
+                    rhs=v_w[a][:, cols].bitcast(FP8X4),
+                    rhs_scale=v_s[4 * a : P, cols],
+                    start=(a == 0),
+                    stop=(a == k_passes - 1),
+                )
+
+            if by_pass:
+                for i in range(PACK):
+                    one_pass(i, 0)
+            for i in range(PACK):
+                if not by_pass:
+                    one_pass(i, 0)
+                one_pass(i, 1)
+                nc.scalar.activation(decay[b, h][:, i, :], sep[i][:], ACT.Abs)
+            nc.scalar.activation(decay[b, h][:], decay[b, h][:], ACT.Exp, scale=-1.0)
 
         z_w, z_s = {}, {}
 
-        def make_z(b, h):
-            grouped = ring.tile([P, HALF * PACK], BF16, name="z_grouped", align_bytes=64)
+        def make_z(b, h, slot=None):
+            grouped = held([P, HALF * PACK], BF16, f"z_grouped{b}{h}", slot)
             nc.vector.tensor_tensor(
                 grouped[:].rearrange("p (c e i) -> p c i e", e=2, i=PACK),
                 decay[b, h][:].rearrange("p i (c e) -> p c i e", e=2),
@@ -155,60 +166,75 @@ def tile_list_zoning_accessibility_step_kernel(
             z_s[b, h] = keep.tile([P, HALF], U8, name=f"z_s{b}{h}", align_bytes=64)
             nc.vector.quantize_mx(out=z_w[b, h][:].bitcast(FP8X4), scales=z_s[b, h][:], in_=grouped[:])
 
-        picked, gap = {}, {}
+        gap = {}
 
-        def pick_state(n):
-            picked[n] = keep.tile([P, S], F32, name=f"picked{n}")
-            nc.vector.tensor_copy(picked[n][:], state[n][:].indirect(offsets[:]))
-            gap[n] = keep.tile([P, S], F32, name=f"gap{n}")
-            nc.scalar.activation(gap[n][:], picked[n][:], ACT.Identity, bias=plan_sb[:, n : n + 1], scale=-1.0)
+        def pick_state(n, picked):
+            nc.vector.tensor_copy(picked, state[n][:].indirect(offsets[:]))
+            gap[n] = held([P, S], F32, f"gap{n}", ("w1_raw00", "w1_raw10", "tab_w0", "tab_w1")[n])
+            nc.scalar.activation(gap[n][:], picked, ACT.Identity, bias=plan_sb[:, n : n + 1], scale=-1.0)
 
-        def second_product(h, pair):
-            steps = {n: psum.tile([P, HALF], F32, name="step") for n in pair}
-            for b in range(r_passes):
-                for n in pair:
-                    nc.tensor.matmul_mx(
-                        out=steps[n][:],
-                        lhsT=w2_w[:, b, 2 * n * P : 2 * (n + 1) * P].bitcast(FP4X4),
-                        lhsT_scale=w2_s[:, b, n * P : (n + 1) * P],
-                        rhs=z_w[b, h][:].bitcast(FP8X4),
-                        rhs_scale=z_s[b, h][:],
-                        start=(b == 0),
-                        stop=(b == r_passes - 1),
-                    )
-            return steps
+        steps = {}
 
-        def update(h, steps):
+        def second_product(h, n, b):
+            if b == 0:
+                steps[h, n] = psum.tile([P, HALF], F32, name="step", tag=f"bank{n}")
+            nc.tensor.matmul_mx(
+                out=steps[h, n][:],
+                lhsT=w2_w[:, b, 2 * n * P : 2 * (n + 1) * P].bitcast(FP4X4),
+                lhsT_scale=w2_s[:, b, n * P : (n + 1) * P],
+                rhs=z_w[b, h][:].bitcast(FP8X4),
+                rhs_scale=z_s[b, h][:],
+                start=(b == 0),
+                stop=(b == r_passes - 1),
+            )
+
+        def update(h, n):
             cols = slice(h * HALF, (h + 1) * HALF)
-            for n, step in steps.items():
-                nc.vector.tensor_tensor(gap[n][:, cols], step[:], gap[n][:, cols], ALU.mult)
-            for n in steps:
-                nc.vector.tensor_tensor(
-                    state[n][:].indirect(offsets[:, h * list_cols : (h + 1) * list_cols]),
-                    picked[n][:, cols],
-                    gap[n][:, cols],
-                    ALU.add,
-                )
-                if h == halves - 1:
-                    nc.sync.dma_start(out[n * P : (n + 1) * P, :], state[n][:])
+            step = steps[h, n]
+            less_one = ring.tile([P, HALF], F32, name="less_one")
+            nc.scalar.activation(less_one[:], step[:], ACT.Copy, bias=-1.0)
+            nc.gpsimd.tensor_tensor(gap[n][:, cols], less_one[:], gap[n][:, cols], ALU.mult)
+            moved = held([P, HALF], F32, f"moved{h}{n}", "decay11" if (h, n) == (0, 2) else None)
+            nc.scalar.activation(moved[:], gap[n][:, cols], ACT.Identity, bias=plan_sb[:, n : n + 1])
+            nc.vector.tensor_copy(
+                state[n][:].indirect(offsets[:, h * list_cols : (h + 1) * list_cols]),
+                moved[:],
+            )
+            if h == halves - 1:
+                nc.sync.dma_start(out[n * P : (n + 1) * P, :], state[n][:])
 
-        prepare_w1(0, 0, nc.scalar.copy)
-        prepare_w1(1, 0, nc.vector.tensor_copy)
-        first_product(0, 0)
-        pick_state(0)
-        prepare_w1(0, 1, nc.vector.tensor_copy)
-        prepare_w1(1, 1, nc.vector.tensor_copy)
-        first_product(1, 0)
-        make_z(0, 0)
-        pick_state(1)
+        def grouped_tile(name, slot):
+            return held([P, PASS * PACK], BF16, name, slot)[:]
+
+        prepare_w1(0, 0, nc.scalar.copy, grouped_tile("w1_grouped00", "chain"))
+        prepare_w1(1, 0, nc.vector.tensor_copy, grouped_tile("w1_grouped10", "chain"))
+        first_product(0, 0, (0, 1, 2, 3), True)
+        second = held([P, 2, PASS * PACK], BF16, "w1_grouped01", "chain")
+        pick_state(0, second[:, 1, :].bitcast(F32))
+        prepare_w1(0, 1, nc.vector.tensor_copy, second[:, 0, :])
+        prepare_w1(1, 1, nc.vector.tensor_copy, grouped_tile("w1_grouped11", "w1_raw01"))
+        first_product(1, 0, (4, 5, 6, 7), True)
+        make_z(0, 0, "w1_raw01")
+        for n in range(n_tiles):
+            second_product(0, n, 0)
+        picked1 = held([P, S], F32, "picked1", "w1_raw01")
+        pick_state(1, picked1[:])
         make_z(1, 0)
-        first_product(0, 1)
-        first_product(1, 1)
-        pick_state(2)
-        update(0, second_product(0, (0, 1)))
-        make_z(0, 1)
+        for n in range(n_tiles):
+            second_product(0, n, 1)
+        update(0, 0)
+        update(0, 1)
+        first_product(0, 1, (7, 6, 7, 6), False)
+        first_product(1, 1, (7, 6, 7, 6), False)
+        picked23 = held([P, 2, S], F32, "picked23", "z_grouped10")
+        pick_state(2, picked23[:, 0, :])
+        pick_state(3, picked23[:, 1, :])
+        make_z(0, 1, "moved00")
         make_z(1, 1)
-        pick_state(3)
-        update(0, second_product(0, (2, 3)))
-        update(1, second_product(1, (0, 1)))
-        update(1, second_product(1, (2, 3)))
+        update(0, 2)
+        update(0, 3)
+        for b in range(r_passes):
+            for n in range(n_tiles):
+                second_product(1, n, b)
+        for n in range(n_tiles):
+            update(1, n)

@@ -34,7 +34,6 @@ def tile_list_zoning_accessibility_step_kernel(
 
     with ExitStack() as ctx:
         keep = ctx.enter_context(tc.tile_pool(name="keep", bufs=1))
-        ring = ctx.enter_context(tc.tile_pool(name="ring", bufs=2))
         psum = ctx.enter_context(tc.psum_pool(name="psum", bufs=1))
 
         def held(shape, dtype, name, slot=None):
@@ -75,21 +74,19 @@ def tile_list_zoning_accessibility_step_kernel(
         def load_state(n):
             nc.sync.dma_start(state[n][:], gT[n * P : (n + 1) * P, :])
 
-        load_tab(0)
+        load_w1(0, 0)
         nc.sync.dma_start(offsets[:], offs)
         for q in range(4):
             nc.sync.dma_start(
                 tab_s[32 * q : 32 * q + 4 * k_passes, :].bitcast(I32),
                 tab_scales[:, 4 * q : 4 * q + 4, :].bitcast(I32),
             )
-        load_tab(1)
-        load_w1(0, 0)
+        load_tab(0)
         load_w1(1, 0)
-        load_state(0)
-        with nc.allow_non_contiguous_dma(reason="one plan value a partition and row tile"):
-            nc.sync.dma_start(plan_sb[:], plan.rearrange("(n p) -> p n", p=P))
+        load_tab(1)
         load_w1(0, 1)
         load_w1(1, 1)
+        load_state(0)
         load_opp(0, 0)
         load_state(1)
         load_opp(1, 0)
@@ -99,15 +96,17 @@ def tile_list_zoning_accessibility_step_kernel(
                 w2_s[32 * q : 32 * q + 4, :, :].bitcast(I32),
                 w2_scales[:, 4 * q : 4 * q + 4, :].rearrange("a r n -> r a n").bitcast(I32),
             )
+        with nc.allow_non_contiguous_dma(reason="one plan value a partition and row tile"):
+            nc.sync.dma_start(plan_sb[:], plan.rearrange("(n p) -> p n", p=P))
         load_state(2)
-        load_state(3)
         load_opp(0, 1)
         load_opp(1, 1)
+        load_state(3)
 
         v_w = [keep.tile([P, S], U32, name=f"v_w{a}", align_bytes=64) for a in range(k_passes)]
         v_s = keep.tile([P, S], U8, name="v_s", align_bytes=64)
-        nc.vector.tensor_copy(v_w[0][:], tab_w[0][:].bitcast(U32).indirect(offsets[:]))
         nc.vector.tensor_copy(v_s[:], tab_s[:].indirect(offsets[:]))
+        nc.vector.tensor_copy(v_w[0][:], tab_w[0][:].bitcast(U32).indirect(offsets[:]))
         nc.vector.tensor_copy(v_w[1][:], tab_w[1][:].bitcast(U32).indirect(offsets[:]))
 
         w1_w, w1_s = {}, {}
@@ -124,7 +123,7 @@ def tile_list_zoning_accessibility_step_kernel(
         decay = {}
 
         def first_product(b, h, banks, by_pass):
-            decay[b, h] = held([P, PACK, HALF], F32, f"decay{b}{h}")
+            decay[b, h] = held([P, PACK, HALF], F32, f"decay{b}{h}", "w1_raw01" if (b, h) == (0, 0) else None)
             cols = slice(h * HALF, (h + 1) * HALF)
             sep = {}
 
@@ -150,34 +149,38 @@ def tile_list_zoning_accessibility_step_kernel(
                     one_pass(i, 0)
                 one_pass(i, 1)
                 nc.scalar.activation(decay[b, h][:, i, :], sep[i][:], ACT.Abs)
-            nc.scalar.activation(decay[b, h][:], decay[b, h][:], ACT.Exp, scale=-1.0)
+            for i in range(0, PACK, 2):
+                pair = decay[b, h][:, i : i + 2, :]
+                nc.scalar.activation(pair, pair, ACT.Exp, scale=-1.0)
 
         z_w, z_s = {}, {}
 
-        def make_z(b, h, slot=None):
-            grouped = held([P, HALF * PACK], BF16, f"z_grouped{b}{h}", slot)
+        def make_z(b, h, grouped):
             nc.vector.tensor_tensor(
-                grouped[:].rearrange("p (c e i) -> p c i e", e=2, i=PACK),
+                grouped.rearrange("p (c e i) -> p c i e", e=2, i=PACK),
                 decay[b, h][:].rearrange("p i (c e) -> p c i e", e=2),
                 opp_sb[b, h][:].rearrange("p i (c e) -> p c i e", e=2),
                 ALU.mult,
             )
             z_w[b, h] = keep.tile([P, HALF], U32, name=f"z_w{b}{h}", align_bytes=64)
             z_s[b, h] = keep.tile([P, HALF], U8, name=f"z_s{b}{h}", align_bytes=64)
-            nc.vector.quantize_mx(out=z_w[b, h][:].bitcast(FP8X4), scales=z_s[b, h][:], in_=grouped[:])
+            nc.vector.quantize_mx(out=z_w[b, h][:].bitcast(FP8X4), scales=z_s[b, h][:], in_=grouped)
 
-        gap = {}
+        picked, gap = {}, {}
 
-        def pick_state(n, picked):
-            nc.vector.tensor_copy(picked, state[n][:].indirect(offsets[:]))
+        def pick_state(n, into):
+            picked[n] = into
+            nc.vector.tensor_copy(into, state[n][:].indirect(offsets[:]))
+
+        def make_gap(n):
             gap[n] = held([P, S], F32, f"gap{n}", ("w1_raw00", "w1_raw10", "tab_w0", "tab_w1")[n])
-            nc.scalar.activation(gap[n][:], picked, ACT.Identity, bias=plan_sb[:, n : n + 1], scale=-1.0)
+            nc.scalar.activation(gap[n][:], picked[n], ACT.Identity, bias=plan_sb[:, n : n + 1], scale=-1.0)
 
         steps = {}
 
         def second_product(h, n, b):
             if b == 0:
-                steps[h, n] = psum.tile([P, HALF], F32, name="step", tag=f"bank{n}")
+                steps[h, n] = psum.tile([P, HALF], F32, name="step", tag=f"bank{n_tiles * h + n}")
             nc.tensor.matmul_mx(
                 out=steps[h, n][:],
                 lhsT=w2_w[:, b, 2 * n * P : 2 * (n + 1) * P].bitcast(FP4X4),
@@ -188,53 +191,80 @@ def tile_list_zoning_accessibility_step_kernel(
                 stop=(b == r_passes - 1),
             )
 
-        def update(h, n):
-            cols = slice(h * HALF, (h + 1) * HALF)
-            step = steps[h, n]
-            less_one = ring.tile([P, HALF], F32, name="less_one")
-            nc.scalar.activation(less_one[:], step[:], ACT.Copy, bias=-1.0)
-            nc.gpsimd.tensor_tensor(gap[n][:, cols], less_one[:], gap[n][:, cols], ALU.mult)
-            moved = held([P, HALF], F32, f"moved{h}{n}", "decay11" if (h, n) == (0, 2) else None)
-            nc.scalar.activation(moved[:], gap[n][:, cols], ACT.Identity, bias=plan_sb[:, n : n + 1])
-            nc.vector.tensor_copy(
-                state[n][:].indirect(offsets[:, h * list_cols : (h + 1) * list_cols]),
-                moved[:],
-            )
-            if h == halves - 1:
-                nc.sync.dma_start(out[n * P : (n + 1) * P, :], state[n][:])
+        move = {}
+
+        def half(h):
+            return slice(h * HALF, (h + 1) * HALF)
+
+        def make_move(h, n):
+            nc.vector.tensor_tensor(move[n][:, half(h)], steps[h, n][:], gap[n][:, half(h)], ALU.mult)
+
+        def put(n, first, second, entries):
+            nc.vector.tensor_tensor(state[n][:].indirect(entries), first, second, ALU.add)
+
+        def put_half(h, n):
+            entries = offsets[:, h * list_cols : (h + 1) * list_cols]
+            put(n, picked[n][:, half(h)], move[n][:, half(h)], entries)
+
+        def store(n):
+            nc.sync.dma_start(out[n * P : (n + 1) * P, :], state[n][:])
+
+        def split_step(h, n):
+            nc.scalar.activation(kept_share[:, half(h)], steps[h, n][:], ACT.Copy, bias=1.0, scale=-1.0)
+            nc.scalar.activation(toward_plan[:, half(h)], steps[h, n][:], ACT.Copy, scale=plan_sb[:, n : n + 1])
 
         def grouped_tile(name, slot):
             return held([P, PASS * PACK], BF16, name, slot)[:]
 
-        prepare_w1(0, 0, nc.scalar.copy, grouped_tile("w1_grouped00", "chain"))
-        prepare_w1(1, 0, nc.vector.tensor_copy, grouped_tile("w1_grouped10", "chain"))
+        prepare_w1(0, 0, nc.scalar.copy, grouped_tile("w1_grouped00", None))
+        prepare_w1(1, 0, nc.scalar.copy, grouped_tile("w1_grouped10", "chain"))
+        prepare_w1(0, 1, nc.scalar.copy, grouped_tile("w1_grouped01", None))
+        prepare_w1(1, 1, nc.vector.tensor_copy, grouped_tile("w1_grouped11", "chain"))
         first_product(0, 0, (0, 1, 2, 3), True)
-        second = held([P, 2, PASS * PACK], BF16, "w1_grouped01", "chain")
-        pick_state(0, second[:, 1, :].bitcast(F32))
-        prepare_w1(0, 1, nc.vector.tensor_copy, second[:, 0, :])
-        prepare_w1(1, 1, nc.vector.tensor_copy, grouped_tile("w1_grouped11", "w1_raw01"))
         first_product(1, 0, (4, 5, 6, 7), True)
-        make_z(0, 0, "w1_raw01")
-        for n in range(n_tiles):
-            second_product(0, n, 0)
+        both = held([P, 2, PASS * PACK], BF16, "picked0_and_z", "chain")
+        pick_state(0, both[:, 1, :].bitcast(F32))
         picked1 = held([P, S], F32, "picked1", "w1_raw01")
+        make_z(0, 0, both[:, 0, :])
         pick_state(1, picked1[:])
-        make_z(1, 0)
+        make_z(1, 0, grouped_tile("z_grouped10", None))
+        make_gap(0)
+        make_gap(1)
+        first_product(0, 1, (0, 1, 2, 3), False)
+        first_product(1, 1, (4, 5, 6, 7), False)
         for n in range(n_tiles):
-            second_product(0, n, 1)
-        update(0, 0)
-        update(0, 1)
-        first_product(0, 1, (7, 6, 7, 6), False)
-        first_product(1, 1, (7, 6, 7, 6), False)
-        picked23 = held([P, 2, S], F32, "picked23", "z_grouped10")
-        pick_state(2, picked23[:, 0, :])
-        pick_state(3, picked23[:, 1, :])
-        make_z(0, 1, "moved00")
-        make_z(1, 1)
-        update(0, 2)
-        update(0, 3)
+            for b in range(r_passes):
+                second_product(0, n, b)
+        picked2 = held([P, S], F32, "picked2", "z_grouped10")
+        pick_state(2, picked2[:])
+        move[0] = held([P, S], F32, "move0")
+        make_move(0, 0)
+        put_half(0, 0)
+        make_gap(2)
+        kept_share = held([P, S], F32, "kept_share")
+        toward_plan = held([P, S], F32, "toward_plan")
+        split_step(0, 3)
+        make_z(0, 1, grouped_tile("z_grouped01", None))
+        move[1] = held([P, S], F32, "move1", "decay11")
+        make_z(1, 1, grouped_tile("z_grouped11", None))
+        make_move(0, 1)
+        put_half(0, 1)
         for b in range(r_passes):
             for n in range(n_tiles):
                 second_product(1, n, b)
-        for n in range(n_tiles):
-            update(1, n)
+        split_step(1, 3)
+        move[2] = held([P, S], F32, "move2")
+        make_move(0, 2)
+        make_move(1, 0)
+        make_move(1, 1)
+        put_half(1, 0)
+        store(0)
+        make_move(1, 2)
+        put_half(1, 1)
+        store(1)
+        move[3] = held([P, S], F32, "move3")
+        nc.vector.tensor_tensor(move[3][:], state[3][:].indirect(offsets[:]), kept_share[:], ALU.mult)
+        put(2, picked[2], move[2][:], offsets[:])
+        store(2)
+        put(3, toward_plan[:], move[3][:], offsets[:])
+        store(3)

@@ -98,9 +98,9 @@ def tile_list_zoning_accessibility_step_kernel(
             )
         with nc.allow_non_contiguous_dma(reason="one plan value a partition and row tile"):
             nc.sync.dma_start(plan_sb[:], plan.rearrange("(n p) -> p n", p=P))
-        load_state(2)
         load_opp(0, 1)
         load_opp(1, 1)
+        load_state(2)
         load_state(3)
 
         v_w = [keep.tile([P, S], U32, name=f"v_w{a}", align_bytes=64) for a in range(k_passes)]
@@ -162,6 +162,8 @@ def tile_list_zoning_accessibility_step_kernel(
                 opp_sb[b, h][:].rearrange("p i (c e) -> p c i e", e=2),
                 ALU.mult,
             )
+
+        def quantize_z(b, h, grouped):
             z_w[b, h] = keep.tile([P, HALF], U32, name=f"z_w{b}{h}", align_bytes=64)
             z_s[b, h] = keep.tile([P, HALF], U8, name=f"z_s{b}{h}", align_bytes=64)
             nc.vector.quantize_mx(out=z_w[b, h][:].bitcast(FP8X4), scales=z_s[b, h][:], in_=grouped)
@@ -173,7 +175,7 @@ def tile_list_zoning_accessibility_step_kernel(
             nc.vector.tensor_copy(into, state[n][:].indirect(offsets[:]))
 
         def make_gap(n):
-            gap[n] = held([P, S], F32, f"gap{n}", ("w1_raw00", "w1_raw10", "tab_w0", "tab_w1")[n])
+            gap[n] = held([P, S], F32, f"gap{n}", f"w1_raw{n}0")
             nc.scalar.activation(gap[n][:], picked[n], ACT.Identity, bias=plan_sb[:, n : n + 1], scale=-1.0)
 
         steps = {}
@@ -210,8 +212,12 @@ def tile_list_zoning_accessibility_step_kernel(
             nc.sync.dma_start(out[n * P : (n + 1) * P, :], state[n][:])
 
         def split_step(h, n):
-            nc.scalar.activation(kept_share[:, half(h)], steps[h, n][:], ACT.Copy, bias=1.0, scale=-1.0)
-            nc.scalar.activation(toward_plan[:, half(h)], steps[h, n][:], ACT.Copy, scale=plan_sb[:, n : n + 1])
+            nc.scalar.activation(parts[n][:, 0, half(h)], steps[h, n][:], ACT.Copy, bias=1.0, scale=-1.0)
+            nc.scalar.activation(parts[n][:, 1, half(h)], steps[h, n][:], ACT.Copy, scale=plan_sb[:, n : n + 1])
+
+        def pick_and_shrink(n):
+            move[n] = held([P, S], F32, f"move{n}")
+            nc.vector.tensor_tensor(move[n][:], state[n][:].indirect(offsets[:]), parts[n][:, 0, :], ALU.mult)
 
         def grouped_tile(name, slot):
             return held([P, PASS * PACK], BF16, name, slot)[:]
@@ -224,47 +230,45 @@ def tile_list_zoning_accessibility_step_kernel(
         first_product(1, 0, (4, 5, 6, 7), True)
         both = held([P, 2, PASS * PACK], BF16, "picked0_and_z", "chain")
         pick_state(0, both[:, 1, :].bitcast(F32))
-        picked1 = held([P, S], F32, "picked1", "w1_raw01")
         make_z(0, 0, both[:, 0, :])
-        pick_state(1, picked1[:])
-        make_z(1, 0, grouped_tile("z_grouped10", None))
+        quantize_z(0, 0, both[:, 0, :])
+        pick_state(1, held([P, S], F32, "picked1")[:])
+        z_grouped = {(b, h): grouped_tile(f"z_grouped{b}{h}", None) for b, h in ((1, 0), (0, 1), (1, 1))}
+        make_z(1, 0, z_grouped[1, 0])
+        quantize_z(1, 0, z_grouped[1, 0])
+        first_product(0, 1, (0, 1, 2, 3), False)
         make_gap(0)
         make_gap(1)
-        first_product(0, 1, (0, 1, 2, 3), False)
         first_product(1, 1, (4, 5, 6, 7), False)
         for n in range(n_tiles):
             for b in range(r_passes):
                 second_product(0, n, b)
-        picked2 = held([P, S], F32, "picked2", "z_grouped10")
-        pick_state(2, picked2[:])
+        parts = {n: held([P, 2, S], F32, f"parts{n}", f"tab_w{n - 2}") for n in (2, 3)}
+        split_step(0, 2)
+        split_step(0, 3)
+        make_z(0, 1, z_grouped[0, 1])
         move[0] = held([P, S], F32, "move0")
         make_move(0, 0)
+        quantize_z(0, 1, z_grouped[0, 1])
         put_half(0, 0)
-        make_gap(2)
-        kept_share = held([P, S], F32, "kept_share")
-        toward_plan = held([P, S], F32, "toward_plan")
-        split_step(0, 3)
-        make_z(0, 1, grouped_tile("z_grouped01", None))
+        make_z(1, 1, z_grouped[1, 1])
         move[1] = held([P, S], F32, "move1", "decay11")
-        make_z(1, 1, grouped_tile("z_grouped11", None))
         make_move(0, 1)
+        quantize_z(1, 1, z_grouped[1, 1])
         put_half(0, 1)
         for b in range(r_passes):
             for n in range(n_tiles):
                 second_product(1, n, b)
+        split_step(1, 2)
         split_step(1, 3)
-        move[2] = held([P, S], F32, "move2")
-        make_move(0, 2)
         make_move(1, 0)
         make_move(1, 1)
         put_half(1, 0)
         store(0)
-        make_move(1, 2)
         put_half(1, 1)
         store(1)
-        move[3] = held([P, S], F32, "move3")
-        nc.vector.tensor_tensor(move[3][:], state[3][:].indirect(offsets[:]), kept_share[:], ALU.mult)
-        put(2, picked[2], move[2][:], offsets[:])
-        store(2)
-        put(3, toward_plan[:], move[3][:], offsets[:])
-        store(3)
+        pick_and_shrink(2)
+        pick_and_shrink(3)
+        for n in (2, 3):
+            put(n, parts[n][:, 1, :], move[n][:], offsets[:])
+            store(n)

@@ -20,6 +20,8 @@ P = 128
 PACK = 4
 PASS = P * PACK
 HALF = 512
+STRIP = 128
+SHARE = 84
 
 
 def tile_list_zoning_accessibility_step_kernel(
@@ -28,9 +30,8 @@ def tile_list_zoning_accessibility_step_kernel(
     nc = tc.nc
     k_passes = K // PASS
     r_passes = H // PASS
-    halves = S // HALF
     n_tiles = N // P
-    list_cols = HALF // 16
+    strips = HALF // STRIP
 
     with ExitStack() as ctx:
         keep = ctx.enter_context(tc.tile_pool(name="keep", bufs=1))
@@ -38,6 +39,12 @@ def tile_list_zoning_accessibility_step_kernel(
 
         def held(shape, dtype, name, slot=None):
             return keep.tile(shape, dtype, name=name, tag=slot or name, align_bytes=64)
+
+        def bank(shape, index, name):
+            return psum.tile(shape, F32, name=name, tag=f"bank{index}")
+
+        def half(h):
+            return slice(h * HALF, (h + 1) * HALF)
 
         offsets = keep.tile([P, S // 16], U16, name="offsets")
         tab_w = [held([P, T], I32, f"tab_w{a}") for a in range(k_passes)]
@@ -50,7 +57,7 @@ def tile_list_zoning_accessibility_step_kernel(
         opp_sb = {
             (b, h): keep.tile([P, PACK, HALF], F32, name=f"opp{b}{h}")
             for b in range(r_passes)
-            for h in range(halves)
+            for h in range(2)
         }
         state = [keep.tile([P, T], F32, name=f"state{n}") for n in range(n_tiles)]
         w2_w = keep.tile([P, r_passes, 2 * N], U8, name="w2_w", align_bytes=64)
@@ -68,27 +75,25 @@ def tile_list_zoning_accessibility_step_kernel(
             nc.sync.dma_start(w1_raw[a, b][:], rows.rearrange("(p i) c -> p i c", i=PACK))
 
         def load_opp(b, h):
-            rows = opp[b * PASS : (b + 1) * PASS, h * HALF : (h + 1) * HALF]
+            rows = opp[b * PASS : (b + 1) * PASS, half(h)]
             nc.sync.dma_start(opp_sb[b, h][:], rows.rearrange("(p i) j -> p i j", i=PACK))
 
         def load_state(n):
             nc.sync.dma_start(state[n][:], gT[n * P : (n + 1) * P, :])
 
-        load_w1(0, 0)
+        load_tab(0)
         nc.sync.dma_start(offsets[:], offs)
         for q in range(4):
             nc.sync.dma_start(
                 tab_s[32 * q : 32 * q + 4 * k_passes, :].bitcast(I32),
                 tab_scales[:, 4 * q : 4 * q + 4, :].bitcast(I32),
             )
-        load_tab(0)
-        load_w1(1, 0)
+        load_w1(0, 0)
         load_tab(1)
+        load_w1(1, 0)
         load_w1(0, 1)
         load_w1(1, 1)
-        load_state(0)
         load_opp(0, 0)
-        load_state(1)
         load_opp(1, 0)
         nc.sync.dma_start(w2_w[:].bitcast(I32), w2_words.rearrange("a p c -> p a c").bitcast(I32))
         for q in range(4):
@@ -98,177 +103,203 @@ def tile_list_zoning_accessibility_step_kernel(
             )
         with nc.allow_non_contiguous_dma(reason="one plan value a partition and row tile"):
             nc.sync.dma_start(plan_sb[:], plan.rearrange("(n p) -> p n", p=P))
+        load_state(0)
+        load_state(1)
         load_opp(0, 1)
         load_opp(1, 1)
         load_state(2)
         load_state(3)
 
-        v_w = [keep.tile([P, S], U32, name=f"v_w{a}", align_bytes=64) for a in range(k_passes)]
+        v_w0 = held([P, S], U32, "v_w0")
+        v_w = {(0, h): v_w0[:, half(h)] for h in range(2)}
+        v_w[1, 0] = held([P, HALF], U32, "v_w10")[:]
         v_s = keep.tile([P, S], U8, name="v_s", align_bytes=64)
         nc.vector.tensor_copy(v_s[:], tab_s[:].indirect(offsets[:]))
-        nc.vector.tensor_copy(v_w[0][:], tab_w[0][:].bitcast(U32).indirect(offsets[:]))
-        nc.vector.tensor_copy(v_w[1][:], tab_w[1][:].bitcast(U32).indirect(offsets[:]))
+        nc.vector.tensor_copy(v_w0[:], tab_w[0][:].bitcast(U32).indirect(offsets[:]))
+        nc.vector.tensor_copy(v_w[1, 0], tab_w[1][:].bitcast(U32).indirect(offsets[:, 0 : HALF // 16]))
 
         w1_w, w1_s = {}, {}
+        whole = slice(0, HALF)
 
-        def prepare_w1(a, b, copy, grouped):
-            copy(
-                grouped.rearrange("p (u e m i) -> p u m i e", u=2, e=2, i=PACK),
-                w1_raw[a, b][:].rearrange("p i (m u e) -> p u m i e", u=2, e=2),
-            )
+        def prepare_w1(a, b, on_vector):
+            grouped = held([P, PASS * PACK], BF16, f"w1_grouped{a}{b}")
+            into = grouped[:].rearrange("p (u e m i) -> p u m i e", u=2, e=2, i=PACK)
+            source = w1_raw[a, b][:].rearrange("p i (m u e) -> p u m i e", u=2, e=2)
+            if on_vector > 0:
+                nc.vector.tensor_copy(into[:, :, :on_vector], source[:, :, :on_vector])
+            if on_vector < P:
+                nc.scalar.copy(into[:, :, on_vector:], source[:, :, on_vector:])
             w1_w[a, b] = held([P, PASS], U32, f"w1_w{a}{b}")
             w1_s[a, b] = held([P, PASS], U8, f"w1_s{a}{b}")
-            nc.vector.quantize_mx(out=w1_w[a, b][:].bitcast(FP8X4), scales=w1_s[a, b][:], in_=grouped)
+            nc.vector.quantize_mx(out=w1_w[a, b][:].bitcast(FP8X4), scales=w1_s[a, b][:], in_=grouped[:])
 
-        decay = {}
+        def first_pass(into, a, b, i, h, cols, start, stop):
+            m = slice(i * P, (i + 1) * P)
+            nc.tensor.matmul_mx(
+                out=into,
+                lhsT=w1_w[a, b][:, m].bitcast(FP8X4),
+                lhsT_scale=w1_s[a, b][:, m],
+                rhs=v_w[a, h][:, cols].bitcast(FP8X4),
+                rhs_scale=v_s[4 * a : P, h * HALF + cols.start : h * HALF + cols.stop],
+                start=start,
+                stop=stop,
+            )
 
-        def first_product(b, h, banks, by_pass):
-            decay[b, h] = held([P, PACK, HALF], F32, f"decay{b}{h}", "w1_raw01" if (b, h) == (0, 0) else None)
-            cols = slice(h * HALF, (h + 1) * HALF)
-            sep = {}
-
-            def one_pass(i, a):
-                if a == 0:
-                    sep[i] = psum.tile([P, HALF], F32, name="sep", tag=f"bank{banks[i]}")
-                m = slice(i * P, (i + 1) * P)
-                nc.tensor.matmul_mx(
-                    out=sep[i][:],
-                    lhsT=w1_w[a, b][:, m].bitcast(FP8X4),
-                    lhsT_scale=w1_s[a, b][:, m],
-                    rhs=v_w[a][:, cols].bitcast(FP8X4),
-                    rhs_scale=v_s[4 * a : P, cols],
-                    start=(a == 0),
-                    stop=(a == k_passes - 1),
-                )
-
-            if by_pass:
-                for i in range(PACK):
-                    one_pass(i, 0)
+        def decay_wide(b, h, banks, slot):
+            decay = held([P, PACK, HALF], F32, f"decay{b}{h}", slot)
+            sep = [bank([P, HALF], banks[i], "sep") for i in range(PACK)]
             for i in range(PACK):
-                if not by_pass:
-                    one_pass(i, 0)
-                one_pass(i, 1)
-                nc.scalar.activation(decay[b, h][:, i, :], sep[i][:], ACT.Abs)
+                first_pass(sep[i][:], 0, b, i, h, whole, True, False)
+                first_pass(sep[i][:], 1, b, i, h, whole, False, True)
+                nc.scalar.activation(decay[:, i, :], sep[i][:], ACT.Abs)
+            return decay
+
+        def discount(decay):
             for i in range(0, PACK, 2):
-                pair = decay[b, h][:, i : i + 2, :]
+                pair = decay[:, i : i + 2, :]
                 nc.scalar.activation(pair, pair, ACT.Exp, scale=-1.0)
 
-        z_w, z_s = {}, {}
+        z_grouped = {(b, h): held([P, HALF * PACK], BF16, f"z_grouped{b}{h}") for b in range(2) for h in range(2)}
+        z_w = {(b, h): held([P, HALF], U32, f"z_w{b}{h}") for b in range(2) for h in range(2)}
+        z_s = {(b, h): held([P, HALF], U8, f"z_s{b}{h}") for b in range(2) for h in range(2)}
 
-        def make_z(b, h, grouped):
+        def make_z(b, h, decay, cols):
+            grouped = z_grouped[b, h][:, PACK * cols.start : PACK * cols.stop]
             nc.vector.tensor_tensor(
                 grouped.rearrange("p (c e i) -> p c i e", e=2, i=PACK),
-                decay[b, h][:].rearrange("p i (c e) -> p c i e", e=2),
-                opp_sb[b, h][:].rearrange("p i (c e) -> p c i e", e=2),
+                decay.rearrange("p i (c e) -> p c i e", e=2),
+                opp_sb[b, h][:, :, cols].rearrange("p i (c e) -> p c i e", e=2),
                 ALU.mult,
             )
 
-        def quantize_z(b, h, grouped):
-            z_w[b, h] = keep.tile([P, HALF], U32, name=f"z_w{b}{h}", align_bytes=64)
-            z_s[b, h] = keep.tile([P, HALF], U8, name=f"z_s{b}{h}", align_bytes=64)
-            nc.vector.quantize_mx(out=z_w[b, h][:].bitcast(FP8X4), scales=z_s[b, h][:], in_=grouped)
+        def quantize_z(b, h, cols):
+            grouped = z_grouped[b, h][:, PACK * cols.start : PACK * cols.stop]
+            nc.vector.quantize_mx(out=z_w[b, h][:, cols].bitcast(FP8X4), scales=z_s[b, h][:, cols], in_=grouped)
 
-        picked, gap = {}, {}
-
-        def pick_state(n, into):
-            picked[n] = into
-            nc.vector.tensor_copy(into, state[n][:].indirect(offsets[:]))
-
-        def make_gap(n):
-            gap[n] = held([P, S], F32, f"gap{n}", f"w1_raw{n}0")
-            nc.scalar.activation(gap[n][:], picked[n], ACT.Identity, bias=plan_sb[:, n : n + 1], scale=-1.0)
-
-        steps = {}
-
-        def second_product(h, n, b):
-            if b == 0:
-                steps[h, n] = psum.tile([P, HALF], F32, name="step", tag=f"bank{n_tiles * h + n}")
+        def second_pass(into, n, b, h, cols, start, stop):
             nc.tensor.matmul_mx(
-                out=steps[h, n][:],
+                out=into,
                 lhsT=w2_w[:, b, 2 * n * P : 2 * (n + 1) * P].bitcast(FP4X4),
                 lhsT_scale=w2_s[:, b, n * P : (n + 1) * P],
-                rhs=z_w[b, h][:].bitcast(FP8X4),
-                rhs_scale=z_s[b, h][:],
-                start=(b == 0),
-                stop=(b == r_passes - 1),
+                rhs=z_w[b, h][:, cols].bitcast(FP8X4),
+                rhs_scale=z_s[b, h][:, cols],
+                start=start,
+                stop=stop,
             )
 
-        move = {}
+        steps, remain, pull, shrunk = {}, {}, {}, {}
 
-        def half(h):
-            return slice(h * HALF, (h + 1) * HALF)
+        def step_wide(n, h, index):
+            steps[n, h] = bank([P, HALF], index, "step")
+            for b in range(r_passes):
+                second_pass(steps[n, h][:], n, b, h, whole, b == 0, b == r_passes - 1)
 
-        def make_move(h, n):
-            nc.vector.tensor_tensor(move[n][:, half(h)], steps[h, n][:], gap[n][:, half(h)], ALU.mult)
+        def make_remain(key, one=None):
+            remain[key] = held(list(steps[key].shape), F32, f"remain{key[0]}{key[1]}")
+            if one is None:
+                nc.scalar.activation(remain[key][:], steps[key][:], ACT.Copy, bias=1.0, scale=-1.0)
+            else:
+                nc.scalar.activation(remain[key][:], steps[key][:], ACT.Identity, bias=one, scale=-1.0)
 
-        def put(n, first, second, entries):
-            nc.vector.tensor_tensor(state[n][:].indirect(entries), first, second, ALU.add)
+        def make_pull(key):
+            pull[key] = held(list(steps[key].shape), F32, f"pull{key[0]}{key[1]}")
+            n = key[0]
+            nc.scalar.activation(pull[key][:], steps[key][:], ACT.Copy, scale=plan_sb[:, n : n + 1])
 
-        def put_half(h, n):
-            entries = offsets[:, h * list_cols : (h + 1) * list_cols]
-            put(n, picked[n][:, half(h)], move[n][:, half(h)], entries)
+        def entries(first, count):
+            return offsets[:, first // 16 : (first + count) // 16]
+
+        def pick(key, first):
+            count = steps[key].shape[1]
+            shrunk[key] = held([P, count], F32, f"shrunk{key[0]}{key[1]}")
+            nc.vector.tensor_tensor(
+                shrunk[key][:], state[key[0]][:].indirect(entries(first, count)), remain[key][:], ALU.mult
+            )
+
+        def put(key, first):
+            count = steps[key].shape[1]
+            nc.vector.tensor_tensor(
+                state[key[0]][:].indirect(entries(first, count)), shrunk[key][:], pull[key][:], ALU.add
+            )
 
         def store(n):
             nc.sync.dma_start(out[n * P : (n + 1) * P, :], state[n][:])
 
-        def split_step(h, n):
-            nc.scalar.activation(parts[n][:, 0, half(h)], steps[h, n][:], ACT.Copy, bias=1.0, scale=-1.0)
-            nc.scalar.activation(parts[n][:, 1, half(h)], steps[h, n][:], ACT.Copy, scale=plan_sb[:, n : n + 1])
+        prepare_w1(0, 0, 0)
+        prepare_w1(1, 0, SHARE)
+        v_w[1, 1] = held([P, HALF], U32, "v_w11", "w1_grouped10")[:]
+        nc.vector.tensor_copy(v_w[1, 1], tab_w[1][:].bitcast(U32).indirect(offsets[:, HALF // 16 : S // 16]))
+        prepare_w1(0, 1, P)
+        prepare_w1(1, 1, P)
 
-        def pick_and_shrink(n):
-            move[n] = held([P, S], F32, f"move{n}")
-            nc.vector.tensor_tensor(move[n][:], state[n][:].indirect(offsets[:]), parts[n][:, 0, :], ALU.mult)
+        decay00 = decay_wide(0, 0, (0, 1, 2, 3), "w1_raw00")
+        discount(decay00)
 
-        def grouped_tile(name, slot):
-            return held([P, PASS * PACK], BF16, name, slot)[:]
+        decay10 = held([P, strips, PACK, STRIP], F32, "decay10", "w1_raw10")
+        sep10 = [bank([P, PACK, STRIP], 4 + c, "sep10") for c in range(strips)]
+        strip = [slice(c * STRIP, (c + 1) * STRIP) for c in range(strips)]
+        for c in range(strips):
+            for i in range(PACK):
+                first_pass(sep10[c][:, i, :], 0, 1, i, 0, strip[c], i == 0, False)
+            for i in range(PACK):
+                first_pass(sep10[c][:, i, :], 1, 1, i, 0, strip[c], False, i == PACK - 1)
+            nc.scalar.activation(decay10[:, c], sep10[c][:], ACT.Abs)
+            nc.scalar.activation(decay10[:, c], decay10[:, c], ACT.Exp, scale=-1.0)
 
-        prepare_w1(0, 0, nc.scalar.copy, grouped_tile("w1_grouped00", None))
-        prepare_w1(1, 0, nc.scalar.copy, grouped_tile("w1_grouped10", "chain"))
-        prepare_w1(0, 1, nc.scalar.copy, grouped_tile("w1_grouped01", None))
-        prepare_w1(1, 1, nc.vector.tensor_copy, grouped_tile("w1_grouped11", "chain"))
-        first_product(0, 0, (0, 1, 2, 3), True)
-        first_product(1, 0, (4, 5, 6, 7), True)
-        both = held([P, 2, PASS * PACK], BF16, "picked0_and_z", "chain")
-        pick_state(0, both[:, 1, :].bitcast(F32))
-        make_z(0, 0, both[:, 0, :])
-        quantize_z(0, 0, both[:, 0, :])
-        pick_state(1, held([P, S], F32, "picked1")[:])
-        z_grouped = {(b, h): grouped_tile(f"z_grouped{b}{h}", None) for b, h in ((1, 0), (0, 1), (1, 1))}
-        make_z(1, 0, z_grouped[1, 0])
-        quantize_z(1, 0, z_grouped[1, 0])
-        first_product(0, 1, (0, 1, 2, 3), False)
-        make_gap(0)
-        make_gap(1)
-        first_product(1, 1, (4, 5, 6, 7), False)
+        make_z(0, 0, decay00[:], whole)
+        quantize_z(0, 0, whole)
+        for u, name in enumerate("ab"):
+            steps[0, name] = bank([P, 2 * STRIP], u, "step")
+            for c in (2 * u, 2 * u + 1):
+                second_pass(steps[0, name][:, strip[c % 2]], 0, 0, 0, strip[c], c % 2 == 0, False)
+        for c in range(strips):
+            make_z(1, 0, decay10[:, c], strip[c])
+            quantize_z(1, 0, strip[c])
+            second_pass(steps[0, "ab"[c // 2]][:, strip[c % 2]], 0, 1, 0, strip[c], False, c % 2 == 1)
+        one = held([P, 1], F32, "one", "w1_raw01")
+        nc.gpsimd.memset(one[:], 1.0)
+        make_remain((0, "a"), one[:])
+        make_pull((0, "a"))
+        pick((0, "a"), 0)
+        put((0, "a"), 0)
+        make_remain((0, "b"))
+        make_pull((0, "b"))
+        step_wide(1, 0, 2)
+        make_remain((1, 0))
+        make_pull((1, 0))
+        pick((0, "b"), 2 * STRIP)
+        pick((1, 0), 0)
+        put((0, "b"), 2 * STRIP)
+        put((1, 0), 0)
+
+        decay01 = decay_wide(0, 1, (4, 5, 6, 7), "w1_raw01")
+        discount(decay01)
+        decay11 = decay_wide(1, 1, (4, 5, 6, 7), "w1_raw11")
+        discount(decay11)
+        step_wide(2, 0, 3)
+        step_wide(3, 0, 0)
+        make_remain((2, 0))
+        make_remain((3, 0))
+        make_pull((2, 0))
+        make_pull((3, 0))
+        make_z(0, 1, decay01[:], whole)
+        make_z(1, 1, decay11[:], whole)
+        quantize_z(0, 1, whole)
+        pick((2, 0), 0)
+        quantize_z(1, 1, whole)
+        pick((3, 0), 0)
+        put((2, 0), 0)
+        put((3, 0), 0)
+
         for n in range(n_tiles):
-            for b in range(r_passes):
-                second_product(0, n, b)
-        parts = {n: held([P, 2, S], F32, f"parts{n}", f"tab_w{n - 2}") for n in (2, 3)}
-        split_step(0, 2)
-        split_step(0, 3)
-        make_z(0, 1, z_grouped[0, 1])
-        move[0] = held([P, S], F32, "move0")
-        make_move(0, 0)
-        quantize_z(0, 1, z_grouped[0, 1])
-        put_half(0, 0)
-        make_z(1, 1, z_grouped[1, 1])
-        move[1] = held([P, S], F32, "move1", "decay11")
-        make_move(0, 1)
-        quantize_z(1, 1, z_grouped[1, 1])
-        put_half(0, 1)
-        for b in range(r_passes):
-            for n in range(n_tiles):
-                second_product(1, n, b)
-        split_step(1, 2)
-        split_step(1, 3)
-        make_move(1, 0)
-        make_move(1, 1)
-        put_half(1, 0)
-        store(0)
-        put_half(1, 1)
-        store(1)
-        pick_and_shrink(2)
-        pick_and_shrink(3)
-        for n in (2, 3):
-            put(n, parts[n][:, 1, :], move[n][:], offsets[:])
-            store(n)
+            step_wide(n, 1, 4 + n)
+        for pair in ((0, 1), (2, 3)):
+            for n in pair:
+                make_remain((n, 1))
+            for n in pair:
+                make_pull((n, 1))
+            for n in pair:
+                pick((n, 1), HALF)
+            for n in pair:
+                put((n, 1), HALF)
+                store(n)

@@ -94,7 +94,6 @@ def tile_list_zoning_accessibility_step_kernel(
         load_w1(0, 1)
         load_w1(1, 1)
         load_opp(0, 0)
-        load_opp(1, 0)
         nc.sync.dma_start(w2_w[:].bitcast(I32), w2_words.rearrange("a p c -> p a c").bitcast(I32))
         for q in range(4):
             nc.sync.dma_start(
@@ -104,10 +103,11 @@ def tile_list_zoning_accessibility_step_kernel(
         with nc.allow_non_contiguous_dma(reason="one plan value a partition and row tile"):
             nc.sync.dma_start(plan_sb[:], plan.rearrange("(n p) -> p n", p=P))
         load_state(0)
+        load_opp(1, 0)
         load_state(1)
         load_opp(0, 1)
-        load_opp(1, 1)
         load_state(2)
+        load_opp(1, 1)
         load_state(3)
 
         v_w0 = held([P, S], U32, "v_w0")
@@ -145,27 +145,28 @@ def tile_list_zoning_accessibility_step_kernel(
                 stop=stop,
             )
 
-        def decay_wide(b, h, banks, slot):
-            decay = held([P, PACK, HALF], F32, f"decay{b}{h}", slot)
+        def size_wide(b, h, banks, slot):
+            size = held([P, PACK, HALF], F32, f"size{b}{h}", slot)
             sep = [bank([P, HALF], banks[i], "sep") for i in range(PACK)]
             for i in range(PACK):
                 first_pass(sep[i][:], 0, b, i, h, whole, True, False)
                 first_pass(sep[i][:], 1, b, i, h, whole, False, True)
-                nc.scalar.activation(decay[:, i, :], sep[i][:], ACT.Abs)
-            return decay
+                nc.scalar.activation(size[:, i, :], sep[i][:], ACT.Abs)
+            return size
 
-        def discount(decay):
+        def discount(size, name=None, slot=None):
+            decay = size if slot is None else held([P, PACK, HALF], F32, name, slot)
             for i in range(0, PACK, 2):
-                pair = decay[:, i : i + 2, :]
-                nc.scalar.activation(pair, pair, ACT.Exp, scale=-1.0)
+                nc.scalar.activation(decay[:, i : i + 2, :], size[:, i : i + 2, :], ACT.Exp, scale=-1.0)
+            return decay
 
         z_grouped = {(b, h): held([P, HALF * PACK], BF16, f"z_grouped{b}{h}") for b in range(2) for h in range(2)}
         z_w = {(b, h): held([P, HALF], U32, f"z_w{b}{h}") for b in range(2) for h in range(2)}
         z_s = {(b, h): held([P, HALF], U8, f"z_s{b}{h}") for b in range(2) for h in range(2)}
 
-        def make_z(b, h, decay, cols):
+        def make_z(b, h, decay, cols, engine=nc.vector):
             grouped = z_grouped[b, h][:, PACK * cols.start : PACK * cols.stop]
-            nc.vector.tensor_tensor(
+            engine.tensor_tensor(
                 grouped.rearrange("p (c e i) -> p c i e", e=2, i=PACK),
                 decay.rearrange("p i (c e) -> p c i e", e=2),
                 opp_sb[b, h][:, :, cols].rearrange("p i (c e) -> p c i e", e=2),
@@ -187,40 +188,42 @@ def tile_list_zoning_accessibility_step_kernel(
                 stop=stop,
             )
 
-        steps, remain, pull, shrunk = {}, {}, {}, {}
+        steps, picked, gap, moved, new = {}, {}, {}, {}, {}
 
         def step_wide(n, h, index):
             steps[n, h] = bank([P, HALF], index, "step")
             for b in range(r_passes):
                 second_pass(steps[n, h][:], n, b, h, whole, b == 0, b == r_passes - 1)
 
-        def make_remain(key, one=None):
-            remain[key] = held(list(steps[key].shape), F32, f"remain{key[0]}{key[1]}")
-            if one is None:
-                nc.scalar.activation(remain[key][:], steps[key][:], ACT.Copy, bias=1.0, scale=-1.0)
-            else:
-                nc.scalar.activation(remain[key][:], steps[key][:], ACT.Identity, bias=one, scale=-1.0)
-
-        def make_pull(key):
-            pull[key] = held(list(steps[key].shape), F32, f"pull{key[0]}{key[1]}")
-            n = key[0]
-            nc.scalar.activation(pull[key][:], steps[key][:], ACT.Copy, scale=plan_sb[:, n : n + 1])
-
         def entries(first, count):
             return offsets[:, first // 16 : (first + count) // 16]
 
-        def pick(key, first):
-            count = steps[key].shape[1]
-            shrunk[key] = held([P, count], F32, f"shrunk{key[0]}{key[1]}")
-            nc.vector.tensor_tensor(
-                shrunk[key][:], state[key[0]][:].indirect(entries(first, count)), remain[key][:], ALU.mult
-            )
+        def pick(n, h, slot=None):
+            picked[n, h] = held([P, HALF], F32, f"picked{n}{h}", slot)
+            nc.vector.tensor_copy(picked[n, h][:], state[n][:].indirect(entries(h * HALF, HALF)))
+
+        def make_gap(n, h, slot=None):
+            gap[n, h] = held([P, HALF], F32, f"gap{n}{h}", slot)
+            nc.scalar.activation(gap[n, h][:], picked[n, h][:], ACT.Identity, bias=plan_sb[:, n : n + 1], scale=-1.0)
+
+        def make_moved(key, gap_part, minus_one=None, slot=None):
+            shape = list(steps[key].shape)
+            moved[key] = held(shape, F32, f"moved{key[0]}{key[1]}", slot)
+            if minus_one is None:
+                nc.scalar.activation(moved[key][:], steps[key][:], ACT.Copy, bias=-1.0)
+            else:
+                nc.scalar.activation(moved[key][:], steps[key][:], ACT.Identity, bias=minus_one)
+            nc.gpsimd.tensor_tensor(moved[key][:], moved[key][:], gap_part, ALU.mult)
+
+        def make_new(key, slot=None):
+            shape = list(steps[key].shape)
+            new[key] = moved[key] if slot is None else held(shape, F32, f"new{key[0]}{key[1]}", slot)
+            n = key[0]
+            nc.scalar.activation(new[key][:], moved[key][:], ACT.Identity, bias=plan_sb[:, n : n + 1])
 
         def put(key, first):
             count = steps[key].shape[1]
-            nc.vector.tensor_tensor(
-                state[key[0]][:].indirect(entries(first, count)), shrunk[key][:], pull[key][:], ALU.add
-            )
+            nc.vector.tensor_copy(state[key[0]][:].indirect(entries(first, count)), new[key][:])
 
         def store(n):
             nc.sync.dma_start(out[n * P : (n + 1) * P, :], state[n][:])
@@ -232,8 +235,7 @@ def tile_list_zoning_accessibility_step_kernel(
         prepare_w1(0, 1, P)
         prepare_w1(1, 1, P)
 
-        decay00 = decay_wide(0, 0, (0, 1, 2, 3), "w1_raw00")
-        discount(decay00)
+        decay00 = discount(size_wide(0, 0, (0, 1, 2, 3), "w1_raw00"))
 
         decay10 = held([P, strips, PACK, STRIP], F32, "decay10", "w1_raw10")
         sep10 = [bank([P, PACK, STRIP], 4 + c, "sep10") for c in range(strips)]
@@ -248,6 +250,9 @@ def tile_list_zoning_accessibility_step_kernel(
 
         make_z(0, 0, decay00[:], whole)
         quantize_z(0, 0, whole)
+        pick(0, 0, "w1_raw01")
+        pick(0, 1)
+        make_gap(0, 0)
         for u, name in enumerate("ab"):
             steps[0, name] = bank([P, 2 * STRIP], u, "step")
             for c in (2 * u, 2 * u + 1):
@@ -256,50 +261,50 @@ def tile_list_zoning_accessibility_step_kernel(
             make_z(1, 0, decay10[:, c], strip[c])
             quantize_z(1, 0, strip[c])
             second_pass(steps[0, "ab"[c // 2]][:, strip[c % 2]], 0, 1, 0, strip[c], False, c % 2 == 1)
-        one = held([P, 1], F32, "one", "w1_raw01")
-        nc.gpsimd.memset(one[:], 1.0)
-        make_remain((0, "a"), one[:])
-        make_pull((0, "a"))
-        pick((0, "a"), 0)
+        pick(1, 0)
+        pick(1, 1)
+        minus_one = held([P, 1], F32, "minus_one", "tab_w0")
+        nc.gpsimd.memset(minus_one[:], -1.0)
+        make_moved((0, "a"), gap[0, 0][:, 0 : 2 * STRIP], minus_one[:])
+        make_new((0, "a"))
+        make_moved((0, "b"), gap[0, 0][:, 2 * STRIP : HALF], slot="w1_raw11")
+        make_new((0, "b"), "new0b")
         put((0, "a"), 0)
-        make_remain((0, "b"))
-        make_pull((0, "b"))
-        step_wide(1, 0, 2)
-        make_remain((1, 0))
-        make_pull((1, 0))
-        pick((0, "b"), 2 * STRIP)
-        pick((1, 0), 0)
         put((0, "b"), 2 * STRIP)
+        make_gap(1, 0)
+        step_wide(1, 0, 2)
+        make_moved((1, 0), gap[1, 0][:])
+        make_new((1, 0))
         put((1, 0), 0)
 
-        decay01 = decay_wide(0, 1, (4, 5, 6, 7), "w1_raw01")
-        discount(decay01)
-        decay11 = decay_wide(1, 1, (4, 5, 6, 7), "w1_raw11")
-        discount(decay11)
+        decay01 = discount(size_wide(0, 1, (4, 5, 6, 7), "w1_raw01"), "decay01", "tab_w0")
+        decay11 = discount(size_wide(1, 1, (4, 5, 6, 7), "w1_raw11"), "decay11", "tab_w1")
+        pick(2, 0)
+        pick(2, 1)
+        pick(3, 0)
+        pick(3, 1)
+        make_gap(2, 0, "w1_raw11")
+        make_gap(3, 0)
         step_wide(2, 0, 3)
+        make_moved((2, 0), gap[2, 0][:])
+        make_new((2, 0), "picked30")
         step_wide(3, 0, 0)
-        make_remain((2, 0))
-        make_remain((3, 0))
-        make_pull((2, 0))
-        make_pull((3, 0))
-        make_z(0, 1, decay01[:], whole)
-        make_z(1, 1, decay11[:], whole)
+        make_moved((3, 0), gap[3, 0][:])
+        for c in range(strips):
+            make_z(0, 1, decay01[:, :, strip[c]], strip[c], nc.gpsimd)
         quantize_z(0, 1, whole)
-        pick((2, 0), 0)
-        quantize_z(1, 1, whole)
-        pick((3, 0), 0)
         put((2, 0), 0)
+        for c in range(strips):
+            make_z(1, 1, decay11[:, :, strip[c]], strip[c], nc.gpsimd if c < strips - 1 else nc.vector)
+        quantize_z(1, 1, whole)
+        make_new((3, 0), "z_grouped11")
         put((3, 0), 0)
 
         for n in range(n_tiles):
+            make_gap(n, 1)
+        for n in range(n_tiles):
             step_wide(n, 1, 4 + n)
-        for pair in ((0, 1), (2, 3)):
-            for n in pair:
-                make_remain((n, 1))
-            for n in pair:
-                make_pull((n, 1))
-            for n in pair:
-                pick((n, 1), HALF)
-            for n in pair:
-                put((n, 1), HALF)
-                store(n)
+            make_moved((n, 1), gap[n, 1][:])
+            make_new((n, 1))
+            put((n, 1), HALF)
+            store(n)

@@ -21,6 +21,7 @@ PACK = 4
 PASS = P * PACK
 HALF = 512
 STRIP = 128
+QUARTER = 256
 SHARE = 84
 
 
@@ -105,8 +106,8 @@ def tile_list_zoning_accessibility_step_kernel(
         load_state(0)
         load_opp(1, 0)
         load_state(1)
-        load_opp(0, 1)
         load_state(2)
+        load_opp(0, 1)
         load_opp(1, 1)
         load_state(3)
 
@@ -161,7 +162,7 @@ def tile_list_zoning_accessibility_step_kernel(
             return decay
 
         z_grouped = {(b, h): held([P, HALF * PACK], BF16, f"z_grouped{b}{h}") for b in range(2) for h in range(2)}
-        z_w = {(b, h): held([P, HALF], U32, f"z_w{b}{h}") for b in range(2) for h in range(2)}
+        z_w = {key: held([P, HALF], U32, f"z_w{key[0]}{key[1]}") for key in ((0, 0), (1, 0), (0, 1))}
         z_s = {(b, h): held([P, HALF], U8, f"z_s{b}{h}") for b in range(2) for h in range(2)}
 
         def make_z(b, h, decay, cols, engine=nc.vector):
@@ -278,31 +279,46 @@ def tile_list_zoning_accessibility_step_kernel(
         put((1, 0), 0)
 
         decay01 = discount(size_wide(0, 1, (4, 5, 6, 7), "w1_raw01"), "decay01", "tab_w0")
-        decay11 = discount(size_wide(1, 1, (4, 5, 6, 7), "w1_raw11"), "decay11", "tab_w1")
+        size11 = size_wide(1, 1, (4, 5, 6, 7), "w1_raw11")
         pick(2, 0)
         pick(2, 1)
-        pick(3, 0)
-        pick(3, 1)
-        make_gap(2, 0, "w1_raw11")
-        make_gap(3, 0)
-        step_wide(2, 0, 3)
-        make_moved((2, 0), gap[2, 0][:])
-        make_new((2, 0), "picked30")
-        step_wide(3, 0, 0)
-        make_moved((3, 0), gap[3, 0][:])
         for c in range(strips):
             make_z(0, 1, decay01[:, :, strip[c]], strip[c], nc.gpsimd)
         quantize_z(0, 1, whole)
+        step_wide(2, 0, 5)
+        minus_one = held([P, 1], F32, "minus_one2", "w1_raw00")
+        nc.gpsimd.memset(minus_one[:], -1.0)
+        moved[2, 0] = held([P, HALF], F32, "moved20")
+        nc.scalar.activation(moved[2, 0][:], steps[2, 0][:], ACT.Identity, bias=minus_one[:])
+        make_gap(2, 0, "w1_raw00")
+        nc.gpsimd.tensor_tensor(moved[2, 0][:], moved[2, 0][:], gap[2, 0][:], ALU.mult)
+        make_new((2, 0))
         put((2, 0), 0)
+        decay11 = discount(size11, "decay11", "tab_w1")
         for c in range(strips):
             make_z(1, 1, decay11[:, :, strip[c]], strip[c], nc.gpsimd if c < strips - 1 else nc.vector)
+        z_w[1, 1] = held([P, HALF], U32, "z_w11", "moved20")
         quantize_z(1, 1, whole)
-        make_new((3, 0), "z_grouped11")
-        put((3, 0), 0)
+        pick(3, 0)
+        pick(3, 1)
+        make_gap(3, 0)
 
-        for n in range(n_tiles):
+        make_gap(0, 1)
+        for u, name in enumerate("cd"):
+            steps[0, name] = bank([P, QUARTER], 1 + 3 * u, "step")
+            for b in range(r_passes):
+                for c in (2 * u, 2 * u + 1):
+                    second_pass(steps[0, name][:, strip[c % 2]], 0, b, 1, strip[c], b + c % 2 == 0, b + c % 2 == 2)
+            make_moved((0, name), gap[0, 1][:, u * QUARTER : (u + 1) * QUARTER])
+            make_new((0, name))
+            put((0, name), HALF + u * QUARTER)
+        store(0)
+        step_wide(3, 0, 0)
+        make_moved((3, 0), gap[3, 0][:])
+        make_new((3, 0))
+        put((3, 0), 0)
+        for n in range(1, n_tiles):
             make_gap(n, 1)
-        for n in range(n_tiles):
             step_wide(n, 1, 4 + n)
             make_moved((n, 1), gap[n, 1][:])
             make_new((n, 1))

@@ -161,9 +161,14 @@ def tile_list_zoning_accessibility_step_kernel(
                 nc.scalar.activation(decay[:, i : i + 2, :], size[:, i : i + 2, :], ACT.Exp, scale=-1.0)
             return decay
 
-        z_grouped = {(b, h): held([P, HALF * PACK], BF16, f"z_grouped{b}{h}") for b in range(2) for h in range(2)}
-        z_w = {key: held([P, HALF], U32, f"z_w{key[0]}{key[1]}") for key in ((0, 0), (1, 0), (0, 1))}
-        z_s = {(b, h): held([P, HALF], U8, f"z_s{b}{h}") for b in range(2) for h in range(2)}
+        z_grouped = {(b, 0): held([P, HALF * PACK], BF16, f"z_grouped{b}0")[:] for b in range(2)}
+        z_w = {(b, 0): held([P, HALF], U32, f"z_w{b}0")[:] for b in range(2)}
+        z_s = {(b, 0): held([P, HALF], U8, f"z_s{b}0")[:] for b in range(2)}
+        late_grouped = held([P, 2 * HALF * PACK], BF16, "late_grouped")
+        late_s = held([P, 2 * HALF], U8, "late_s")
+        for b in range(2):
+            z_grouped[b, 1] = late_grouped[:, b * HALF * PACK : (b + 1) * HALF * PACK]
+            z_s[b, 1] = late_s[:, half(b)]
 
         def make_z(b, h, decay, cols, engine=nc.vector):
             grouped = z_grouped[b, h][:, PACK * cols.start : PACK * cols.stop]
@@ -284,7 +289,6 @@ def tile_list_zoning_accessibility_step_kernel(
         pick(2, 1)
         for c in range(strips):
             make_z(0, 1, decay01[:, :, strip[c]], strip[c], nc.gpsimd)
-        quantize_z(0, 1, whole)
         step_wide(2, 0, 5)
         minus_one = held([P, 1], F32, "minus_one2", "w1_raw00")
         nc.gpsimd.memset(minus_one[:], -1.0)
@@ -296,12 +300,18 @@ def tile_list_zoning_accessibility_step_kernel(
         put((2, 0), 0)
         decay11 = discount(size11, "decay11", "tab_w1")
         for c in range(strips):
-            make_z(1, 1, decay11[:, :, strip[c]], strip[c], nc.gpsimd if c < strips - 1 else nc.vector)
-        z_w[1, 1] = held([P, HALF], U32, "z_w11", "moved20")
-        quantize_z(1, 1, whole)
+            make_z(1, 1, decay11[:, :, strip[c]], strip[c], nc.gpsimd)
+        late_w = held([P, 2 * HALF], U32, "late_w", "moved20")
+        for b in range(2):
+            z_w[b, 1] = late_w[:, half(b)]
+        nc.vector.quantize_mx(out=late_w[:].bitcast(FP8X4), scales=late_s[:], in_=late_grouped[:])
         pick(3, 0)
         pick(3, 1)
         make_gap(3, 0)
+        step_wide(3, 0, 0)
+        make_moved((3, 0), gap[3, 0][:])
+        make_new((3, 0), "tab_w1")
+        put((3, 0), 0)
 
         make_gap(0, 1)
         for u, name in enumerate("cd"):
@@ -313,10 +323,6 @@ def tile_list_zoning_accessibility_step_kernel(
             make_new((0, name))
             put((0, name), HALF + u * QUARTER)
         store(0)
-        step_wide(3, 0, 0)
-        make_moved((3, 0), gap[3, 0][:])
-        make_new((3, 0))
-        put((3, 0), 0)
         for n in range(1, n_tiles):
             make_gap(n, 1)
             step_wide(n, 1, 4 + n)

@@ -157,18 +157,17 @@ def tile_list_zoning_accessibility_step_kernel(
 
         def discount(size, name=None, slot=None):
             decay = size if slot is None else held([P, PACK, HALF], F32, name, slot)
-            for i in range(0, PACK, 2):
-                nc.scalar.activation(decay[:, i : i + 2, :], size[:, i : i + 2, :], ACT.Exp, scale=-1.0)
+            for c in range(2):
+                cols = slice(c * QUARTER, (c + 1) * QUARTER)
+                nc.scalar.activation(decay[:, :, cols], size[:, :, cols], ACT.Exp, scale=-1.0)
             return decay
 
         z_grouped = {(b, 0): held([P, HALF * PACK], BF16, f"z_grouped{b}0")[:] for b in range(2)}
         z_w = {(b, 0): held([P, HALF], U32, f"z_w{b}0")[:] for b in range(2)}
         z_s = {(b, 0): held([P, HALF], U8, f"z_s{b}0")[:] for b in range(2)}
         late_grouped = held([P, 2 * HALF * PACK], BF16, "late_grouped")
-        late_s = held([P, 2 * HALF], U8, "late_s")
         for b in range(2):
             z_grouped[b, 1] = late_grouped[:, b * HALF * PACK : (b + 1) * HALF * PACK]
-            z_s[b, 1] = late_s[:, half(b)]
 
         def make_z(b, h, decay, cols, engine=nc.vector):
             grouped = z_grouped[b, h][:, PACK * cols.start : PACK * cols.stop]
@@ -208,9 +207,10 @@ def tile_list_zoning_accessibility_step_kernel(
             picked[n, h] = held([P, HALF], F32, f"picked{n}{h}", slot)
             nc.vector.tensor_copy(picked[n, h][:], state[n][:].indirect(entries(h * HALF, HALF)))
 
-        def make_gap(n, h, slot=None):
-            gap[n, h] = held([P, HALF], F32, f"gap{n}{h}", slot)
-            nc.scalar.activation(gap[n, h][:], picked[n, h][:], ACT.Identity, bias=plan_sb[:, n : n + 1], scale=-1.0)
+        def make_gap(n, h, slot=None, into=None):
+            gap[n, h] = held([P, HALF], F32, f"gap{n}{h}", slot)[:] if into is None else into
+            nc.scalar.activation(gap[n, h], picked[n, h][:], ACT.Identity, bias=plan_sb[:, n : n + 1], scale=-1.0)
+
 
         def make_moved(key, gap_part, minus_one=None, slot=None):
             shape = list(steps[key].shape)
@@ -279,41 +279,45 @@ def tile_list_zoning_accessibility_step_kernel(
         put((0, "b"), 2 * STRIP)
         make_gap(1, 0)
         step_wide(1, 0, 2)
-        make_moved((1, 0), gap[1, 0][:])
+        make_moved((1, 0), gap[1, 0])
         make_new((1, 0))
         put((1, 0), 0)
 
         decay01 = discount(size_wide(0, 1, (4, 5, 6, 7), "w1_raw01"), "decay01", "tab_w0")
-        size11 = size_wide(1, 1, (4, 5, 6, 7), "w1_raw11")
+        size11 = size_wide(1, 1, (0, 1, 2, 0), "w1_raw11")
         pick(2, 0)
         pick(2, 1)
         for c in range(strips):
             make_z(0, 1, decay01[:, :, strip[c]], strip[c], nc.gpsimd)
-        step_wide(2, 0, 5)
+        step_wide(2, 0, 1)
         minus_one = held([P, 1], F32, "minus_one2", "w1_raw00")
         nc.gpsimd.memset(minus_one[:], -1.0)
         moved[2, 0] = held([P, HALF], F32, "moved20")
         nc.scalar.activation(moved[2, 0][:], steps[2, 0][:], ACT.Identity, bias=minus_one[:])
         make_gap(2, 0, "w1_raw00")
-        nc.gpsimd.tensor_tensor(moved[2, 0][:], moved[2, 0][:], gap[2, 0][:], ALU.mult)
+        nc.gpsimd.tensor_tensor(moved[2, 0][:], moved[2, 0][:], gap[2, 0], ALU.mult)
         make_new((2, 0))
         put((2, 0), 0)
         decay11 = discount(size11, "decay11", "tab_w1")
         for c in range(strips):
             make_z(1, 1, decay11[:, :, strip[c]], strip[c], nc.gpsimd)
-        late_w = held([P, 2 * HALF], U32, "late_w", "moved20")
-        for b in range(2):
-            z_w[b, 1] = late_w[:, half(b)]
-        nc.vector.quantize_mx(out=late_w[:].bitcast(FP8X4), scales=late_s[:], in_=late_grouped[:])
         pick(3, 0)
         pick(3, 1)
         make_gap(3, 0)
         step_wide(3, 0, 0)
-        make_moved((3, 0), gap[3, 0][:])
+        moved[3, 0] = held([P, HALF], F32, "moved30")
+        nc.vector.scalar_tensor_tensor(moved[3, 0][:], steps[3, 0][:], -1.0, gap[3, 0], ALU.add, ALU.mult)
+        late_s = held([P, 2 * HALF], U8, "late_s", "gap30")
+        late_w = held([P, 2 * HALF], U32, "late_w", "moved20")
+        for b in range(2):
+            z_w[b, 1] = late_w[:, half(b)]
+            z_s[b, 1] = late_s[:, half(b)]
+        nc.vector.quantize_mx(out=late_w[:].bitcast(FP8X4), scales=late_s[:], in_=late_grouped[:])
         make_new((3, 0), "tab_w1")
         put((3, 0), 0)
 
-        make_gap(0, 1)
+        late_gaps = held([P, 3, HALF], F32, "late_gaps", "w1_raw11")
+        make_gap(0, 1, into=late_gaps[:, 0, :])
         for u, name in enumerate("cd"):
             steps[0, name] = bank([P, QUARTER], 1 + 3 * u, "step")
             for b in range(r_passes):
@@ -324,9 +328,9 @@ def tile_list_zoning_accessibility_step_kernel(
             put((0, name), HALF + u * QUARTER)
         store(0)
         for n in range(1, n_tiles):
-            make_gap(n, 1)
+            make_gap(n, 1, into=late_gaps[:, n, :] if n < 3 else None)
             step_wide(n, 1, 4 + n)
-            make_moved((n, 1), gap[n, 1][:])
+            make_moved((n, 1), gap[n, 1])
             make_new((n, 1))
             put((n, 1), HALF)
             store(n)

@@ -19,9 +19,8 @@ ALU = mybir.AluOpType
 P = 128
 PACK = 4
 PASS = P * PACK
-HALF = 512
+CHUNK = 256
 STRIP = 128
-QUARTER = 256
 SHARE = 84
 
 
@@ -29,13 +28,12 @@ def tile_list_zoning_accessibility_step_kernel(
     tc, tab_words, tab_scales, offs, w1, opp, w2_words, w2_scales, gT, plan, out
 ):
     nc = tc.nc
-    k_passes = K // PASS
-    r_passes = H // PASS
     n_tiles = N // P
-    strips = HALF // STRIP
+    chunks = S // CHUNK
 
     with ExitStack() as ctx:
         keep = ctx.enter_context(tc.tile_pool(name="keep", bufs=1))
+        shared = ctx.enter_context(tc.tile_pool(name="shared", bufs=1))
         psum = ctx.enter_context(tc.psum_pool(name="psum", bufs=1))
 
         def held(shape, dtype, name, slot=None):
@@ -44,26 +42,25 @@ def tile_list_zoning_accessibility_step_kernel(
         def bank(shape, index, name):
             return psum.tile(shape, F32, name=name, tag=f"bank{index}")
 
-        def half(h):
-            return slice(h * HALF, (h + 1) * HALF)
+        def span(first, count):
+            return slice(first, first + count)
 
         offsets = keep.tile([P, S // 16], U16, name="offsets")
-        tab_w = [held([P, T], I32, f"tab_w{a}") for a in range(k_passes)]
+        tab_w = [held([P, T], I32, f"tab_w{a}") for a in range(2)]
         tab_s = keep.tile([P, T], U8, name="tab_s")
-        w1_raw = {
-            (a, b): held([P, PACK, PASS], F32, f"w1_raw{a}{b}")
-            for a in range(k_passes)
-            for b in range(r_passes)
-        }
-        opp_sb = {
-            (b, h): keep.tile([P, PACK, HALF], F32, name=f"opp{b}{h}")
-            for b in range(r_passes)
-            for h in range(2)
-        }
+        w1_raw = {(a, b): held([P, PACK, PASS], F32, f"w1_raw{a}{b}") for a in range(2) for b in range(2)}
+        opp_tile = {(b, c): held([P, PACK, CHUNK * max(c, 1)], F32, f"opp{b}{c}") for b in range(2) for c in range(3)}
+        opp_sb = {(b, c): opp_tile[b, c][:] for b in range(2) for c in range(2)}
+        for b in range(2):
+            for c in (2, 3):
+                opp_sb[b, c] = opp_tile[b, 2][:, :, span((c - 2) * CHUNK, CHUNK)]
         state = [keep.tile([P, T], F32, name=f"state{n}") for n in range(n_tiles)]
-        w2_w = keep.tile([P, r_passes, 2 * N], U8, name="w2_w", align_bytes=64)
-        w2_s = keep.tile([P, r_passes, N], U8, name="w2_s", align_bytes=64)
+        w2_w = held([P, 2, 2 * N], U8, "w2_w")
+        w2_s = held([P, 2, N], U8, "w2_s")
         plan_sb = keep.tile([P, n_tiles], F32, name="plan_sb")
+
+        def entries(first, count):
+            return offsets[:, first // 16 : (first + count) // 16]
 
         nc.vector.memset(tab_s[:].bitcast(I32), 0)
         nc.vector.memset(w2_s[:].bitcast(I32), 0)
@@ -72,21 +69,21 @@ def tile_list_zoning_accessibility_step_kernel(
             nc.sync.dma_start(tab_w[a][:], tab_words[a].rearrange("p t i -> p (t i)").bitcast(I32))
 
         def load_w1(a, b):
-            rows = w1[a * PASS : (a + 1) * PASS, b * PASS : (b + 1) * PASS]
+            rows = w1[span(a * PASS, PASS), span(b * PASS, PASS)]
             nc.sync.dma_start(w1_raw[a, b][:], rows.rearrange("(p i) c -> p i c", i=PACK))
 
-        def load_opp(b, h):
-            rows = opp[b * PASS : (b + 1) * PASS, half(h)]
-            nc.sync.dma_start(opp_sb[b, h][:], rows.rearrange("(p i) j -> p i j", i=PACK))
+        def load_opp(b, c):
+            rows = opp[span(b * PASS, PASS), span(c * CHUNK, CHUNK * max(c, 1))]
+            nc.sync.dma_start(opp_tile[b, c][:], rows.rearrange("(p i) j -> p i j", i=PACK))
 
         def load_state(n):
-            nc.sync.dma_start(state[n][:], gT[n * P : (n + 1) * P, :])
+            nc.sync.dma_start(state[n][:], gT[span(n * P, P), :])
 
         load_tab(0)
         nc.sync.dma_start(offsets[:], offs)
         for q in range(4):
             nc.sync.dma_start(
-                tab_s[32 * q : 32 * q + 4 * k_passes, :].bitcast(I32),
+                tab_s[32 * q : 32 * q + 8, :].bitcast(I32),
                 tab_scales[:, 4 * q : 4 * q + 4, :].bitcast(I32),
             )
         load_w1(0, 0)
@@ -95,32 +92,35 @@ def tile_list_zoning_accessibility_step_kernel(
         load_w1(0, 1)
         load_w1(1, 1)
         load_opp(0, 0)
-        nc.sync.dma_start(w2_w[:].bitcast(I32), w2_words.rearrange("a p c -> p a c").bitcast(I32))
         for q in range(4):
             nc.sync.dma_start(
                 w2_s[32 * q : 32 * q + 4, :, :].bitcast(I32),
                 w2_scales[:, 4 * q : 4 * q + 4, :].rearrange("a r n -> r a n").bitcast(I32),
             )
-        with nc.allow_non_contiguous_dma(reason="one plan value a partition and row tile"):
-            nc.sync.dma_start(plan_sb[:], plan.rearrange("(n p) -> p n", p=P))
         load_state(0)
         load_opp(1, 0)
-        load_state(1)
-        load_state(2)
+        nc.sync.dma_start(w2_w[:].bitcast(I32), w2_words.rearrange("a p c -> p a c").bitcast(I32))
+        with nc.allow_non_contiguous_dma(reason="one plan value a partition and row tile"):
+            nc.sync.dma_start(plan_sb[:], plan.rearrange("(n p) -> p n", p=P))
         load_opp(0, 1)
         load_opp(1, 1)
+        load_state(1)
+        load_opp(0, 2)
+        load_state(2)
+        load_opp(1, 2)
         load_state(3)
 
         v_w0 = held([P, S], U32, "v_w0")
-        v_w = {(0, h): v_w0[:, half(h)] for h in range(2)}
-        v_w[1, 0] = held([P, HALF], U32, "v_w10")[:]
-        v_s = keep.tile([P, S], U8, name="v_s", align_bytes=64)
-        nc.vector.tensor_copy(v_s[:], tab_s[:].indirect(offsets[:]))
-        nc.vector.tensor_copy(v_w0[:], tab_w[0][:].bitcast(U32).indirect(offsets[:]))
-        nc.vector.tensor_copy(v_w[1, 0], tab_w[1][:].bitcast(U32).indirect(offsets[:, 0 : HALF // 16]))
+        v_s = held([P, S], U8, "v_s")
+        v_w = {(0, u): v_w0[:, span(u * STRIP, STRIP)] for u in range(S // STRIP)}
+
+        def pick_words(first, count, slot=None):
+            words = held([P, count], U32, f"v_w1_{first}", slot)
+            nc.vector.tensor_copy(words[:], tab_w[1][:].bitcast(U32).indirect(entries(first, count)))
+            for u in range(count // STRIP):
+                v_w[1, first // STRIP + u] = words[:, span(u * STRIP, STRIP)]
 
         w1_w, w1_s = {}, {}
-        whole = slice(0, HALF)
 
         def prepare_w1(a, b, on_vector):
             grouped = held([P, PASS * PACK], BF16, f"w1_grouped{a}{b}")
@@ -134,203 +134,211 @@ def tile_list_zoning_accessibility_step_kernel(
             w1_s[a, b] = held([P, PASS], U8, f"w1_s{a}{b}")
             nc.vector.quantize_mx(out=w1_w[a, b][:].bitcast(FP8X4), scales=w1_s[a, b][:], in_=grouped[:])
 
-        def first_pass(into, a, b, i, h, cols, start, stop):
-            m = slice(i * P, (i + 1) * P)
-            nc.tensor.matmul_mx(
-                out=into,
-                lhsT=w1_w[a, b][:, m].bitcast(FP8X4),
-                lhsT_scale=w1_s[a, b][:, m],
-                rhs=v_w[a, h][:, cols].bitcast(FP8X4),
-                rhs_scale=v_s[4 * a : P, h * HALF + cols.start : h * HALF + cols.stop],
-                start=start,
-                stop=stop,
-            )
+        decay = {}
 
-        def size_wide(b, h, banks, slot):
-            size = held([P, PACK, HALF], F32, f"size{b}{h}", slot)
-            sep = [bank([P, HALF], banks[i], "sep") for i in range(PACK)]
-            for i in range(PACK):
-                first_pass(sep[i][:], 0, b, i, h, whole, True, False)
-                first_pass(sep[i][:], 1, b, i, h, whole, False, True)
-                nc.scalar.activation(size[:, i, :], sep[i][:], ACT.Abs)
-            return size
+        def make_size(b, c, banks, slot=None):
+            decay[b, c] = spot([P, 2, PACK, STRIP], f"decay{b}{c}", slot)
+            for u in range(2):
+                cols = span(c * CHUNK + u * STRIP, STRIP)
+                sep = bank([P, PACK, STRIP], banks[u], "sep")
+                for a in range(2):
+                    for i in range(PACK):
+                        m = span(i * P, P)
+                        nc.tensor.matmul_mx(
+                            out=sep[:, i, :],
+                            lhsT=w1_w[a, b][:, m].bitcast(FP8X4),
+                            lhsT_scale=w1_s[a, b][:, m],
+                            rhs=v_w[a, 2 * c + u].bitcast(FP8X4),
+                            rhs_scale=v_s[4 * a : P, cols],
+                            start=a + i == 0,
+                            stop=a + i == PACK,
+                        )
+                if (b, c) == (1, 0):
+                    nc.scalar.activation(decay[b, c][:, u], sep[:], ACT.Abs)
+                    nc.scalar.activation(decay[b, c][:, u], decay[b, c][:, u], ACT.Exp, scale=-1.0)
+                else:
+                    woven = decay[b, c][:, u].rearrange("p i c -> p (i c)").rearrange("p (c i) -> p c i", i=PACK)
+                    nc.scalar.activation(woven, sep[:].rearrange("p i c -> p c i"), ACT.Abs)
+            if (b, c) != (1, 0):
+                nc.scalar.activation(decay[b, c][:], decay[b, c][:], ACT.Exp, scale=-1.0)
 
-        def discount(size, name=None, slot=None):
-            decay = size if slot is None else held([P, PACK, HALF], F32, name, slot)
-            for c in range(2):
-                cols = slice(c * QUARTER, (c + 1) * QUARTER)
-                nc.scalar.activation(decay[:, :, cols], size[:, :, cols], ACT.Exp, scale=-1.0)
-            return decay
+        z_grouped, z_w, z_s = {}, {}, {}
 
-        z_grouped = {(b, 0): held([P, HALF * PACK], BF16, f"z_grouped{b}0")[:] for b in range(2)}
-        z_w = {(b, 0): held([P, HALF], U32, f"z_w{b}0")[:] for b in range(2)}
-        z_s = {(b, 0): held([P, HALF], U8, f"z_s{b}0")[:] for b in range(2)}
-        late_grouped = held([P, 2 * HALF * PACK], BF16, "late_grouped")
-        for b in range(2):
-            z_grouped[b, 1] = late_grouped[:, b * HALF * PACK : (b + 1) * HALF * PACK]
+        def make_z_first(b):
+            for u in range(2):
+                grouped = z_grouped[0][:, b, span(u * STRIP * PACK, STRIP * PACK)]
+                nc.vector.tensor_tensor(
+                    grouped.rearrange("p (c e i) -> p c i e", e=2, i=PACK),
+                    decay[b, 0][:, u].rearrange("p i (c e) -> p c i e", e=2),
+                    opp_sb[b, 0][:, :, span(u * STRIP, STRIP)].rearrange("p i (c e) -> p c i e", e=2),
+                    ALU.mult,
+                )
 
-        def make_z(b, h, decay, cols, engine=nc.vector):
-            grouped = z_grouped[b, h][:, PACK * cols.start : PACK * cols.stop]
-            engine.tensor_tensor(
-                grouped.rearrange("p (c e i) -> p c i e", e=2, i=PACK),
-                decay.rearrange("p i (c e) -> p c i e", e=2),
-                opp_sb[b, h][:, :, cols].rearrange("p i (c e) -> p c i e", e=2),
+        def make_z(b, c):
+            nc.gpsimd.tensor_tensor(
+                z_grouped[c][:, b, :].rearrange("p (c i) -> p c i", i=PACK),
+                decay[b, c][:].rearrange("p u i c -> p (u i c)").rearrange("p (c i) -> p c i", i=PACK),
+                opp_sb[b, c].rearrange("p i c -> p c i"),
                 ALU.mult,
             )
 
-        def quantize_z(b, h, cols):
-            grouped = z_grouped[b, h][:, PACK * cols.start : PACK * cols.stop]
-            nc.vector.quantize_mx(out=z_w[b, h][:, cols].bitcast(FP8X4), scales=z_s[b, h][:, cols], in_=grouped)
+        placed = {"new10": 0, "picked30": 1536, "decay13": 2048, "picked31": 6144, "gap30": 6656, "pair_gap1": 7168,
+                  "z_w1": 13312, "gap10": 14848, "pair_gap0": 15360}
 
-        def second_pass(into, n, b, h, cols, start, stop):
-            nc.tensor.matmul_mx(
-                out=into,
-                lhsT=w2_w[:, b, 2 * n * P : 2 * (n + 1) * P].bitcast(FP4X4),
-                lhsT_scale=w2_s[:, b, n * P : (n + 1) * P],
-                rhs=z_w[b, h][:, cols].bitcast(FP8X4),
-                rhs_scale=z_s[b, h][:, cols],
-                start=start,
-                stop=stop,
-            )
+        def spot(shape, name, slot=None, dtype=F32):
+            if name in placed:
+                return shared.tile(shape, dtype, name=name, offset=placed[name], align_bytes=64)
+            return held(shape, dtype, name, slot)
 
-        steps, picked, gap, moved, new = {}, {}, {}, {}, {}
+        def open_codes(c, slot=None):
+            z_w[c] = spot([P, 2 * CHUNK], f"z_w{c}", slot, U32)
+            z_s[c] = held([P, 2 * CHUNK], U8, f"z_s{c}")
 
-        def step_wide(n, h, index):
-            steps[n, h] = bank([P, HALF], index, "step")
-            for b in range(r_passes):
-                second_pass(steps[n, h][:], n, b, h, whole, b == 0, b == r_passes - 1)
-
-        def entries(first, count):
-            return offsets[:, first // 16 : (first + count) // 16]
-
-        def pick(n, h, slot=None):
-            picked[n, h] = held([P, HALF], F32, f"picked{n}{h}", slot)
-            nc.vector.tensor_copy(picked[n, h][:], state[n][:].indirect(entries(h * HALF, HALF)))
-
-        def make_gap(n, h, slot=None, into=None):
-            gap[n, h] = held([P, HALF], F32, f"gap{n}{h}", slot)[:] if into is None else into
-            nc.scalar.activation(gap[n, h], picked[n, h][:], ACT.Identity, bias=plan_sb[:, n : n + 1], scale=-1.0)
-
-
-        def make_moved(key, gap_part, minus_one=None, slot=None):
-            shape = list(steps[key].shape)
-            moved[key] = held(shape, F32, f"moved{key[0]}{key[1]}", slot)
-            if minus_one is None:
-                nc.scalar.activation(moved[key][:], steps[key][:], ACT.Copy, bias=-1.0)
+        def quantize_z(c, b=None):
+            if b is None:
+                cols, source = slice(0, 2 * CHUNK), z_grouped[c][:].rearrange("p b x -> p (b x)")
             else:
-                nc.scalar.activation(moved[key][:], steps[key][:], ACT.Identity, bias=minus_one)
-            nc.gpsimd.tensor_tensor(moved[key][:], moved[key][:], gap_part, ALU.mult)
+                cols, source = span(b * CHUNK, CHUNK), z_grouped[c][:, b, :]
+            nc.vector.quantize_mx(out=z_w[c][:, cols].bitcast(FP8X4), scales=z_s[c][:, cols], in_=source)
 
-        def make_new(key, slot=None):
-            shape = list(steps[key].shape)
-            new[key] = moved[key] if slot is None else held(shape, F32, f"new{key[0]}{key[1]}", slot)
-            n = key[0]
-            nc.scalar.activation(new[key][:], moved[key][:], ACT.Identity, bias=plan_sb[:, n : n + 1])
+        picked, gap, new = {}, {}, {}
 
-        def put(key, first):
-            count = steps[key].shape[1]
-            nc.vector.tensor_copy(state[key[0]][:].indirect(entries(first, count)), new[key][:])
+        def pick(n, first, count, slot=None):
+            picked[n, first] = spot([P, count], f"picked{n}{first // CHUNK}", slot)
+            nc.vector.tensor_copy(picked[n, first][:], state[n][:].indirect(entries(first, count)))
+
+        def gap_rest(pair, slot=None):
+            gap[pair] = spot([P, 2, S - CHUNK], f"pair_gap{pair}", slot)
+            for (n, first), values in picked.items():
+                if n // 2 == pair and first > 0:
+                    into = gap[pair][:, n % 2, span(first - CHUNK, values.shape[1])]
+                    nc.scalar.activation(into, values[:], ACT.Identity, bias=plan_sb[:, n : n + 1], scale=-1.0)
+
+        def update(parts, index, gaps, slot=None):
+            step = bank([P, len(parts), CHUNK], index, "step")
+            for k, (c, n) in enumerate(parts):
+                for u in range(2):
+                    for b in range(2):
+                        cols = span(b * CHUNK + u * STRIP, STRIP)
+                        nc.tensor.matmul_mx(
+                            out=step[:, k, span(u * STRIP, STRIP)],
+                            lhsT=w2_w[:, b, span(2 * n * P, 2 * P)].bitcast(FP4X4),
+                            lhsT_scale=w2_s[:, b, span(n * P, P)],
+                            rhs=z_w[c][:, cols].bitcast(FP8X4),
+                            rhs_scale=z_s[c][:, cols],
+                            start=k + u + b == 0,
+                            stop=k + u + b == len(parts) + 1,
+                        )
+            moved = spot([P, len(parts), CHUNK], f"new{parts[0][0]}{parts[0][1]}", slot)
+            if parts[0] in ((0, 0), (0, 3)):
+                nc.vector.scalar_tensor_tensor(moved[:], step[:], -1.0, gaps, ALU.add, ALU.mult)
+            else:
+                nc.scalar.activation(moved[:], step[:], ACT.Copy, bias=-1.0)
+                nc.gpsimd.tensor_tensor(moved[:], moved[:], gaps, ALU.mult)
+            if parts[0][1] == parts[-1][1]:
+                c, n = parts[0]
+                new[c, n] = moved[:].rearrange("p k j -> p (k j)")
+                nc.scalar.activation(new[c, n], new[c, n], ACT.Identity, bias=plan_sb[:, n : n + 1])
+            else:
+                for k, (c, n) in enumerate(parts):
+                    new[c, n] = moved[:, k, :]
+                    nc.scalar.activation(new[c, n], new[c, n], ACT.Identity, bias=plan_sb[:, n : n + 1])
+
+        def put(c, n):
+            count = new[c, n].shape[1]
+            nc.vector.tensor_copy(state[n][:].indirect(entries(c * CHUNK, count)), new[c, n])
 
         def store(n):
-            nc.sync.dma_start(out[n * P : (n + 1) * P, :], state[n][:])
+            nc.sync.dma_start(out[span(n * P, P), :], state[n][:])
 
+        def first_gap(n):
+            pick(n, 0, CHUNK)
+            gap[n, 0] = spot([P, 1, CHUNK], f"gap{n}0")
+            nc.scalar.activation(gap[n, 0][:, 0, :], picked[n, 0][:], ACT.Identity, bias=plan_sb[:, n : n + 1], scale=-1.0)
+
+        def pair_update(c, pair, index, slot=None):
+            update([(c, 2 * pair), (c, 2 * pair + 1)], index, gap[pair][:, :, span((c - 1) * CHUNK, CHUNK)], slot)
+
+        def lone_update(c, n, index, count=1):
+            gaps = gap[n // 2][:, n % 2, span((c - 1) * CHUNK, count * CHUNK)]
+            update([(c + k, n) for k in range(count)], index, gaps.rearrange("p (k j) -> p k j", k=count))
+
+        nc.vector.tensor_copy(v_w0[:], tab_w[0][:].bitcast(U32).indirect(offsets[:]))
+        nc.vector.tensor_copy(v_s[:], tab_s[:].indirect(offsets[:]))
+        pick_words(0, CHUNK)
         prepare_w1(0, 0, 0)
+        pick_words(CHUNK, 384, "w1_grouped00")
         prepare_w1(1, 0, SHARE)
-        v_w[1, 1] = held([P, HALF], U32, "v_w11", "w1_grouped10")[:]
-        nc.vector.tensor_copy(v_w[1, 1], tab_w[1][:].bitcast(U32).indirect(offsets[:, HALF // 16 : S // 16]))
+        make_size(0, 0, (0, 1))
         prepare_w1(0, 1, P)
+        make_size(0, 1, (2, 3))
         prepare_w1(1, 1, P)
+        make_size(1, 0, (0, 1))
+        for c in range(chunks):
+            z_grouped[c] = held([P, 2, CHUNK * PACK], BF16, f"z_grouped{c}", f"w1_raw{c % 2}{c // 2}")
+        make_z(0, 0)
+        first_gap(0)
+        pick(0, 2 * CHUNK, 2 * CHUNK)
+        make_z_first(1)
+        open_codes(0)
+        quantize_z(0)
+        pick(0, CHUNK, CHUNK, "w1_raw00")
+        make_size(1, 1, (2, 3))
+        update([(0, 0)], 4, gap[0, 0][:])
+        pick_words(CHUNK + 384, 384, "gap00")
+        put(0, 0)
+        make_z(0, 1)
+        make_z(1, 1)
+        make_size(0, 2, (4, 0))
 
-        decay00 = discount(size_wide(0, 0, (0, 1, 2, 3), "w1_raw00"))
+        first_gap(1)
+        pick(1, CHUNK, S - CHUNK)
+        update([(0, 1)], 5, gap[1, 0][:])
+        open_codes(1, "gap10")
+        quantize_z(1)
+        put(0, 1)
+        make_size(1, 2, (1, 2), "picked10")
+        gap_rest(0)
+        make_z(0, 2)
 
-        decay10 = held([P, strips, PACK, STRIP], F32, "decay10", "w1_raw10")
-        sep10 = [bank([P, PACK, STRIP], 4 + c, "sep10") for c in range(strips)]
-        strip = [slice(c * STRIP, (c + 1) * STRIP) for c in range(strips)]
-        for c in range(strips):
-            for i in range(PACK):
-                first_pass(sep10[c][:, i, :], 0, 1, i, 0, strip[c], i == 0, False)
-            for i in range(PACK):
-                first_pass(sep10[c][:, i, :], 1, 1, i, 0, strip[c], False, i == PACK - 1)
-            nc.scalar.activation(decay10[:, c], sep10[c][:], ACT.Abs)
-            nc.scalar.activation(decay10[:, c], decay10[:, c], ACT.Exp, scale=-1.0)
+        first_gap(2)
+        pick(2, CHUNK, S - CHUNK)
+        update([(0, 2)], 6, gap[2, 0][:])
+        put(0, 2)
+        make_size(0, 3, (3, 0), "picked20")
+        make_z(1, 2)
+        make_z(0, 3)
 
-        make_z(0, 0, decay00[:], whole)
-        quantize_z(0, 0, whole)
-        pick(0, 0, "w1_raw01")
-        pick(0, 1)
-        make_gap(0, 0)
-        for u, name in enumerate("ab"):
-            steps[0, name] = bank([P, 2 * STRIP], u, "step")
-            for c in (2 * u, 2 * u + 1):
-                second_pass(steps[0, name][:, strip[c % 2]], 0, 0, 0, strip[c], c % 2 == 0, False)
-        for c in range(strips):
-            make_z(1, 0, decay10[:, c], strip[c])
-            quantize_z(1, 0, strip[c])
-            second_pass(steps[0, "ab"[c // 2]][:, strip[c % 2]], 0, 1, 0, strip[c], False, c % 2 == 1)
-        pick(1, 0)
-        pick(1, 1)
-        minus_one = held([P, 1], F32, "minus_one", "tab_w0")
-        nc.gpsimd.memset(minus_one[:], -1.0)
-        make_moved((0, "a"), gap[0, 0][:, 0 : 2 * STRIP], minus_one[:])
-        make_new((0, "a"))
-        make_moved((0, "b"), gap[0, 0][:, 2 * STRIP : HALF], slot="w1_raw11")
-        make_new((0, "b"), "new0b")
-        put((0, "a"), 0)
-        put((0, "b"), 2 * STRIP)
-        make_gap(1, 0)
-        step_wide(1, 0, 2)
-        make_moved((1, 0), gap[1, 0])
-        make_new((1, 0))
-        put((1, 0), 0)
-
-        decay01 = discount(size_wide(0, 1, (4, 5, 6, 7), "w1_raw01"), "decay01", "tab_w0")
-        size11 = size_wide(1, 1, (0, 1, 2, 0), "w1_raw11")
-        pick(2, 0)
-        pick(2, 1)
-        for c in range(strips):
-            make_z(0, 1, decay01[:, :, strip[c]], strip[c], nc.gpsimd)
-        step_wide(2, 0, 1)
-        minus_one = held([P, 1], F32, "minus_one2", "w1_raw00")
-        nc.gpsimd.memset(minus_one[:], -1.0)
-        moved[2, 0] = held([P, HALF], F32, "moved20")
-        nc.scalar.activation(moved[2, 0][:], steps[2, 0][:], ACT.Identity, bias=minus_one[:])
-        make_gap(2, 0, "w1_raw00")
-        nc.gpsimd.tensor_tensor(moved[2, 0][:], moved[2, 0][:], gap[2, 0], ALU.mult)
-        make_new((2, 0))
-        put((2, 0), 0)
-        decay11 = discount(size11, "decay11", "tab_w1")
-        for c in range(strips):
-            make_z(1, 1, decay11[:, :, strip[c]], strip[c], nc.gpsimd)
-        pick(3, 0)
-        pick(3, 1)
-        make_gap(3, 0)
-        step_wide(3, 0, 0)
-        moved[3, 0] = held([P, HALF], F32, "moved30")
-        nc.vector.scalar_tensor_tensor(moved[3, 0][:], steps[3, 0][:], -1.0, gap[3, 0], ALU.add, ALU.mult)
-        late_s = held([P, 2 * HALF], U8, "late_s", "gap30")
-        late_w = held([P, 2 * HALF], U32, "late_w", "moved20")
-        for b in range(2):
-            z_w[b, 1] = late_w[:, half(b)]
-            z_s[b, 1] = late_s[:, half(b)]
-        nc.vector.quantize_mx(out=late_w[:].bitcast(FP8X4), scales=late_s[:], in_=late_grouped[:])
-        make_new((3, 0), "tab_w1")
-        put((3, 0), 0)
-
-        late_gaps = held([P, 3, HALF], F32, "late_gaps", "w1_raw11")
-        make_gap(0, 1, into=late_gaps[:, 0, :])
-        for u, name in enumerate("cd"):
-            steps[0, name] = bank([P, QUARTER], 1 + 3 * u, "step")
-            for b in range(r_passes):
-                for c in (2 * u, 2 * u + 1):
-                    second_pass(steps[0, name][:, strip[c % 2]], 0, b, 1, strip[c], b + c % 2 == 0, b + c % 2 == 2)
-            make_moved((0, name), gap[0, 1][:, u * QUARTER : (u + 1) * QUARTER])
-            make_new((0, name))
-            put((0, name), HALF + u * QUARTER)
-        store(0)
-        for n in range(1, n_tiles):
-            make_gap(n, 1, into=late_gaps[:, n, :] if n < 3 else None)
-            step_wide(n, 1, 4 + n)
-            make_moved((n, 1), gap[n, 1])
-            make_new((n, 1))
-            put((n, 1), HALF)
+        first_gap(3)
+        pick(3, 2 * CHUNK, 2 * CHUNK)
+        update([(0, 3)], 7, gap[3, 0][:])
+        pick(3, CHUNK, CHUNK)
+        put(0, 3)
+        pair_update(1, 0, 4)
+        put(1, 0)
+        open_codes(2, "new03")
+        quantize_z(2)
+        put(1, 1)
+        gap_rest(1)
+        pair_update(1, 1, 5)
+        make_size(1, 3, (1, 2))
+        put(1, 2)
+        put(1, 3)
+        make_z(1, 3)
+        open_codes(3)
+        quantize_z(3)
+        pair_update(2, 0, 6)
+        put(2, 0)
+        put(2, 1)
+        lone_update(2, 2, 7)
+        put(2, 2)
+        pair_update(3, 0, 4)
+        for n in range(2):
+            put(3, n)
             store(n)
+        lone_update(3, 2, 5)
+        put(3, 2)
+        store(2)
+        lone_update(2, 3, 6, count=2)
+        put(2, 3)
+        store(3)

@@ -110,20 +110,37 @@ def tile_list_zoning_accessibility_step_kernel(
         load_opp(1, 2)
         load_state(3)
 
-        v_w0 = held([P, S], U32, "v_w0")
-        v_s = held([P, S], U8, "v_s")
-        v_w = {(0, u): v_w0[:, span(u * STRIP, STRIP)] for u in range(S // STRIP)}
+        placed = {}
 
-        def pick_words(first, count, slot=None):
-            words = held([P, count], U32, f"v_w1_{first}", slot)
-            nc.vector.tensor_copy(words[:], tab_w[1][:].bitcast(U32).indirect(entries(first, count)))
+        def heirs(start, left, left_bytes, donor, right):
+            placed[left] = start
+            placed[donor] = start + left_bytes - 512
+            placed[right] = start + left_bytes
+
+        heirs(0, "z_w1", 2048, "gap10", "picked11")
+        placed.update({"size13": 4096, "moved03": 4096, "new20": 4096})
+        heirs(8192, "z_w2", 2048, "gap30", "picked31")
+        placed.update({"w1_grouped11": 12288, "v_w0_640": 12288 - 1024, "z_grouped0": 12288 + 512})
+        placed.update({"picked01": 16384, "z_grouped1": 12800, "z_grouped2": 12800, "z_grouped3": 12800, "new22": 12800})
+
+        def spot(shape, name, slot=None, dtype=F32):
+            if name in placed:
+                return shared.tile(shape, dtype, name=name, offset=placed[name], align_bytes=64)
+            return held(shape, dtype, name, slot)
+
+        v_s = held([P, S], U8, "v_s")
+        v_w = {}
+
+        def pick_words(a, first, count, slot=None):
+            words = spot([P, count], f"v_w{a}_{first}", slot, U32)
+            nc.vector.tensor_copy(words[:], tab_w[a][:].bitcast(U32).indirect(entries(first, count)))
             for u in range(count // STRIP):
-                v_w[1, first // STRIP + u] = words[:, span(u * STRIP, STRIP)]
+                v_w[a, first // STRIP + u] = words[:, span(u * STRIP, STRIP)]
 
         w1_w, w1_s = {}, {}
 
         def prepare_w1(a, b, on_vector):
-            grouped = held([P, PASS * PACK], BF16, f"w1_grouped{a}{b}")
+            grouped = spot([P, PASS * PACK], f"w1_grouped{a}{b}", None, BF16)
             into = grouped[:].rearrange("p (u e m i) -> p u m i e", u=2, e=2, i=PACK)
             source = w1_raw[a, b][:].rearrange("p i (m u e) -> p u m i e", u=2, e=2)
             if on_vector > 0:
@@ -137,7 +154,7 @@ def tile_list_zoning_accessibility_step_kernel(
         decay = {}
 
         def make_size(b, c, banks, slot=None):
-            decay[b, c] = spot([P, 2, PACK, STRIP], f"decay{b}{c}", slot)
+            decay[b, c] = spot([P, 2, PACK, STRIP], f"size{b}{c}", slot)
             for u in range(2):
                 cols = span(c * CHUNK + u * STRIP, STRIP)
                 sep = bank([P, PACK, STRIP], banks[u], "sep")
@@ -160,7 +177,10 @@ def tile_list_zoning_accessibility_step_kernel(
                     woven = decay[b, c][:, u].rearrange("p i c -> p (i c)").rearrange("p (c i) -> p c i", i=PACK)
                     nc.scalar.activation(woven, sep[:].rearrange("p i c -> p c i"), ACT.Abs)
             if (b, c) != (1, 0):
-                nc.scalar.activation(decay[b, c][:], decay[b, c][:], ACT.Exp, scale=-1.0)
+                size = decay[b, c]
+                if (b, c) == (1, 3):
+                    decay[b, c] = spot([P, 2, PACK, STRIP], f"decay{b}{c}", "w1_raw10")
+                nc.scalar.activation(decay[b, c][:], size[:], ACT.Exp, scale=-1.0)
 
         z_grouped, z_w, z_s = {}, {}, {}
 
@@ -175,20 +195,14 @@ def tile_list_zoning_accessibility_step_kernel(
                 )
 
         def make_z(b, c):
+            if b == 0:
+                z_grouped[c] = spot([P, 2, CHUNK * PACK], f"z_grouped{c}", None, BF16)
             nc.gpsimd.tensor_tensor(
                 z_grouped[c][:, b, :].rearrange("p (c i) -> p c i", i=PACK),
                 decay[b, c][:].rearrange("p u i c -> p (u i c)").rearrange("p (c i) -> p c i", i=PACK),
                 opp_sb[b, c].rearrange("p i c -> p c i"),
                 ALU.mult,
             )
-
-        placed = {"new10": 0, "picked30": 1536, "decay13": 2048, "picked31": 6144, "gap30": 6656, "pair_gap1": 7168,
-                  "z_w1": 13312, "gap10": 14848, "pair_gap0": 15360}
-
-        def spot(shape, name, slot=None, dtype=F32):
-            if name in placed:
-                return shared.tile(shape, dtype, name=name, offset=placed[name], align_bytes=64)
-            return held(shape, dtype, name, slot)
 
         def open_codes(c, slot=None):
             z_w[c] = spot([P, 2 * CHUNK], f"z_w{c}", slot, U32)
@@ -201,20 +215,19 @@ def tile_list_zoning_accessibility_step_kernel(
                 cols, source = span(b * CHUNK, CHUNK), z_grouped[c][:, b, :]
             nc.vector.quantize_mx(out=z_w[c][:, cols].bitcast(FP8X4), scales=z_s[c][:, cols], in_=source)
 
-        picked, gap, new = {}, {}, {}
+        picked, first_gaps, gap, new = {}, {}, {}, {}
 
         def pick(n, first, count, slot=None):
             picked[n, first] = spot([P, count], f"picked{n}{first // CHUNK}", slot)
             nc.vector.tensor_copy(picked[n, first][:], state[n][:].indirect(entries(first, count)))
 
-        def gap_rest(pair, slot=None):
-            gap[pair] = spot([P, 2, S - CHUNK], f"pair_gap{pair}", slot)
-            for (n, first), values in picked.items():
-                if n // 2 == pair and first > 0:
-                    into = gap[pair][:, n % 2, span(first - CHUNK, values.shape[1])]
-                    nc.scalar.activation(into, values[:], ACT.Identity, bias=plan_sb[:, n : n + 1], scale=-1.0)
+        def gap_rest(n, c, slot=None):
+            if n % 2 == 0:
+                gap[n // 2, c] = spot([P, 2, c * CHUNK], f"pair_gap{n // 2}{c}", slot)
+            into = gap[n // 2, c][:, n % 2, :]
+            nc.scalar.activation(into, picked[n, c * CHUNK][:], ACT.Identity, bias=plan_sb[:, n : n + 1], scale=-1.0)
 
-        def update(parts, index, gaps, slot=None):
+        def update(parts, index, gaps, slot=None, later=None):
             step = bank([P, len(parts), CHUNK], index, "step")
             for k, (c, n) in enumerate(parts):
                 for u in range(2):
@@ -229,20 +242,25 @@ def tile_list_zoning_accessibility_step_kernel(
                             start=k + u + b == 0,
                             stop=k + u + b == len(parts) + 1,
                         )
-            moved = spot([P, len(parts), CHUNK], f"new{parts[0][0]}{parts[0][1]}", slot)
-            if parts[0] in ((0, 0), (0, 3)):
+            if parts[0][0] == 0:
+                n = parts[0][1]
+                moved = spot([P, 1, CHUNK], f"moved0{n}")
                 nc.vector.scalar_tensor_tensor(moved[:], step[:], -1.0, gaps, ALU.add, ALU.mult)
-            else:
-                nc.scalar.activation(moved[:], step[:], ACT.Copy, bias=-1.0)
-                nc.gpsimd.tensor_tensor(moved[:], moved[:], gaps, ALU.mult)
+                new[0, n] = spot([P, CHUNK], f"new0{n}")[:]
+                nc.scalar.activation(new[0, n], moved[:, 0, :], ACT.Identity, bias=plan_sb[:, n : n + 1])
+                return
+            moved = spot([P, len(parts), CHUNK], f"new{parts[0][0]}{parts[0][1]}", slot)
+            nc.scalar.activation(moved[:], step[:], ACT.Copy, bias=-1.0)
+            nc.gpsimd.tensor_tensor(moved[:], moved[:], gaps, ALU.mult)
             if parts[0][1] == parts[-1][1]:
                 c, n = parts[0]
                 new[c, n] = moved[:].rearrange("p k j -> p (k j)")
                 nc.scalar.activation(new[c, n], new[c, n], ACT.Identity, bias=plan_sb[:, n : n + 1])
             else:
+                sums = moved if later is None else held([P, len(parts), CHUNK], F32, "sums", later)
                 for k, (c, n) in enumerate(parts):
-                    new[c, n] = moved[:, k, :]
-                    nc.scalar.activation(new[c, n], new[c, n], ACT.Identity, bias=plan_sb[:, n : n + 1])
+                    new[c, n] = sums[:, k, :]
+                    nc.scalar.activation(new[c, n], moved[:, k, :], ACT.Identity, bias=plan_sb[:, n : n + 1])
 
         def put(c, n):
             count = new[c, n].shape[1]
@@ -253,29 +271,28 @@ def tile_list_zoning_accessibility_step_kernel(
 
         def first_gap(n):
             pick(n, 0, CHUNK)
-            gap[n, 0] = spot([P, 1, CHUNK], f"gap{n}0")
-            nc.scalar.activation(gap[n, 0][:, 0, :], picked[n, 0][:], ACT.Identity, bias=plan_sb[:, n : n + 1], scale=-1.0)
+            first_gaps[n] = spot([P, 1, CHUNK], f"gap{n}0")
+            nc.scalar.activation(first_gaps[n][:, 0, :], picked[n, 0][:], ACT.Identity, bias=plan_sb[:, n : n + 1], scale=-1.0)
 
-        def pair_update(c, pair, index, slot=None):
-            update([(c, 2 * pair), (c, 2 * pair + 1)], index, gap[pair][:, :, span((c - 1) * CHUNK, CHUNK)], slot)
+        def pair_update(c, pair, index, slot=None, later=None):
+            update([(c, 2 * pair), (c, 2 * pair + 1)], index, gap[pair, min(c, 2)][:, :, span(c // 3 * CHUNK, CHUNK)], slot, later)
 
         def lone_update(c, n, index, count=1):
-            gaps = gap[n // 2][:, n % 2, span((c - 1) * CHUNK, count * CHUNK)]
+            gaps = gap[n // 2, 2][:, n % 2, span((c - 2) * CHUNK, count * CHUNK)]
             update([(c + k, n) for k in range(count)], index, gaps.rearrange("p (k j) -> p k j", k=count))
 
-        nc.vector.tensor_copy(v_w0[:], tab_w[0][:].bitcast(U32).indirect(offsets[:]))
+        pick_words(0, 0, CHUNK + 384)
         nc.vector.tensor_copy(v_s[:], tab_s[:].indirect(offsets[:]))
-        pick_words(0, CHUNK)
+        pick_words(1, 0, CHUNK)
         prepare_w1(0, 0, 0)
-        pick_words(CHUNK, 384, "w1_grouped00")
+        pick_words(1, CHUNK, 384, "w1_grouped00")
         prepare_w1(1, 0, SHARE)
         make_size(0, 0, (0, 1))
         prepare_w1(0, 1, P)
         make_size(0, 1, (2, 3))
         prepare_w1(1, 1, P)
+        pick_words(0, CHUNK + 384, 384, "w1_grouped11")
         make_size(1, 0, (0, 1))
-        for c in range(chunks):
-            z_grouped[c] = held([P, 2, CHUNK * PACK], BF16, f"z_grouped{c}", f"w1_raw{c % 2}{c // 2}")
         make_z(0, 0)
         first_gap(0)
         pick(0, 2 * CHUNK, 2 * CHUNK)
@@ -284,61 +301,69 @@ def tile_list_zoning_accessibility_step_kernel(
         quantize_z(0)
         pick(0, CHUNK, CHUNK, "w1_raw00")
         make_size(1, 1, (2, 3))
-        update([(0, 0)], 4, gap[0, 0][:])
-        pick_words(CHUNK + 384, 384, "gap00")
+        update([(0, 0)], 4, first_gaps[0][:])
+        pick_words(1, CHUNK + 384, 384, "gap00")
+        gap_rest(0, 1)
         put(0, 0)
         make_z(0, 1)
         make_z(1, 1)
-        make_size(0, 2, (4, 0))
-
-        first_gap(1)
-        pick(1, CHUNK, S - CHUNK)
-        update([(0, 1)], 5, gap[1, 0][:])
-        open_codes(1, "gap10")
-        quantize_z(1)
-        put(0, 1)
-        make_size(1, 2, (1, 2), "picked10")
-        gap_rest(0)
+        make_size(0, 2, (0, 1), "moved00")
         make_z(0, 2)
 
-        first_gap(2)
-        pick(2, CHUNK, S - CHUNK)
-        update([(0, 2)], 6, gap[2, 0][:])
-        put(0, 2)
-        make_size(0, 3, (3, 0), "picked20")
+        first_gap(1)
+        pick(1, 2 * CHUNK, 2 * CHUNK)
+        update([(0, 1)], 5, first_gaps[1][:])
+        pick(1, CHUNK, CHUNK)
+        open_codes(1)
+        quantize_z(1)
+        gap_rest(1, 1)
+        put(0, 1)
+        make_size(1, 2, (2, 3), "moved01")
         make_z(1, 2)
-        make_z(0, 3)
+
+        first_gap(2)
+        pick(2, 2 * CHUNK, 2 * CHUNK)
+        update([(0, 2)], 6, first_gaps[2][:])
+        pick(2, CHUNK, CHUNK, "gap20")
+        gap_rest(2, 1)
+        put(0, 2)
+        make_size(0, 3, (0, 1), "moved02")
 
         first_gap(3)
         pick(3, 2 * CHUNK, 2 * CHUNK)
-        update([(0, 3)], 7, gap[3, 0][:])
-        pick(3, CHUNK, CHUNK)
-        put(0, 3)
-        pair_update(1, 0, 4)
-        put(1, 0)
-        open_codes(2, "new03")
+        update([(0, 3)], 7, first_gaps[3][:])
+        open_codes(2)
         quantize_z(2)
+        pick(3, CHUNK, CHUNK)
+        pair_update(1, 0, 4, None, "picked30")
+        gap_rest(3, 1)
+        put(0, 3)
+        make_z(0, 3)
+        put(1, 0)
         put(1, 1)
-        gap_rest(1)
-        pair_update(1, 1, 5)
-        make_size(1, 3, (1, 2))
+        make_size(1, 3, (2, 3))
+        pair_update(1, 1, 7)
+        gap_rest(0, 2, "new03")
+        gap_rest(1, 2)
         put(1, 2)
         put(1, 3)
         make_z(1, 3)
         open_codes(3)
         quantize_z(3)
         pair_update(2, 0, 6)
+        gap_rest(2, 2, "picked30")
+        gap_rest(3, 2)
         put(2, 0)
         put(2, 1)
-        lone_update(2, 2, 7)
+        lone_update(2, 2, 5)
         put(2, 2)
         pair_update(3, 0, 4)
         for n in range(2):
             put(3, n)
             store(n)
-        lone_update(3, 2, 5)
+        lone_update(3, 2, 1)
         put(3, 2)
         store(2)
-        lone_update(2, 3, 6, count=2)
+        lone_update(2, 3, 0, count=2)
         put(2, 3)
         store(3)

@@ -154,7 +154,7 @@ def tile_list_zoning_accessibility_step_kernel(
         decay = {}
 
         def make_size(b, c, banks, slot=None):
-            decay[b, c] = spot([P, 2, PACK, STRIP], f"size{b}{c}", slot)
+            decay[b, c] = spot([P, PACK, CHUNK], f"size{b}{c}", slot)
             for u in range(2):
                 cols = span(c * CHUNK + u * STRIP, STRIP)
                 sep = bank([P, PACK, STRIP], banks[u], "sep")
@@ -170,16 +170,14 @@ def tile_list_zoning_accessibility_step_kernel(
                             start=a + i == 0,
                             stop=a + i == PACK,
                         )
+                strip = decay[b, c][:, :, span(u * STRIP, STRIP)]
+                nc.scalar.activation(strip, sep[:], ACT.Abs)
                 if (b, c) == (1, 0):
-                    nc.scalar.activation(decay[b, c][:, u], sep[:], ACT.Abs)
-                    nc.scalar.activation(decay[b, c][:, u], decay[b, c][:, u], ACT.Exp, scale=-1.0)
-                else:
-                    woven = decay[b, c][:, u].rearrange("p i c -> p (i c)").rearrange("p (c i) -> p c i", i=PACK)
-                    nc.scalar.activation(woven, sep[:].rearrange("p i c -> p c i"), ACT.Abs)
+                    nc.scalar.activation(strip, strip, ACT.Exp, scale=-1.0)
             if (b, c) != (1, 0):
                 size = decay[b, c]
                 if (b, c) == (1, 3):
-                    decay[b, c] = spot([P, 2, PACK, STRIP], f"decay{b}{c}", "w1_raw10")
+                    decay[b, c] = spot([P, PACK, CHUNK], f"decay{b}{c}", "w1_raw10")
                 nc.scalar.activation(decay[b, c][:], size[:], ACT.Exp, scale=-1.0)
 
         z_grouped, z_w, z_s = {}, {}, {}
@@ -189,7 +187,7 @@ def tile_list_zoning_accessibility_step_kernel(
                 grouped = z_grouped[0][:, b, span(u * STRIP * PACK, STRIP * PACK)]
                 nc.vector.tensor_tensor(
                     grouped.rearrange("p (c e i) -> p c i e", e=2, i=PACK),
-                    decay[b, 0][:, u].rearrange("p i (c e) -> p c i e", e=2),
+                    decay[b, 0][:, :, span(u * STRIP, STRIP)].rearrange("p i (c e) -> p c i e", e=2),
                     opp_sb[b, 0][:, :, span(u * STRIP, STRIP)].rearrange("p i (c e) -> p c i e", e=2),
                     ALU.mult,
                 )
@@ -198,9 +196,9 @@ def tile_list_zoning_accessibility_step_kernel(
             if b == 0:
                 z_grouped[c] = spot([P, 2, CHUNK * PACK], f"z_grouped{c}", None, BF16)
             nc.gpsimd.tensor_tensor(
-                z_grouped[c][:, b, :].rearrange("p (c i) -> p c i", i=PACK),
-                decay[b, c][:].rearrange("p u i c -> p (u i c)").rearrange("p (c i) -> p c i", i=PACK),
-                opp_sb[b, c].rearrange("p i c -> p c i"),
+                z_grouped[c][:, b, :].rearrange("p (c e i) -> p c i e", e=4, i=PACK),
+                decay[b, c][:].rearrange("p i (c e) -> p c i e", e=4),
+                opp_sb[b, c].rearrange("p i (c e) -> p c i e", e=4),
                 ALU.mult,
             )
 

@@ -118,10 +118,11 @@ def tile_list_zoning_accessibility_step_kernel(
             placed[right] = start + left_bytes
 
         heirs(0, "z_w1", 2048, "gap10", "picked11")
-        placed.update({"size13": 4096, "moved03": 4096, "new20": 4096})
-        heirs(8192, "z_w2", 2048, "gap30", "picked31")
-        placed.update({"w1_grouped11": 12288, "v_w0_640": 12288 - 1024, "z_grouped0": 12288 + 512})
-        placed.update({"picked01": 16384, "z_grouped1": 12800, "z_grouped2": 12800, "z_grouped3": 12800, "new22": 12800})
+        placed.update({"size13": 4096, "moved03": 4096})
+        placed.update({"pair_gap01": 17920, "z_grouped3": 17920, "new22": 17920, "new21": 17920 + 1024})
+        placed.update({"w1_grouped11": 12288, "v_w0_640": 12288 - 1024, "z_grouped0": 12800, "picked01": 12800})
+        placed.update({"z_grouped1": 13824, "z_grouped2": 13824, "new10": 13824, "pair_gap12": 13824})
+        placed.update({"picked30": 15872, "sums": 15872})
 
         def spot(shape, name, slot=None, dtype=F32):
             if name in placed:
@@ -194,11 +195,11 @@ def tile_list_zoning_accessibility_step_kernel(
 
         def make_z(b, c):
             if b == 0:
-                z_grouped[c] = spot([P, 2, CHUNK * PACK], f"z_grouped{c}", None, BF16)
+                z_grouped[c] = spot([P, 2, CHUNK * PACK], f"z_grouped{c}", "pair_gap01", BF16)
             nc.gpsimd.tensor_tensor(
-                z_grouped[c][:, b, :].rearrange("p (c e i) -> p c i e", e=4, i=PACK),
-                decay[b, c][:].rearrange("p i (c e) -> p c i e", e=4),
-                opp_sb[b, c].rearrange("p i (c e) -> p c i e", e=4),
+                z_grouped[c][:, b, :].rearrange("p (c e i) -> p c i e", e=2, i=PACK),
+                decay[b, c][:].rearrange("p i (c e) -> p c i e", e=2),
+                opp_sb[b, c].rearrange("p i (c e) -> p c i e", e=2),
                 ALU.mult,
             )
 
@@ -224,6 +225,10 @@ def tile_list_zoning_accessibility_step_kernel(
                 gap[n // 2, c] = spot([P, 2, c * CHUNK], f"pair_gap{n // 2}{c}", slot)
             into = gap[n // 2, c][:, n % 2, :]
             nc.scalar.activation(into, picked[n, c * CHUNK][:], ACT.Identity, bias=plan_sb[:, n : n + 1], scale=-1.0)
+
+        def add_plan(c, n, into, moved):
+            new[c, n] = into
+            nc.scalar.activation(into, moved, ACT.Identity, bias=plan_sb[:, n : n + 1])
 
         def update(parts, index, gaps, slot=None, later=None):
             step = bank([P, len(parts), CHUNK], index, "step")
@@ -255,10 +260,11 @@ def tile_list_zoning_accessibility_step_kernel(
                 new[c, n] = moved[:].rearrange("p k j -> p (k j)")
                 nc.scalar.activation(new[c, n], new[c, n], ACT.Identity, bias=plan_sb[:, n : n + 1])
             else:
-                sums = moved if later is None else held([P, len(parts), CHUNK], F32, "sums", later)
+                sums = moved if later is None else spot([P, len(parts), CHUNK], "sums")
                 for k, (c, n) in enumerate(parts):
-                    new[c, n] = sums[:, k, :]
-                    nc.scalar.activation(new[c, n], moved[:, k, :], ACT.Identity, bias=plan_sb[:, n : n + 1])
+                    if (c, n) == (2, 1):
+                        return lambda: add_plan(2, 1, spot([P, CHUNK], "new21")[:], moved[:, 1, :])
+                    add_plan(c, n, sums[:, k, :], moved[:, k, :])
 
         def put(c, n):
             count = new[c, n].shape[1]
@@ -273,11 +279,11 @@ def tile_list_zoning_accessibility_step_kernel(
             nc.scalar.activation(first_gaps[n][:, 0, :], picked[n, 0][:], ACT.Identity, bias=plan_sb[:, n : n + 1], scale=-1.0)
 
         def pair_update(c, pair, index, slot=None, later=None):
-            update([(c, 2 * pair), (c, 2 * pair + 1)], index, gap[pair, min(c, 2)][:, :, span(c // 3 * CHUNK, CHUNK)], slot, later)
+            return update([(c, 2 * pair), (c, 2 * pair + 1)], index, gap[pair, min(c, 2)][:, :, span(c // 3 * CHUNK, CHUNK)], slot, later)
 
-        def lone_update(c, n, index, count=1):
+        def lone_update(c, n, index, count=1, slot=None):
             gaps = gap[n // 2, 2][:, n % 2, span((c - 2) * CHUNK, count * CHUNK)]
-            update([(c + k, n) for k in range(count)], index, gaps.rearrange("p (k j) -> p k j", k=count))
+            update([(c + k, n) for k in range(count)], index, gaps.rearrange("p (k j) -> p k j", k=count), slot)
 
         pick_words(0, 0, CHUNK + 384)
         nc.vector.tensor_copy(v_s[:], tab_s[:].indirect(offsets[:]))
@@ -326,13 +332,13 @@ def tile_list_zoning_accessibility_step_kernel(
         gap_rest(2, 1)
         put(0, 2)
         make_size(0, 3, (0, 1), "moved02")
+        open_codes(2, "new02")
+        quantize_z(2)
 
         first_gap(3)
         pick(3, 2 * CHUNK, 2 * CHUNK)
         update([(0, 3)], 7, first_gaps[3][:])
-        open_codes(2)
-        quantize_z(2)
-        pick(3, CHUNK, CHUNK)
+        pick(3, CHUNK, CHUNK, "gap30")
         pair_update(1, 0, 4, None, "picked30")
         gap_rest(3, 1)
         put(0, 3)
@@ -345,23 +351,21 @@ def tile_list_zoning_accessibility_step_kernel(
         gap_rest(1, 2)
         put(1, 2)
         put(1, 3)
+        steps20 = pair_update(2, 0, 6, "gap30")
         make_z(1, 3)
-        open_codes(3)
-        quantize_z(3)
-        pair_update(2, 0, 6)
         gap_rest(2, 2, "picked30")
         gap_rest(3, 2)
         put(2, 0)
+        open_codes(3)
+        quantize_z(3)
+        steps20()
         put(2, 1)
         lone_update(2, 2, 5)
         put(2, 2)
-        pair_update(3, 0, 4)
-        for n in range(2):
+        for n in range(3):
+            lone_update(3, n, (4, 1, 2)[n])
             put(3, n)
             store(n)
-        lone_update(3, 2, 1)
-        put(3, 2)
-        store(2)
         lone_update(2, 3, 0, count=2)
         put(2, 3)
         store(3)

@@ -22,6 +22,7 @@ PASS = P * PACK
 CHUNK = 256
 STRIP = 128
 SHARE = 84
+RUN = 4
 
 
 def tile_list_zoning_accessibility_step_kernel(
@@ -154,6 +155,9 @@ def tile_list_zoning_accessibility_step_kernel(
 
         decay = {}
 
+        def in_runs(tile):
+            return tile[:].rearrange("p i c -> p (i c)").rearrange("p (c i e) -> p c i e", i=PACK, e=RUN)
+
         def make_size(b, c, banks, slot=None):
             decay[b, c] = spot([P, PACK, CHUNK], f"size{b}{c}", slot)
             for u in range(2):
@@ -171,10 +175,13 @@ def tile_list_zoning_accessibility_step_kernel(
                             start=a + i == 0,
                             stop=a + i == PACK,
                         )
-                strip = decay[b, c][:, :, span(u * STRIP, STRIP)]
-                nc.scalar.activation(strip, sep[:], ACT.Abs)
                 if (b, c) == (1, 0):
+                    strip = decay[b, c][:, :, span(u * STRIP, STRIP)]
+                    nc.scalar.activation(strip, sep[:], ACT.Abs)
                     nc.scalar.activation(strip, strip, ACT.Exp, scale=-1.0)
+                else:
+                    strip = in_runs(decay[b, c])[:, span(u * STRIP // RUN, STRIP // RUN)]
+                    nc.scalar.activation(strip, sep[:].rearrange("p i (c e) -> p c i e", e=RUN), ACT.Abs)
             if (b, c) != (1, 0):
                 size = decay[b, c]
                 if (b, c) == (1, 3):
@@ -197,9 +204,9 @@ def tile_list_zoning_accessibility_step_kernel(
             if b == 0:
                 z_grouped[c] = spot([P, 2, CHUNK * PACK], f"z_grouped{c}", "pair_gap01", BF16)
             nc.gpsimd.tensor_tensor(
-                z_grouped[c][:, b, :].rearrange("p (c e i) -> p c i e", e=2, i=PACK),
-                decay[b, c][:].rearrange("p i (c e) -> p c i e", e=2),
-                opp_sb[b, c].rearrange("p i (c e) -> p c i e", e=2),
+                z_grouped[c][:, b, :].rearrange("p (c e i) -> p c i e", e=RUN, i=PACK),
+                in_runs(decay[b, c]),
+                opp_sb[b, c].rearrange("p i (c e) -> p c i e", e=RUN),
                 ALU.mult,
             )
 

@@ -103,27 +103,18 @@ def tile_list_zoning_accessibility_step_kernel(
         nc.sync.dma_start(w2_w[:].bitcast(I32), w2_words.rearrange("a p c -> p a c").bitcast(I32))
         with nc.allow_non_contiguous_dma(reason="one plan value a partition and row tile"):
             nc.sync.dma_start(plan_sb[:], plan.rearrange("(n p) -> p n", p=P))
+        load_state(1)
         load_opp(0, 1)
         load_opp(1, 1)
-        load_state(1)
-        load_opp(0, 2)
         load_state(2)
-        load_opp(1, 2)
+        load_opp(0, 2)
         load_state(3)
+        load_opp(1, 2)
 
-        placed = {}
-
-        def heirs(start, left, left_bytes, donor, right):
-            placed[left] = start
-            placed[donor] = start + left_bytes - 512
-            placed[right] = start + left_bytes
-
-        heirs(0, "z_w1", 2048, "gap10", "picked11")
-        placed.update({"size13": 4096, "moved03": 4096})
-        placed.update({"pair_gap01": 17920, "z_grouped3": 17920, "new22": 17920, "new21": 17920 + 1024})
-        placed.update({"w1_grouped11": 12288, "v_w0_640": 12288 - 1024, "z_grouped0": 12800, "picked01": 12800})
-        placed.update({"z_grouped1": 13824, "z_grouped2": 13824, "new10": 13824, "pair_gap12": 13824})
-        placed.update({"picked30": 15872, "sums": 15872})
+        placed = {"w1_grouped11": 1024, "v_w0_640": 0, "v_w1_640": 1536, "z_first": 3072, "z_middle": 4096}
+        placed.update({"z_last": 4096, "picked31": 8192, "new02": 11264})
+        placed.update({"new00": 12288, "picked20": 13824, "gap_rest0": 14336})
+        placed.update({"moved00": 20480, "size12": 20480, "moved02": 20480, "size13": 20480, "moved13": 20480, "moved20": 21504})
 
         def spot(shape, name, slot=None, dtype=F32):
             if name in placed:
@@ -158,7 +149,7 @@ def tile_list_zoning_accessibility_step_kernel(
         def in_runs(tile):
             return tile[:].rearrange("p i c -> p (i c)").rearrange("p (c i e) -> p c i e", i=PACK, e=RUN)
 
-        def make_size(b, c, banks, slot=None):
+        def make_size(b, c, banks, slot=None, later=None):
             decay[b, c] = spot([P, PACK, CHUNK], f"size{b}{c}", slot)
             for u in range(2):
                 cols = span(c * CHUNK + u * STRIP, STRIP)
@@ -175,103 +166,130 @@ def tile_list_zoning_accessibility_step_kernel(
                             start=a + i == 0,
                             stop=a + i == PACK,
                         )
-                if (b, c) == (1, 0):
+                if (b, c) in ((1, 0), (1, 2)):
                     strip = decay[b, c][:, :, span(u * STRIP, STRIP)]
                     nc.scalar.activation(strip, sep[:], ACT.Abs)
-                    nc.scalar.activation(strip, strip, ACT.Exp, scale=-1.0)
+                    if c == 0:
+                        nc.scalar.activation(strip, strip, ACT.Exp, scale=-1.0)
                 else:
                     strip = in_runs(decay[b, c])[:, span(u * STRIP // RUN, STRIP // RUN)]
                     nc.scalar.activation(strip, sep[:].rearrange("p i (c e) -> p c i e", e=RUN), ACT.Abs)
             if (b, c) != (1, 0):
                 size = decay[b, c]
-                if (b, c) == (1, 3):
-                    decay[b, c] = spot([P, PACK, CHUNK], f"decay{b}{c}", "w1_raw10")
+                if later is not None:
+                    decay[b, c] = spot([P, PACK, CHUNK], f"decay{b}{c}", later)
                 nc.scalar.activation(decay[b, c][:], size[:], ACT.Exp, scale=-1.0)
 
-        z_grouped, z_w, z_s = {}, {}, {}
+        grouped_z, codes, scales = {}, {}, {}
 
-        def make_z_first(b):
-            for u in range(2):
-                grouped = z_grouped[0][:, b, span(u * STRIP * PACK, STRIP * PACK)]
-                nc.vector.tensor_tensor(
-                    grouped.rearrange("p (c e i) -> p c i e", e=2, i=PACK),
-                    decay[b, 0][:, :, span(u * STRIP, STRIP)].rearrange("p i (c e) -> p c i e", e=2),
-                    opp_sb[b, 0][:, :, span(u * STRIP, STRIP)].rearrange("p i (c e) -> p c i e", e=2),
-                    ALU.mult,
-                )
+        def open_z(name, first, count):
+            tile = spot([P, 2, count * CHUNK * PACK], name, None, BF16)
+            for k in range(count):
+                for b in range(2):
+                    grouped_z[b, first + k] = tile[:, b, span(k * CHUNK * PACK, CHUNK * PACK)]
+            return tile
 
-        def make_z(b, c):
-            if b == 0:
-                z_grouped[c] = spot([P, 2, CHUNK * PACK], f"z_grouped{c}", "pair_gap01", BF16)
-            nc.gpsimd.tensor_tensor(
-                z_grouped[c][:, b, :].rearrange("p (c e i) -> p c i e", e=RUN, i=PACK),
-                in_runs(decay[b, c]),
-                opp_sb[b, c].rearrange("p i (c e) -> p c i e", e=RUN),
+        def make_z_on_vector(b, c, first, count):
+            cols = span(first, count)
+            nc.vector.tensor_tensor(
+                grouped_z[b, c][:, span(first * PACK, count * PACK)].rearrange("p (c e i) -> p c i e", e=2, i=PACK),
+                decay[b, c][:, :, cols].rearrange("p i (c e) -> p c i e", e=2),
+                opp_sb[b, c][:, :, cols].rearrange("p i (c e) -> p c i e", e=2),
                 ALU.mult,
             )
 
-        def open_codes(c, slot=None):
-            z_w[c] = spot([P, 2 * CHUNK], f"z_w{c}", slot, U32)
-            z_s[c] = held([P, 2 * CHUNK], U8, f"z_s{c}")
+        def make_z(b, c, first=0, count=CHUNK):
+            nc.gpsimd.tensor_tensor(
+                grouped_z[b, c][:, span(first * PACK, count * PACK)].rearrange("p (c e i) -> p c i e", e=RUN, i=PACK),
+                in_runs(decay[b, c])[:, span(first // RUN, count // RUN)],
+                opp_sb[b, c][:, :, span(first, count)].rearrange("p i (c e) -> p c i e", e=RUN),
+                ALU.mult,
+            )
 
-        def quantize_z(c, b=None):
-            if b is None:
-                cols, source = slice(0, 2 * CHUNK), z_grouped[c][:].rearrange("p b x -> p (b x)")
-            else:
-                cols, source = span(b * CHUNK, CHUNK), z_grouped[c][:, b, :]
-            nc.vector.quantize_mx(out=z_w[c][:, cols].bitcast(FP8X4), scales=z_s[c][:, cols], in_=source)
+        def quantize_z(tile, first, count, slot=None):
+            words = held([P, 2, count * CHUNK], U32, f"z_w{first}", slot)
+            bytes_of_scale = held([P, 2, count * CHUNK], U8, f"z_s{first}")
+            nc.vector.quantize_mx(
+                out=words[:].rearrange("p b j -> p (b j)").bitcast(FP8X4),
+                scales=bytes_of_scale[:].rearrange("p b j -> p (b j)"),
+                in_=tile[:].rearrange("p b x -> p (b x)"),
+            )
+            codes[first], scales[first] = words, bytes_of_scale
 
-        picked, first_gaps, gap, new = {}, {}, {}, {}
+        def second_pass(into, n, b, first, count, start, stop):
+            c = {0: 0, 1: 1, 2: 1, 3: 3}[first // CHUNK]
+            cols = span(first - c * CHUNK, count)
+            nc.tensor.matmul_mx(
+                out=into,
+                lhsT=w2_w[:, b, span(2 * n * P, 2 * P)].bitcast(FP4X4),
+                lhsT_scale=w2_s[:, b, span(n * P, P)],
+                rhs=codes[c][:, b, cols].bitcast(FP8X4),
+                rhs_scale=scales[c][:, b, cols],
+                start=start,
+                stop=stop,
+            )
+
+        picked, first_gap, later_gap, new = {}, {}, {}, {}
 
         def pick(n, first, count, slot=None):
             picked[n, first] = spot([P, count], f"picked{n}{first // CHUNK}", slot)
             nc.vector.tensor_copy(picked[n, first][:], state[n][:].indirect(entries(first, count)))
 
-        def gap_rest(n, c, slot=None):
-            if n % 2 == 0:
-                gap[n // 2, c] = spot([P, 2, c * CHUNK], f"pair_gap{n // 2}{c}", slot)
-            into = gap[n // 2, c][:, n % 2, :]
-            nc.scalar.activation(into, picked[n, c * CHUNK][:], ACT.Identity, bias=plan_sb[:, n : n + 1], scale=-1.0)
+        def difference(into, values, n):
+            nc.scalar.activation(into, values, ACT.Identity, bias=plan_sb[:, n : n + 1], scale=-1.0)
 
-        def add_plan(c, n, into, moved):
-            new[c, n] = into
+        def make_first_gap(n):
+            if n % 2 == 0:
+                first_gap[n // 2] = held([P, 2, CHUNK], F32, f"first_gap{n // 2}")
+            difference(first_gap[n // 2][:, n % 2, :], picked[n, 0][:, 0:CHUNK], n)
+
+        def make_later_gap(n, slot=None):
+            if n % 2 == 0:
+                later_gap[n // 2] = spot([P, 2, S - CHUNK], f"gap_rest{n // 2}", slot)
+            values = picked[0, 0][:, CHUNK:S] if n == 0 else picked[n, CHUNK][:]
+            difference(later_gap[n // 2][:, n % 2, :], values, n)
+
+        def add_plan(into, moved, n):
             nc.scalar.activation(into, moved, ACT.Identity, bias=plan_sb[:, n : n + 1])
 
-        def update(parts, index, gaps, slot=None, later=None):
-            step = bank([P, len(parts), CHUNK], index, "step")
-            for k, (c, n) in enumerate(parts):
+        def first_product(pair, index):
+            step = bank([P, 2, CHUNK], index, "step")
+            for k in range(2):
                 for u in range(2):
                     for b in range(2):
-                        cols = span(b * CHUNK + u * STRIP, STRIP)
-                        nc.tensor.matmul_mx(
-                            out=step[:, k, span(u * STRIP, STRIP)],
-                            lhsT=w2_w[:, b, span(2 * n * P, 2 * P)].bitcast(FP4X4),
-                            lhsT_scale=w2_s[:, b, span(n * P, P)],
-                            rhs=z_w[c][:, cols].bitcast(FP8X4),
-                            rhs_scale=z_s[c][:, cols],
-                            start=k + u + b == 0,
-                            stop=k + u + b == len(parts) + 1,
-                        )
-            if parts[0][0] == 0:
-                n = parts[0][1]
-                moved = spot([P, 1, CHUNK], f"moved0{n}")
-                nc.vector.scalar_tensor_tensor(moved[:], step[:], -1.0, gaps, ALU.add, ALU.mult)
-                new[0, n] = spot([P, CHUNK], f"new0{n}")[:]
-                nc.scalar.activation(new[0, n], moved[:, 0, :], ACT.Identity, bias=plan_sb[:, n : n + 1])
-                return
-            moved = spot([P, len(parts), CHUNK], f"new{parts[0][0]}{parts[0][1]}", slot)
+                        into = step[:, k, span(u * STRIP, STRIP)]
+                        second_pass(into, 2 * pair + k, b, u * STRIP, STRIP, k + u + b == 0, k + u + b == 3)
+            moved = spot([P, 2, CHUNK], f"moved0{2 * pair}")
+            nc.vector.scalar_tensor_tensor(moved[:], step[:], -1.0, first_gap[pair][:], ALU.add, ALU.mult)
+            return moved
+
+        def first_sums(pair, moved):
+            sums = spot([P, 2, CHUNK], f"new0{2 * pair}")
+            for k in range(2):
+                new[0, 2 * pair + k] = sums[:, k, :]
+                add_plan(sums[:, k, :], moved[:, k, :], 2 * pair + k)
+
+        def open_update(c, n, count, index, slot=None):
+            first, width = c * CHUNK, count * CHUNK
+            step = bank([P, width], index, "step")
+            run = PASS if (c, count) == (1, 2) else STRIP
+            for u in range(width // run):
+                for b in range(2):
+                    last = u == width // run - 1 and b == 1
+                    second_pass(step[:, span(u * run, run)], n, b, first + u * run, run, u + b == 0, last)
+            moved = spot([P, width], f"moved{c}{n}", slot)
             nc.scalar.activation(moved[:], step[:], ACT.Copy, bias=-1.0)
-            nc.gpsimd.tensor_tensor(moved[:], moved[:], gaps, ALU.mult)
-            if parts[0][1] == parts[-1][1]:
-                c, n = parts[0]
-                new[c, n] = moved[:].rearrange("p k j -> p (k j)")
-                nc.scalar.activation(new[c, n], new[c, n], ACT.Identity, bias=plan_sb[:, n : n + 1])
-            else:
-                sums = moved if later is None else spot([P, len(parts), CHUNK], "sums")
-                for k, (c, n) in enumerate(parts):
-                    if (c, n) == (2, 1):
-                        return lambda: add_plan(2, 1, spot([P, CHUNK], "new21")[:], moved[:, 1, :])
-                    add_plan(c, n, sums[:, k, :], moved[:, k, :])
+            new[c, n] = moved[:]
+
+        def close_update(c, n):
+            moved = new[c, n]
+            gap = later_gap[n // 2][:, n % 2, span((c - 1) * CHUNK, moved.shape[1])]
+            nc.gpsimd.tensor_tensor(moved, moved, gap, ALU.mult)
+            add_plan(moved, moved, n)
+
+        def update(c, n, count, index, slot=None):
+            open_update(c, n, count, index, slot)
+            close_update(c, n)
 
         def put(c, n):
             count = new[c, n].shape[1]
@@ -279,18 +297,6 @@ def tile_list_zoning_accessibility_step_kernel(
 
         def store(n):
             nc.sync.dma_start(out[span(n * P, P), :], state[n][:])
-
-        def first_gap(n):
-            pick(n, 0, CHUNK)
-            first_gaps[n] = spot([P, 1, CHUNK], f"gap{n}0")
-            nc.scalar.activation(first_gaps[n][:, 0, :], picked[n, 0][:], ACT.Identity, bias=plan_sb[:, n : n + 1], scale=-1.0)
-
-        def pair_update(c, pair, index, slot=None, later=None):
-            return update([(c, 2 * pair), (c, 2 * pair + 1)], index, gap[pair, min(c, 2)][:, :, span(c // 3 * CHUNK, CHUNK)], slot, later)
-
-        def lone_update(c, n, index, count=1, slot=None):
-            gaps = gap[n // 2, 2][:, n % 2, span((c - 2) * CHUNK, count * CHUNK)]
-            update([(c + k, n) for k in range(count)], index, gaps.rearrange("p (k j) -> p k j", k=count), slot)
 
         pick_words(0, 0, CHUNK + 384)
         nc.vector.tensor_copy(v_s[:], tab_s[:].indirect(offsets[:]))
@@ -302,77 +308,69 @@ def tile_list_zoning_accessibility_step_kernel(
         prepare_w1(0, 1, P)
         make_size(0, 1, (2, 3))
         prepare_w1(1, 1, P)
-        pick_words(0, CHUNK + 384, 384, "w1_grouped11")
+        pick_words(0, CHUNK + 384, 384)
+        pick_words(1, CHUNK + 384, 384)
         make_size(1, 0, (0, 1))
+        z_first = open_z("z_first", 0, 1)
         make_z(0, 0)
-        first_gap(0)
-        pick(0, 2 * CHUNK, 2 * CHUNK)
-        make_z_first(1)
-        open_codes(0)
-        quantize_z(0)
-        pick(0, CHUNK, CHUNK, "w1_raw00")
+        pick(0, 0, S)
+        for u in range(2):
+            make_z_on_vector(1, 0, u * STRIP, STRIP)
+        quantize_z(z_first, 0, 1)
         make_size(1, 1, (2, 3))
-        update([(0, 0)], 4, first_gaps[0][:])
-        pick_words(1, CHUNK + 384, 384, "gap00")
-        gap_rest(0, 1)
-        put(0, 0)
+        z_middle = open_z("z_middle", 1, 2)
         make_z(0, 1)
         make_z(1, 1)
-        make_size(0, 2, (0, 1), "moved00")
+
+        make_first_gap(0)
+        pick(1, 0, CHUNK)
+        make_first_gap(1)
+        pick(1, CHUNK, S - CHUNK)
+        moved = first_product(0, 4)
+        make_size(0, 2, (0, 1), "picked10")
         make_z(0, 2)
-
-        first_gap(1)
-        pick(1, 2 * CHUNK, 2 * CHUNK)
-        update([(0, 1)], 5, first_gaps[1][:])
-        pick(1, CHUNK, CHUNK)
-        open_codes(1)
-        quantize_z(1)
-        gap_rest(1, 1)
+        pick(2, 0, CHUNK)
+        make_first_gap(2)
+        pick(2, CHUNK, S - CHUNK)
+        first_sums(0, moved)
+        put(0, 0)
         put(0, 1)
-        make_size(1, 2, (2, 3), "moved01")
-        make_z(1, 2)
+        make_size(1, 2, (2, 3))
+        make_later_gap(0)
+        make_later_gap(1)
 
-        first_gap(2)
-        pick(2, 2 * CHUNK, 2 * CHUNK)
-        update([(0, 2)], 6, first_gaps[2][:])
-        pick(2, CHUNK, CHUNK, "gap20")
-        gap_rest(2, 1)
+        pick(3, 0, CHUNK)
+        make_first_gap(3)
+        make_z_on_vector(1, 2, 0, CHUNK)
+        moved = first_product(1, 5)
+        quantize_z(z_middle, 1, 2)
+        pick(3, CHUNK, S - CHUNK)
+        first_sums(1, moved)
         put(0, 2)
-        make_size(0, 3, (0, 1), "moved02")
-        open_codes(2, "new02")
-        quantize_z(2)
-
-        first_gap(3)
-        pick(3, 2 * CHUNK, 2 * CHUNK)
-        update([(0, 3)], 7, first_gaps[3][:])
-        pick(3, CHUNK, CHUNK, "gap30")
-        pair_update(1, 0, 4, None, "picked30")
-        gap_rest(3, 1)
         put(0, 3)
+        make_size(0, 3, (0, 1), "picked30")
+        z_last = open_z("z_last", 3, 1)
         make_z(0, 3)
-        put(1, 0)
-        put(1, 1)
-        make_size(1, 3, (2, 3))
-        pair_update(1, 1, 7)
-        gap_rest(0, 2, "new03")
-        gap_rest(1, 2)
-        put(1, 2)
-        put(1, 3)
-        steps20 = pair_update(2, 0, 6, "gap30")
+        open_update(1, 0, 1, 4)
+        open_update(1, 1, 2, 6)
+        make_size(1, 3, (2, 3), None, "w1_raw10")
+        for n in range(2):
+            close_update(1, n)
+            put(1, n)
         make_z(1, 3)
-        gap_rest(2, 2, "picked30")
-        gap_rest(3, 2)
+        quantize_z(z_last, 3, 1)
+        make_later_gap(2, "first_gap1")
+        update(1, 2, 2, 7, "w1_raw01")
+        put(1, 2)
+        make_later_gap(3)
+        update(1, 3, 1, 5)
+        put(1, 3)
+        update(2, 0, 1, 4)
         put(2, 0)
-        open_codes(3)
-        quantize_z(3)
-        steps20()
-        put(2, 1)
-        lone_update(2, 2, 5)
-        put(2, 2)
         for n in range(3):
-            lone_update(3, n, (4, 1, 2)[n])
+            update(3, n, 1, n, f"tab_w{n % 2}" if n < 2 else None)
             put(3, n)
             store(n)
-        lone_update(2, 3, 0, count=2)
+        update(2, 3, 2, 3, "w1_raw11")
         put(2, 3)
         store(3)

@@ -100,10 +100,10 @@ def tile_list_zoning_accessibility_step_kernel(
             )
         load_state(0)
         load_opp(1, 0)
+        load_state(1)
         nc.sync.dma_start(w2_w[:].bitcast(I32), w2_words.rearrange("a p c -> p a c").bitcast(I32))
         with nc.allow_non_contiguous_dma(reason="one plan value a partition and row tile"):
             nc.sync.dma_start(plan_sb[:], plan.rearrange("(n p) -> p n", p=P))
-        load_state(1)
         load_opp(0, 1)
         load_opp(1, 1)
         load_state(2)
@@ -111,10 +111,11 @@ def tile_list_zoning_accessibility_step_kernel(
         load_state(3)
         load_opp(1, 2)
 
-        placed = {"w1_grouped11": 1024, "v_w0_640": 0, "v_w1_640": 1536, "z_first": 3072, "z_middle": 4096}
-        placed.update({"z_last": 4096, "picked31": 8192, "new02": 11264})
-        placed.update({"new00": 12288, "picked20": 13824, "gap_rest0": 14336})
-        placed.update({"moved00": 20480, "size12": 20480, "moved02": 20480, "size13": 20480, "moved13": 20480, "moved20": 21504})
+        placed = {"w1_grouped11": 0, "z_first": 0, "z_middle": 0, "picked31": 0, "new03": 4096}
+        placed.update({"moved10": 8192, "z_last": 8192})
+        placed.update({"decay02": 12288, "moved00": 15360, "size12": 16384, "moved03": 16384})
+        placed.update({"size13": 16384, "moved13": 16384, "moved20": 17408})
+        placed.update({"gap01": 20480, "moved02": 23040, "gap11": 23552})
 
         def spot(shape, name, slot=None, dtype=F32):
             if name in placed:
@@ -207,7 +208,7 @@ def tile_list_zoning_accessibility_step_kernel(
             )
 
         def quantize_z(tile, first, count, slot=None):
-            words = held([P, 2, count * CHUNK], U32, f"z_w{first}", slot)
+            words = spot([P, 2, count * CHUNK], f"z_w{first}", slot, U32)
             bytes_of_scale = held([P, 2, count * CHUNK], U8, f"z_s{first}")
             nc.vector.quantize_mx(
                 out=words[:].rearrange("p b j -> p (b j)").bitcast(FP8X4),
@@ -229,45 +230,50 @@ def tile_list_zoning_accessibility_step_kernel(
                 stop=stop,
             )
 
-        picked, first_gap, later_gap, new = {}, {}, {}, {}
+        picked, gap, new = {}, {}, {}
 
-        def pick(n, first, count, slot=None):
-            picked[n, first] = spot([P, count], f"picked{n}{first // CHUNK}", slot)
-            nc.vector.tensor_copy(picked[n, first][:], state[n][:].indirect(entries(first, count)))
+        def pick(n, c, count, slot=None):
+            picked[n, c] = spot([P, count * CHUNK], f"picked{n}{c}", slot)
+            nc.vector.tensor_copy(picked[n, c][:], state[n][:].indirect(entries(c * CHUNK, count * CHUNK)))
 
         def difference(into, values, n):
             nc.scalar.activation(into, values, ACT.Identity, bias=plan_sb[:, n : n + 1], scale=-1.0)
 
-        def make_first_gap(n):
-            if n % 2 == 0:
-                first_gap[n // 2] = held([P, 2, CHUNK], F32, f"first_gap{n // 2}")
-            difference(first_gap[n // 2][:, n % 2, :], picked[n, 0][:, 0:CHUNK], n)
-
-        def make_later_gap(n, slot=None):
-            if n % 2 == 0:
-                later_gap[n // 2] = spot([P, 2, S - CHUNK], f"gap_rest{n // 2}", slot)
-            values = picked[0, 0][:, CHUNK:S] if n == 0 else picked[n, CHUNK][:]
-            difference(later_gap[n // 2][:, n % 2, :], values, n)
+        def make_gap(n, c, count, source, slot=None):
+            tile = spot([P, count * CHUNK], f"gap{n}{c}", slot)
+            difference(tile[:], picked[n, source][:, span((c - source) * CHUNK, count * CHUNK)], n)
+            for k in range(count):
+                gap[n, c + k] = (tile, k)
 
         def add_plan(into, moved, n):
             nc.scalar.activation(into, moved, ACT.Identity, bias=plan_sb[:, n : n + 1])
 
-        def first_product(pair, index):
-            step = bank([P, 2, CHUNK], index, "step")
-            for k in range(2):
+        def make_wide_gap(n, slot=None):
+            tile = spot([P, 3 * CHUNK], f"gap{n}1", slot)
+            difference(tile[:, 0:CHUNK], picked[n, 1][:], n)
+            difference(tile[:, CHUNK:], picked[n, 2][:], n)
+            for k in range(3):
+                gap[n, 1 + k] = (tile, k)
+
+        def first_product(tiles, index, gaps):
+            step = bank([P, len(tiles), CHUNK], index, "step")
+            for k, n in enumerate(tiles):
                 for u in range(2):
                     for b in range(2):
                         into = step[:, k, span(u * STRIP, STRIP)]
-                        second_pass(into, 2 * pair + k, b, u * STRIP, STRIP, k + u + b == 0, k + u + b == 3)
-            moved = spot([P, 2, CHUNK], f"moved0{2 * pair}")
-            nc.vector.scalar_tensor_tensor(moved[:], step[:], -1.0, first_gap[pair][:], ALU.add, ALU.mult)
+                        second_pass(into, n, b, u * STRIP, STRIP, k + u + b == 0, k + u + b == len(tiles) + 1)
+            moved = spot([P, len(tiles), CHUNK], f"moved0{tiles[0]}")
+            nc.vector.scalar_tensor_tensor(moved[:], step[:], -1.0, gaps, ALU.add, ALU.mult)
             return moved
 
-        def first_sums(pair, moved):
-            sums = spot([P, 2, CHUNK], f"new0{2 * pair}")
-            for k in range(2):
-                new[0, 2 * pair + k] = sums[:, k, :]
-                add_plan(sums[:, k, :], moved[:, k, :], 2 * pair + k)
+        def first_sums(tiles, moved):
+            sums = spot([P, len(tiles), CHUNK], f"new0{tiles[0]}")
+            for k, n in enumerate(tiles):
+                new[0, n] = sums[:, k, :]
+                add_plan(sums[:, k, :], moved[:, k, :], n)
+
+        def first_update(tiles, index, gaps):
+            first_sums(tiles, first_product(tiles, index, gaps))
 
         def open_update(c, n, count, index, slot=None):
             first, width = c * CHUNK, count * CHUNK
@@ -281,11 +287,13 @@ def tile_list_zoning_accessibility_step_kernel(
             nc.scalar.activation(moved[:], step[:], ACT.Copy, bias=-1.0)
             new[c, n] = moved[:]
 
-        def close_update(c, n):
+        def close_update(c, n, slot=None):
             moved = new[c, n]
-            gap = later_gap[n // 2][:, n % 2, span((c - 1) * CHUNK, moved.shape[1])]
-            nc.gpsimd.tensor_tensor(moved, moved, gap, ALU.mult)
-            add_plan(moved, moved, n)
+            tile, k = gap[n, c]
+            nc.gpsimd.tensor_tensor(moved, moved, tile[:, span(k * CHUNK, moved.shape[1])], ALU.mult)
+            if slot is not None:
+                new[c, n] = held(list(moved.shape), F32, f"new{c}{n}", slot)[:]
+            add_plan(new[c, n], moved, n)
 
         def update(c, n, count, index, slot=None):
             open_update(c, n, count, index, slot)
@@ -298,22 +306,20 @@ def tile_list_zoning_accessibility_step_kernel(
         def store(n):
             nc.sync.dma_start(out[span(n * P, P), :], state[n][:])
 
-        pick_words(0, 0, CHUNK + 384)
+        pick_words(0, 0, S)
         nc.vector.tensor_copy(v_s[:], tab_s[:].indirect(offsets[:]))
         pick_words(1, 0, CHUNK)
         prepare_w1(0, 0, 0)
-        pick_words(1, CHUNK, 384, "w1_grouped00")
+        pick_words(1, CHUNK, S - CHUNK, "w1_grouped00")
         prepare_w1(1, 0, SHARE)
         make_size(0, 0, (0, 1))
         prepare_w1(0, 1, P)
         make_size(0, 1, (2, 3))
         prepare_w1(1, 1, P)
-        pick_words(0, CHUNK + 384, 384)
-        pick_words(1, CHUNK + 384, 384)
         make_size(1, 0, (0, 1))
         z_first = open_z("z_first", 0, 1)
         make_z(0, 0)
-        pick(0, 0, S)
+        pick(0, 0, chunks)
         for u in range(2):
             make_z_on_vector(1, 0, u * STRIP, STRIP)
         quantize_z(z_first, 0, 1)
@@ -322,53 +328,59 @@ def tile_list_zoning_accessibility_step_kernel(
         make_z(0, 1)
         make_z(1, 1)
 
-        make_first_gap(0)
-        pick(1, 0, CHUNK)
-        make_first_gap(1)
-        pick(1, CHUNK, S - CHUNK)
-        moved = first_product(0, 4)
-        make_size(0, 2, (0, 1), "picked10")
-        make_z(0, 2)
-        pick(2, 0, CHUNK)
-        make_first_gap(2)
-        pick(2, CHUNK, S - CHUNK)
-        first_sums(0, moved)
+        first_gaps = held([P, 2, CHUNK], F32, "first_gaps")
+        difference(first_gaps[:, 0, :], picked[0, 0][:, 0:CHUNK], 0)
+        pick(1, 0, 1)
+        difference(first_gaps[:, 1, :], picked[1, 0][:], 1)
+        pick(1, 2, 2)
+        first_update((0, 1), 4, first_gaps[:])
+        pick(1, 1, 1, "first_gaps")
         put(0, 0)
         put(0, 1)
+        make_size(0, 2, (0, 1), "picked10", "placed")
+        make_z(0, 2)
         make_size(1, 2, (2, 3))
-        make_later_gap(0)
-        make_later_gap(1)
 
-        pick(3, 0, CHUNK)
-        make_first_gap(3)
-        make_z_on_vector(1, 2, 0, CHUNK)
-        moved = first_product(1, 5)
-        quantize_z(z_middle, 1, 2)
-        pick(3, CHUNK, S - CHUNK)
-        first_sums(1, moved)
+        pick(2, 0, 1)
+        make_gap(2, 0, 1, 0)
+        pick(2, 2, 2)
+        first_update((2,), 5, gap[2, 0][0][:].rearrange("p (k j) -> p k j", k=1))
+        pick(2, 1, 1, "gap20")
         put(0, 2)
+        make_gap(0, 1, 3, 0)
+        make_wide_gap(1)
+        make_wide_gap(2, "new02")
+
+        pick(3, 0, 1)
+        make_gap(3, 0, 1, 0)
+        make_z_on_vector(1, 2, 0, CHUNK)
+        last_first = first_product((3,), 7, gap[3, 0][0][:].rearrange("p (k j) -> p k j", k=1))
+        quantize_z(z_middle, 1, 2)
+        pick(3, 1, 3)
+        first_sums((3,), last_first)
         put(0, 3)
         make_size(0, 3, (0, 1), "picked30")
-        z_last = open_z("z_last", 3, 1)
-        make_z(0, 3)
+
         open_update(1, 0, 1, 4)
         open_update(1, 1, 2, 6)
-        make_size(1, 3, (2, 3), None, "w1_raw10")
-        for n in range(2):
+        open_update(1, 2, 2, 5, "w1_raw01")
+        close_update(1, 0, "tab_w0")
+        put(1, 0)
+        for n in (1, 2):
             close_update(1, n)
             put(1, n)
+        z_last = open_z("z_last", 3, 1)
+        make_z(0, 3)
+        make_size(1, 3, (2, 3), None, "w1_raw10")
         make_z(1, 3)
         quantize_z(z_last, 3, 1)
-        make_later_gap(2, "first_gap1")
-        update(1, 2, 2, 7, "w1_raw01")
-        put(1, 2)
-        make_later_gap(3)
-        update(1, 3, 1, 5)
+        make_gap(3, 1, 3, 1, "tab_w0")
+        update(1, 3, 1, 7)
         put(1, 3)
         update(2, 0, 1, 4)
         put(2, 0)
         for n in range(3):
-            update(3, n, 1, n, f"tab_w{n % 2}" if n < 2 else None)
+            update(3, n, 1, n, "tab_w1" if n == 0 else None)
             put(3, n)
             store(n)
         update(2, 3, 2, 3, "w1_raw11")

@@ -23,6 +23,7 @@ CHUNK = 256
 STRIP = 128
 SHARE = 84
 RUN = 4
+HALF_REST = (S - CHUNK) // 2
 
 
 def tile_list_zoning_accessibility_step_kernel(
@@ -50,11 +51,13 @@ def tile_list_zoning_accessibility_step_kernel(
         tab_w = [held([P, T], I32, f"tab_w{a}") for a in range(2)]
         tab_s = keep.tile([P, T], U8, name="tab_s")
         w1_raw = {(a, b): held([P, PACK, PASS], F32, f"w1_raw{a}{b}") for a in range(2) for b in range(2)}
-        opp_tile = {(b, c): held([P, PACK, CHUNK * max(c, 1)], F32, f"opp{b}{c}") for b in range(2) for c in range(3)}
+        opp_tile = {(b, c): held([P, PACK, CHUNK * max(c, 1)], F32, f"opp{b}{c}") for b in range(2) for c in range(3 - b)}
+        opp_early = held([P, PACK, STRIP], F32, "opp_early")
+        opp_late = held([P, PACK, 2 * CHUNK - STRIP], F32, "opp_late")
         opp_sb = {(b, c): opp_tile[b, c][:] for b in range(2) for c in range(2)}
-        for b in range(2):
-            for c in (2, 3):
-                opp_sb[b, c] = opp_tile[b, 2][:, :, span((c - 2) * CHUNK, CHUNK)]
+        for c in (2, 3):
+            opp_sb[0, c] = opp_tile[0, 2][:, :, span((c - 2) * CHUNK, CHUNK)]
+        opp_sb[1, 3] = opp_late[:, :, span(STRIP, CHUNK)]
         state = [keep.tile([P, T], F32, name=f"state{n}") for n in range(n_tiles)]
         w2_w = held([P, 2, 2 * N], U8, "w2_w")
         w2_s = held([P, 2, N], U8, "w2_s")
@@ -77,6 +80,10 @@ def tile_list_zoning_accessibility_step_kernel(
             rows = opp[span(b * PASS, PASS), span(c * CHUNK, CHUNK * max(c, 1))]
             nc.sync.dma_start(opp_tile[b, c][:], rows.rearrange("(p i) j -> p i j", i=PACK))
 
+        def load_opp_part(tile, first):
+            rows = opp[span(PASS, PASS), span(first, tile.shape[2])]
+            nc.sync.dma_start(tile[:], rows.rearrange("(p i) j -> p i j", i=PACK))
+
         def load_state(n):
             nc.sync.dma_start(state[n][:], gT[span(n * P, P), :])
 
@@ -93,29 +100,30 @@ def tile_list_zoning_accessibility_step_kernel(
         load_w1(0, 1)
         load_w1(1, 1)
         load_opp(0, 0)
+        load_state(0)
+        load_opp(1, 0)
+        load_opp(0, 1)
+        load_state(1)
         for q in range(4):
             nc.sync.dma_start(
                 w2_s[32 * q : 32 * q + 4, :, :].bitcast(I32),
                 w2_scales[:, 4 * q : 4 * q + 4, :].rearrange("a r n -> r a n").bitcast(I32),
             )
-        load_state(0)
-        load_opp(1, 0)
-        load_state(1)
         nc.sync.dma_start(w2_w[:].bitcast(I32), w2_words.rearrange("a p c -> p a c").bitcast(I32))
         with nc.allow_non_contiguous_dma(reason="one plan value a partition and row tile"):
             nc.sync.dma_start(plan_sb[:], plan.rearrange("(n p) -> p n", p=P))
-        load_opp(0, 1)
         load_opp(1, 1)
         load_state(2)
         load_opp(0, 2)
+        load_opp_part(opp_early, 2 * CHUNK)
         load_state(3)
-        load_opp(1, 2)
+        load_opp_part(opp_late, 2 * CHUNK + STRIP)
 
-        placed = {"w1_grouped11": 0, "z_first": 0, "z_middle": 0, "picked31": 0, "new03": 4096}
-        placed.update({"moved10": 8192, "z_last": 8192})
+        placed = {"w1_grouped11": 0, "z_first": 0, "z_middle": 0, "picked31": 0, "new03": 3072, "z_last": 4096}
         placed.update({"decay02": 12288, "moved00": 15360, "size12": 16384, "moved03": 16384})
-        placed.update({"size13": 16384, "moved13": 16384, "moved20": 17408})
-        placed.update({"gap01": 20480, "moved02": 23040, "gap11": 23552})
+        placed.update({"late_strip": 8192, "moved10": 9728, "size13": 10240, "moved13": 10240, "moved20": 11264})
+        placed.update({"size03": 20480, "moved02": 24064, "gap01": 24576})
+        placed.update({"gap11": 27648, "picked30": 30208, "gap21": 30720})
 
         def spot(shape, name, slot=None, dtype=F32):
             if name in placed:
@@ -150,7 +158,10 @@ def tile_list_zoning_accessibility_step_kernel(
         def in_runs(tile):
             return tile[:].rearrange("p i c -> p (i c)").rearrange("p (c i e) -> p c i e", i=PACK, e=RUN)
 
-        def make_size(b, c, banks, slot=None, later=None):
+        def in_strips(tile):
+            return tile[:].rearrange("p i c -> p (i c)").rearrange("p (u i c) -> p u i c", u=2, i=PACK)
+
+        def make_size(b, c, banks, slot=None, later=None, now=True):
             decay[b, c] = spot([P, PACK, CHUNK], f"size{b}{c}", slot)
             for u in range(2):
                 cols = span(c * CHUNK + u * STRIP, STRIP)
@@ -167,7 +178,9 @@ def tile_list_zoning_accessibility_step_kernel(
                             start=a + i == 0,
                             stop=a + i == PACK,
                         )
-                if (b, c) in ((1, 0), (1, 2)):
+                if (b, c, u) == (1, 2, 1):
+                    nc.scalar.activation(in_strips(decay[b, c])[:, u], sep[:], ACT.Abs)
+                elif (b, c) == (1, 0):
                     strip = decay[b, c][:, :, span(u * STRIP, STRIP)]
                     nc.scalar.activation(strip, sep[:], ACT.Abs)
                     if c == 0:
@@ -175,7 +188,7 @@ def tile_list_zoning_accessibility_step_kernel(
                 else:
                     strip = in_runs(decay[b, c])[:, span(u * STRIP // RUN, STRIP // RUN)]
                     nc.scalar.activation(strip, sep[:].rearrange("p i (c e) -> p c i e", e=RUN), ACT.Abs)
-            if (b, c) != (1, 0):
+            if now and (b, c) != (1, 0):
                 size = decay[b, c]
                 if later is not None:
                     decay[b, c] = spot([P, PACK, CHUNK], f"decay{b}{c}", later)
@@ -190,19 +203,18 @@ def tile_list_zoning_accessibility_step_kernel(
                     grouped_z[b, first + k] = tile[:, b, span(k * CHUNK * PACK, CHUNK * PACK)]
             return tile
 
-        def make_z_on_vector(b, c, first, count):
-            cols = span(first, count)
+        def make_z_on_vector(b, c, first, count, factors):
             nc.vector.tensor_tensor(
                 grouped_z[b, c][:, span(first * PACK, count * PACK)].rearrange("p (c e i) -> p c i e", e=2, i=PACK),
-                decay[b, c][:, :, cols].rearrange("p i (c e) -> p c i e", e=2),
-                opp_sb[b, c][:, :, cols].rearrange("p i (c e) -> p c i e", e=2),
+                factors[0].rearrange("p i (c e) -> p c i e", e=2),
+                factors[1].rearrange("p i (c e) -> p c i e", e=2),
                 ALU.mult,
             )
 
-        def make_z(b, c, first=0, count=CHUNK):
+        def make_z(b, c, first=0, count=CHUNK, source=None):
             nc.gpsimd.tensor_tensor(
                 grouped_z[b, c][:, span(first * PACK, count * PACK)].rearrange("p (c e i) -> p c i e", e=RUN, i=PACK),
-                in_runs(decay[b, c])[:, span(first // RUN, count // RUN)],
+                in_runs(decay[b, c])[:, span(first // RUN, count // RUN)] if source is None else source,
                 opp_sb[b, c][:, :, span(first, count)].rearrange("p i (c e) -> p c i e", e=RUN),
                 ALU.mult,
             )
@@ -236,6 +248,10 @@ def tile_list_zoning_accessibility_step_kernel(
             picked[n, c] = spot([P, count * CHUNK], f"picked{n}{c}", slot)
             nc.vector.tensor_copy(picked[n, c][:], state[n][:].indirect(entries(c * CHUNK, count * CHUNK)))
 
+        def pick_half(n, k, slot=None):
+            picked[n, k] = spot([P, HALF_REST], f"picked{n}{k}", slot)
+            nc.vector.tensor_copy(picked[n, k][:], state[n][:].indirect(entries(CHUNK + (k - 1) * HALF_REST, HALF_REST)))
+
         def difference(into, values, n):
             nc.scalar.activation(into, values, ACT.Identity, bias=plan_sb[:, n : n + 1], scale=-1.0)
 
@@ -250,8 +266,8 @@ def tile_list_zoning_accessibility_step_kernel(
 
         def make_wide_gap(n, slot=None):
             tile = spot([P, 3 * CHUNK], f"gap{n}1", slot)
-            difference(tile[:, 0:CHUNK], picked[n, 1][:], n)
-            difference(tile[:, CHUNK:], picked[n, 2][:], n)
+            difference(tile[:, 0:HALF_REST], picked[n, 1][:], n)
+            difference(tile[:, HALF_REST:], picked[n, 2][:], n)
             for k in range(3):
                 gap[n, 1 + k] = (tile, k)
 
@@ -321,7 +337,8 @@ def tile_list_zoning_accessibility_step_kernel(
         make_z(0, 0)
         pick(0, 0, chunks)
         for u in range(2):
-            make_z_on_vector(1, 0, u * STRIP, STRIP)
+            cols = span(u * STRIP, STRIP)
+            make_z_on_vector(1, 0, u * STRIP, STRIP, (decay[1, 0][:, :, cols], opp_sb[1, 0][:, :, cols]))
         quantize_z(z_first, 0, 1)
         make_size(1, 1, (2, 3))
         z_middle = open_z("z_middle", 1, 2)
@@ -332,49 +349,60 @@ def tile_list_zoning_accessibility_step_kernel(
         difference(first_gaps[:, 0, :], picked[0, 0][:, 0:CHUNK], 0)
         pick(1, 0, 1)
         difference(first_gaps[:, 1, :], picked[1, 0][:], 1)
-        pick(1, 2, 2)
+        pick_half(1, 2)
         first_update((0, 1), 4, first_gaps[:])
-        pick(1, 1, 1, "first_gaps")
+        pick_half(1, 1, "first_gaps")
         put(0, 0)
         put(0, 1)
         make_size(0, 2, (0, 1), "picked10", "placed")
         make_z(0, 2)
         make_size(1, 2, (2, 3))
+        opp_sb[1, 2] = opp_early[:]
+        make_z(1, 2, 0, STRIP)
 
         pick(2, 0, 1)
         make_gap(2, 0, 1, 0)
-        pick(2, 2, 2)
+        pick_half(2, 2)
         first_update((2,), 5, gap[2, 0][0][:].rearrange("p (k j) -> p k j", k=1))
-        pick(2, 1, 1, "gap20")
+        pick_half(2, 1, "gap20")
         put(0, 2)
+        make_size(0, 3, (0, 1), now=False)
+        strips = [in_runs(decay[0, 3])[:, span(u * STRIP // RUN, STRIP // RUN)] for u in range(2)]
+        nc.scalar.activation(strips[0], strips[0], ACT.Exp, scale=-1.0)
         make_gap(0, 1, 3, 0)
-        make_wide_gap(1)
-        make_wide_gap(2, "new02")
 
         pick(3, 0, 1)
         make_gap(3, 0, 1, 0)
-        make_z_on_vector(1, 2, 0, CHUNK)
+        make_z_on_vector(1, 2, STRIP, STRIP, (in_strips(decay[1, 2])[:, 1], opp_late[:, :, 0:STRIP]))
         last_first = first_product((3,), 7, gap[3, 0][0][:].rearrange("p (k j) -> p k j", k=1))
         quantize_z(z_middle, 1, 2)
         pick(3, 1, 3)
         first_sums((3,), last_first)
         put(0, 3)
-        make_size(0, 3, (0, 1), "picked30")
+        make_wide_gap(1)
+        make_wide_gap(2)
+        z_last = open_z("z_last", 3, 1)
+        make_z(0, 3, 0, STRIP)
 
-        open_update(1, 0, 1, 4)
+        open_update(1, 0, 1, 4, "tab_w0")
         open_update(1, 1, 2, 6)
         open_update(1, 2, 2, 5, "w1_raw01")
-        close_update(1, 0, "tab_w0")
+        close_update(1, 0, "w1_raw00")
         put(1, 0)
-        for n in (1, 2):
-            close_update(1, n)
-            put(1, n)
-        z_last = open_z("z_last", 3, 1)
-        make_z(0, 3)
-        make_size(1, 3, (2, 3), None, "w1_raw10")
+        make_size(1, 3, (2, 3), now=False)
+        close_update(1, 1)
+        put(1, 1)
+        late_strip = spot([P, STRIP // RUN, PACK, RUN], "late_strip")
+        nc.scalar.activation(late_strip[:], strips[1], ACT.Exp, scale=-1.0)
+        last_size = decay[1, 3]
+        decay[1, 3] = held([P, PACK, CHUNK], F32, "decay13", "w1_raw10")
+        nc.scalar.activation(decay[1, 3][:], last_size[:], ACT.Exp, scale=-1.0)
+        close_update(1, 2)
+        put(1, 2)
+        make_z(0, 3, STRIP, STRIP, late_strip[:])
         make_z(1, 3)
         quantize_z(z_last, 3, 1)
-        make_gap(3, 1, 3, 1, "tab_w0")
+        make_gap(3, 1, 3, 1, "w1_raw00")
         update(1, 3, 1, 7)
         put(1, 3)
         update(2, 0, 1, 4)

@@ -51,13 +51,11 @@ def tile_list_zoning_accessibility_step_kernel(
         tab_w = [held([P, T], I32, f"tab_w{a}") for a in range(2)]
         tab_s = keep.tile([P, T], U8, name="tab_s")
         w1_raw = {(a, b): held([P, PACK, PASS], F32, f"w1_raw{a}{b}") for a in range(2) for b in range(2)}
-        opp_tile = {(b, c): held([P, PACK, CHUNK * max(c, 1)], F32, f"opp{b}{c}") for b in range(2) for c in range(3 - b)}
-        opp_early = held([P, PACK, STRIP], F32, "opp_early")
-        opp_late = held([P, PACK, 2 * CHUNK - STRIP], F32, "opp_late")
+        opp_tile = {(b, c): held([P, PACK, CHUNK * max(c, 1)], F32, f"opp{b}{c}") for b in range(2) for c in range(3)}
         opp_sb = {(b, c): opp_tile[b, c][:] for b in range(2) for c in range(2)}
-        for c in (2, 3):
-            opp_sb[0, c] = opp_tile[0, 2][:, :, span((c - 2) * CHUNK, CHUNK)]
-        opp_sb[1, 3] = opp_late[:, :, span(STRIP, CHUNK)]
+        for b in range(2):
+            for c in (2, 3):
+                opp_sb[b, c] = opp_tile[b, 2][:, :, span((c - 2) * CHUNK, CHUNK)]
         state = [keep.tile([P, T], F32, name=f"state{n}") for n in range(n_tiles)]
         w2_w = held([P, 2, 2 * N], U8, "w2_w")
         w2_s = held([P, 2, N], U8, "w2_s")
@@ -80,10 +78,6 @@ def tile_list_zoning_accessibility_step_kernel(
             rows = opp[span(b * PASS, PASS), span(c * CHUNK, CHUNK * max(c, 1))]
             nc.sync.dma_start(opp_tile[b, c][:], rows.rearrange("(p i) j -> p i j", i=PACK))
 
-        def load_opp_part(tile, first):
-            rows = opp[span(PASS, PASS), span(first, tile.shape[2])]
-            nc.sync.dma_start(tile[:], rows.rearrange("(p i) j -> p i j", i=PACK))
-
         def load_state(n):
             nc.sync.dma_start(state[n][:], gT[span(n * P, P), :])
 
@@ -100,24 +94,23 @@ def tile_list_zoning_accessibility_step_kernel(
         load_w1(0, 1)
         load_w1(1, 1)
         load_opp(0, 0)
-        load_state(0)
-        load_opp(1, 0)
-        load_opp(0, 1)
-        load_state(1)
         for q in range(4):
             nc.sync.dma_start(
                 w2_s[32 * q : 32 * q + 4, :, :].bitcast(I32),
                 w2_scales[:, 4 * q : 4 * q + 4, :].rearrange("a r n -> r a n").bitcast(I32),
             )
+        load_state(0)
+        load_opp(1, 0)
+        load_state(1)
         nc.sync.dma_start(w2_w[:].bitcast(I32), w2_words.rearrange("a p c -> p a c").bitcast(I32))
         with nc.allow_non_contiguous_dma(reason="one plan value a partition and row tile"):
             nc.sync.dma_start(plan_sb[:], plan.rearrange("(n p) -> p n", p=P))
+        load_opp(0, 1)
         load_opp(1, 1)
         load_state(2)
         load_opp(0, 2)
-        load_opp_part(opp_early, 2 * CHUNK)
         load_state(3)
-        load_opp_part(opp_late, 2 * CHUNK + STRIP)
+        load_opp(1, 2)
 
         placed = {"w1_grouped11": 0, "z_first": 0, "z_middle": 0, "picked31": 0, "new03": 3072, "z_last": 4096}
         placed.update({"decay02": 12288, "moved00": 15360, "size12": 16384, "moved03": 16384})
@@ -158,9 +151,6 @@ def tile_list_zoning_accessibility_step_kernel(
         def in_runs(tile):
             return tile[:].rearrange("p i c -> p (i c)").rearrange("p (c i e) -> p c i e", i=PACK, e=RUN)
 
-        def in_strips(tile):
-            return tile[:].rearrange("p i c -> p (i c)").rearrange("p (u i c) -> p u i c", u=2, i=PACK)
-
         def make_size(b, c, banks, slot=None, later=None, now=True):
             decay[b, c] = spot([P, PACK, CHUNK], f"size{b}{c}", slot)
             for u in range(2):
@@ -178,9 +168,7 @@ def tile_list_zoning_accessibility_step_kernel(
                             start=a + i == 0,
                             stop=a + i == PACK,
                         )
-                if (b, c, u) == (1, 2, 1):
-                    nc.scalar.activation(in_strips(decay[b, c])[:, u], sep[:], ACT.Abs)
-                elif (b, c) == (1, 0):
+                if (b, c) in ((1, 0), (1, 2)):
                     strip = decay[b, c][:, :, span(u * STRIP, STRIP)]
                     nc.scalar.activation(strip, sep[:], ACT.Abs)
                     if c == 0:
@@ -357,8 +345,6 @@ def tile_list_zoning_accessibility_step_kernel(
         make_size(0, 2, (0, 1), "picked10", "placed")
         make_z(0, 2)
         make_size(1, 2, (2, 3))
-        opp_sb[1, 2] = opp_early[:]
-        make_z(1, 2, 0, STRIP)
 
         pick(2, 0, 1)
         make_gap(2, 0, 1, 0)
@@ -373,7 +359,7 @@ def tile_list_zoning_accessibility_step_kernel(
 
         pick(3, 0, 1)
         make_gap(3, 0, 1, 0)
-        make_z_on_vector(1, 2, STRIP, STRIP, (in_strips(decay[1, 2])[:, 1], opp_late[:, :, 0:STRIP]))
+        make_z_on_vector(1, 2, 0, CHUNK, (decay[1, 2][:], opp_sb[1, 2]))
         last_first = first_product((3,), 7, gap[3, 0][0][:].rearrange("p (k j) -> p k j", k=1))
         quantize_z(z_middle, 1, 2)
         pick(3, 1, 3)

@@ -1,6 +1,7 @@
 from contextlib import ExitStack
 
 import concourse.mybir as mybir
+from concourse.masks import make_identity
 
 K, H, N, T, S = 1024, 1024, 512, 2048, 1024
 FLOPS = 2 * K * H * S + 2 * H * N * S
@@ -51,11 +52,8 @@ def tile_list_zoning_accessibility_step_kernel(
         tab_w = [held([P, T], I32, f"tab_w{a}") for a in range(2)]
         tab_s = keep.tile([P, T], U8, name="tab_s")
         w1_raw = {(a, b): held([P, PACK, PASS], F32, f"w1_raw{a}{b}") for a in range(2) for b in range(2)}
-        opp_tile = {(b, c): held([P, PACK, CHUNK * max(c, 1)], F32, f"opp{b}{c}") for b in range(2) for c in range(3)}
-        opp_sb = {(b, c): opp_tile[b, c][:] for b in range(2) for c in range(2)}
-        for b in range(2):
-            for c in (2, 3):
-                opp_sb[b, c] = opp_tile[b, 2][:, :, span((c - 2) * CHUNK, CHUNK)]
+        opp_tile = {(b, c): held([P, PACK, CHUNK], F32, f"opp{b}{c}") for b in range(2) for c in range(chunks)}
+        opp_sb = {key: tile[:] for key, tile in opp_tile.items()}
         state = [keep.tile([P, T], F32, name=f"state{n}") for n in range(n_tiles)]
         w2_w = held([P, 2, 2 * N], U8, "w2_w")
         w2_s = held([P, 2, N], U8, "w2_s")
@@ -67,6 +65,11 @@ def tile_list_zoning_accessibility_step_kernel(
         nc.vector.memset(tab_s[:].bitcast(I32), 0)
         nc.vector.memset(w2_s[:].bitcast(I32), 0)
 
+        identity = keep.tile([P, P], F32, name="identity")
+        make_identity(nc, identity[:])
+        plan_rows = keep.tile([P, P], F32, name="plan_rows")
+        nc.gpsimd.memset(plan_rows[:], 0.0)
+
         def load_tab(a):
             nc.sync.dma_start(tab_w[a][:], tab_words[a].rearrange("p t i -> p (t i)").bitcast(I32))
 
@@ -75,7 +78,7 @@ def tile_list_zoning_accessibility_step_kernel(
             nc.sync.dma_start(w1_raw[a, b][:], rows.rearrange("(p i) c -> p i c", i=PACK))
 
         def load_opp(b, c):
-            rows = opp[span(b * PASS, PASS), span(c * CHUNK, CHUNK * max(c, 1))]
+            rows = opp[span(b * PASS, PASS), span(c * CHUNK, CHUNK)]
             nc.sync.dma_start(opp_tile[b, c][:], rows.rearrange("(p i) j -> p i j", i=PACK))
 
         def load_state(n):
@@ -88,6 +91,7 @@ def tile_list_zoning_accessibility_step_kernel(
                 tab_s[32 * q : 32 * q + 8, :].bitcast(I32),
                 tab_scales[:, 4 * q : 4 * q + 4, :].bitcast(I32),
             )
+        nc.sync.dma_start(plan_rows[0:n_tiles, :], plan.rearrange("(n p) -> n p", p=P))
         load_w1(0, 0)
         load_tab(1)
         load_w1(1, 0)
@@ -103,17 +107,17 @@ def tile_list_zoning_accessibility_step_kernel(
         load_opp(1, 0)
         load_state(1)
         nc.sync.dma_start(w2_w[:].bitcast(I32), w2_words.rearrange("a p c -> p a c").bitcast(I32))
-        with nc.allow_non_contiguous_dma(reason="one plan value a partition and row tile"):
-            nc.sync.dma_start(plan_sb[:], plan.rearrange("(n p) -> p n", p=P))
         load_opp(0, 1)
         load_opp(1, 1)
         load_state(2)
         load_opp(0, 2)
-        load_state(3)
         load_opp(1, 2)
+        load_state(3)
+        load_opp(0, 3)
+        load_opp(1, 3)
 
-        placed = {"w1_grouped11": 0, "z_first": 0, "z_middle": 0, "picked31": 0, "new03": 3072, "z_last": 4096}
-        placed.update({"decay02": 12288, "moved00": 15360, "size12": 16384, "moved03": 16384})
+        placed = {"w1_grouped11": 0, "z_first": 0, "z_middle": 0, "picked32": 0, "new03": 3072, "z_last": 4096}
+        placed.update({"decay02": 12288, "moved00": 15360, "size12": 16384})
         placed.update({"late_strip": 8192, "moved10": 9728, "size13": 10240, "moved13": 10240, "moved20": 11264})
         placed.update({"size03": 20480, "moved02": 24064, "gap01": 24576})
         placed.update({"gap11": 27648, "picked30": 30208, "gap21": 30720})
@@ -122,6 +126,10 @@ def tile_list_zoning_accessibility_step_kernel(
             if name in placed:
                 return shared.tile(shape, dtype, name=name, offset=placed[name], align_bytes=64)
             return held(shape, dtype, name, slot)
+
+        plan_turned = bank([P, P], 7, "plan_turned")
+        nc.tensor.transpose(plan_turned[:], plan_rows[:], identity[:])
+        nc.scalar.copy(plan_sb[:], plan_turned[:, 0:n_tiles])
 
         v_s = held([P, S], U8, "v_s")
         v_w = {}
@@ -168,7 +176,7 @@ def tile_list_zoning_accessibility_step_kernel(
                             start=a + i == 0,
                             stop=a + i == PACK,
                         )
-                if (b, c) in ((1, 0), (1, 2)):
+                if (b, c) == (1, 0):
                     strip = decay[b, c][:, :, span(u * STRIP, STRIP)]
                     nc.scalar.activation(strip, sep[:], ACT.Abs)
                     if c == 0:
@@ -345,6 +353,7 @@ def tile_list_zoning_accessibility_step_kernel(
         make_size(0, 2, (0, 1), "picked10", "placed")
         make_z(0, 2)
         make_size(1, 2, (2, 3))
+        make_z(1, 2)
 
         pick(2, 0, 1)
         make_gap(2, 0, 1, 0)
@@ -359,10 +368,10 @@ def tile_list_zoning_accessibility_step_kernel(
 
         pick(3, 0, 1)
         make_gap(3, 0, 1, 0)
-        make_z_on_vector(1, 2, 0, CHUNK, (decay[1, 2][:], opp_sb[1, 2]))
+        pick_half(3, 1)
         last_first = first_product((3,), 7, gap[3, 0][0][:].rearrange("p (k j) -> p k j", k=1))
-        quantize_z(z_middle, 1, 2)
-        pick(3, 1, 3)
+        quantize_z(z_middle, 1, 2, "gap30")
+        pick_half(3, 2)
         first_sums((3,), last_first)
         put(0, 3)
         make_wide_gap(1)
@@ -388,7 +397,7 @@ def tile_list_zoning_accessibility_step_kernel(
         make_z(0, 3, STRIP, STRIP, late_strip[:])
         make_z(1, 3)
         quantize_z(z_last, 3, 1)
-        make_gap(3, 1, 3, 1, "w1_raw00")
+        make_wide_gap(3, "w1_raw00")
         update(1, 3, 1, 7)
         put(1, 3)
         update(2, 0, 1, 4)

@@ -52,10 +52,11 @@ def tile_list_zoning_accessibility_step_kernel(
         tab_w = [held([P, T], I32, f"tab_w{a}") for a in range(2)]
         tab_s = keep.tile([P, T], U8, name="tab_s")
         w1_raw = {(a, b): held([P, PACK, PASS], F32, f"w1_raw{a}{b}") for a in range(2) for b in range(2)}
-        opp_tile = {(b, c): held([P, PACK, CHUNK], F32, f"opp{b}{c}") for b in range(2) for c in range(chunks)}
+        opp_tile = {(b, c): held([P, PACK, CHUNK], F32, f"opp{b}{c}") for b in range(2) for c in range(chunks) if (b, c) != (1, 2)}
+        opp_strip = [held([P, PACK, STRIP], F32, f"opp_strip{u}") for u in range(2)]
         opp_sb = {key: tile[:] for key, tile in opp_tile.items()}
         state = [keep.tile([P, T], F32, name=f"state{n}") for n in range(n_tiles)]
-        w2_w = held([P, 2, 2 * N], U8, "w2_w")
+        w2_w = [held([P, 2, N], U8, f"w2_w{pair}") for pair in range(2)]
         w2_s = held([P, 2, N], U8, "w2_s")
         plan_sb = keep.tile([P, n_tiles], F32, name="plan_sb")
 
@@ -81,6 +82,14 @@ def tile_list_zoning_accessibility_step_kernel(
             rows = opp[span(b * PASS, PASS), span(c * CHUNK, CHUNK)]
             nc.sync.dma_start(opp_tile[b, c][:], rows.rearrange("(p i) j -> p i j", i=PACK))
 
+        def load_opp_strip(u):
+            rows = opp[span(PASS, PASS), span(2 * CHUNK + u * STRIP, STRIP)]
+            nc.sync.dma_start(opp_strip[u][:], rows.rearrange("(p i) j -> p i j", i=PACK))
+
+        def load_w2(pair):
+            words = w2_words[:, :, span(pair * N, N)].rearrange("a p c -> p a c")
+            nc.sync.dma_start(w2_w[pair][:].bitcast(I32), words.bitcast(I32))
+
         def load_state(n):
             nc.sync.dma_start(state[n][:], gT[span(n * P, P), :])
 
@@ -105,20 +114,23 @@ def tile_list_zoning_accessibility_step_kernel(
             )
         load_state(0)
         load_opp(1, 0)
+        load_w2(0)
         load_state(1)
-        nc.sync.dma_start(w2_w[:].bitcast(I32), w2_words.rearrange("a p c -> p a c").bitcast(I32))
         load_opp(0, 1)
+        load_w2(1)
         load_opp(1, 1)
         load_state(2)
         load_opp(0, 2)
-        load_opp(1, 2)
+        load_opp_strip(0)
         load_state(3)
+        load_opp_strip(1)
         load_opp(0, 3)
         load_opp(1, 3)
 
-        placed = {"w1_grouped11": 0, "z_first": 0, "z_middle": 0, "picked32": 0, "new03": 3072, "z_last": 4096}
-        placed.update({"decay02": 12288, "moved00": 15360, "size12": 16384})
-        placed.update({"late_strip": 8192, "moved10": 9728, "size13": 10240, "moved13": 10240, "moved20": 11264})
+        placed = {"v_w1_640": 0, "w1_grouped11": 1024, "z_first": 1536, "z_middle": 1536, "picked31": 1536}
+        placed.update({"new03": 4608, "z_last": 5632})
+        placed.update({"size02": 12288, "moved00": 15360, "size12": 16384})
+        placed.update({"late_strip": 12288, "moved10": 13824, "size13": 14336, "moved13": 14336, "moved20": 15360})
         placed.update({"size03": 20480, "moved02": 24064, "gap01": 24576})
         placed.update({"gap11": 27648, "picked30": 30208, "gap21": 30720})
 
@@ -159,8 +171,13 @@ def tile_list_zoning_accessibility_step_kernel(
         def in_runs(tile):
             return tile[:].rearrange("p i c -> p (i c)").rearrange("p (c i e) -> p c i e", i=PACK, e=RUN)
 
+        def second_strip(tile):
+            return tile[:].rearrange("p i c -> p (i c)").rearrange("p (u i c) -> p u i c", u=2, i=PACK)[:, 1]
+
         def make_size(b, c, banks, slot=None, later=None, now=True):
-            decay[b, c] = spot([P, PACK, CHUNK], f"size{b}{c}", slot)
+            size = decay[b, c] = spot([P, PACK, CHUNK], f"size{b}{c}", slot)
+            if (b, c) == (1, 0):
+                decay[b, c] = held([P, PACK, CHUNK], F32, "decay10")
             for u in range(2):
                 cols = span(c * CHUNK + u * STRIP, STRIP)
                 sep = bank([P, PACK, STRIP], banks[u], "sep")
@@ -177,18 +194,22 @@ def tile_list_zoning_accessibility_step_kernel(
                             stop=a + i == PACK,
                         )
                 if (b, c) == (1, 0):
-                    strip = decay[b, c][:, :, span(u * STRIP, STRIP)]
-                    nc.scalar.activation(strip, sep[:], ACT.Abs)
-                    if c == 0:
-                        nc.scalar.activation(strip, strip, ACT.Exp, scale=-1.0)
+                    strip = span(u * STRIP, STRIP)
+                    nc.scalar.activation(size[:, :, strip], sep[:], ACT.Abs)
+                    nc.scalar.activation(decay[b, c][:, :, strip], size[:, :, strip], ACT.Exp, scale=-1.0)
+                elif (b, c, u) == (1, 2, 1):
+                    nc.scalar.activation(second_strip(size), sep[:], ACT.Abs)
                 else:
-                    strip = in_runs(decay[b, c])[:, span(u * STRIP // RUN, STRIP // RUN)]
+                    strip = in_runs(size)[:, span(u * STRIP // RUN, STRIP // RUN)]
                     nc.scalar.activation(strip, sep[:].rearrange("p i (c e) -> p c i e", e=RUN), ACT.Abs)
             if now and (b, c) != (1, 0):
-                size = decay[b, c]
-                if later is not None:
-                    decay[b, c] = spot([P, PACK, CHUNK], f"decay{b}{c}", later)
-                nc.scalar.activation(decay[b, c][:], size[:], ACT.Exp, scale=-1.0)
+                make_decay(b, c)
+
+        def make_decay(b, c, slot=None):
+            size = decay[b, c]
+            if slot is not None:
+                decay[b, c] = held([P, PACK, CHUNK], F32, f"decay{b}{c}", slot)
+            nc.scalar.activation(decay[b, c][:], size[:], ACT.Exp, scale=-1.0)
 
         grouped_z, codes, scales = {}, {}, {}
 
@@ -230,7 +251,7 @@ def tile_list_zoning_accessibility_step_kernel(
             cols = span(first - c * CHUNK, count)
             nc.tensor.matmul_mx(
                 out=into,
-                lhsT=w2_w[:, b, span(2 * n * P, 2 * P)].bitcast(FP4X4),
+                lhsT=w2_w[n // 2][:, b, span(2 * (n % 2) * P, 2 * P)].bitcast(FP4X4),
                 lhsT_scale=w2_s[:, b, span(n * P, P)],
                 rhs=codes[c][:, b, cols].bitcast(FP8X4),
                 rhs_scale=scales[c][:, b, cols],
@@ -267,14 +288,14 @@ def tile_list_zoning_accessibility_step_kernel(
             for k in range(3):
                 gap[n, 1 + k] = (tile, k)
 
-        def first_product(tiles, index, gaps):
+        def first_product(tiles, index, gaps, slot=None):
             step = bank([P, len(tiles), CHUNK], index, "step")
             for k, n in enumerate(tiles):
                 for u in range(2):
                     for b in range(2):
                         into = step[:, k, span(u * STRIP, STRIP)]
                         second_pass(into, n, b, u * STRIP, STRIP, k + u + b == 0, k + u + b == len(tiles) + 1)
-            moved = spot([P, len(tiles), CHUNK], f"moved0{tiles[0]}")
+            moved = spot([P, len(tiles), CHUNK], f"moved0{tiles[0]}", slot)
             nc.vector.scalar_tensor_tensor(moved[:], step[:], -1.0, gaps, ALU.add, ALU.mult)
             return moved
 
@@ -322,13 +343,15 @@ def tile_list_zoning_accessibility_step_kernel(
         nc.vector.tensor_copy(v_s[:], tab_s[:].indirect(offsets[:]))
         pick_words(1, 0, CHUNK)
         prepare_w1(0, 0, 0)
-        pick_words(1, CHUNK, S - CHUNK, "w1_grouped00")
+        pick_words(1, CHUNK, HALF_REST, "w1_grouped00")
         prepare_w1(1, 0, SHARE)
         make_size(0, 0, (0, 1))
         prepare_w1(0, 1, P)
-        make_size(0, 1, (2, 3))
+        make_size(0, 1, (2, 3), now=False)
         prepare_w1(1, 1, P)
-        make_size(1, 0, (0, 1))
+        pick_words(1, CHUNK + HALF_REST, HALF_REST)
+        make_size(1, 0, (0, 1), later="now")
+        make_decay(0, 1, "size10")
         z_first = open_z("z_first", 0, 1)
         make_z(0, 0)
         pick(0, 0, chunks)
@@ -336,27 +359,30 @@ def tile_list_zoning_accessibility_step_kernel(
             cols = span(u * STRIP, STRIP)
             make_z_on_vector(1, 0, u * STRIP, STRIP, (decay[1, 0][:, :, cols], opp_sb[1, 0][:, :, cols]))
         quantize_z(z_first, 0, 1)
-        make_size(1, 1, (2, 3))
+        make_size(1, 1, (2, 3), now=False)
         z_middle = open_z("z_middle", 1, 2)
         make_z(0, 1)
-        make_z(1, 1)
 
         first_gaps = held([P, 2, CHUNK], F32, "first_gaps")
         difference(first_gaps[:, 0, :], picked[0, 0][:, 0:CHUNK], 0)
         pick(1, 0, 1)
         difference(first_gaps[:, 1, :], picked[1, 0][:], 1)
+        make_decay(1, 1, "picked10")
+        make_z(1, 1)
         pick_half(1, 2)
         first_update((0, 1), 4, first_gaps[:])
         pick_half(1, 1, "first_gaps")
         put(0, 0)
         put(0, 1)
-        make_size(0, 2, (0, 1), "picked10", "placed")
+        make_size(0, 2, (0, 1))
         make_z(0, 2)
-        make_size(1, 2, (2, 3))
-        make_z(1, 2)
+        make_size(1, 2, (2, 3), now=False)
 
         pick(2, 0, 1)
         make_gap(2, 0, 1, 0)
+        make_decay(1, 2, "picked20")
+        opp_sb[1, 2] = opp_strip[0][:]
+        make_z(1, 2, 0, STRIP)
         pick_half(2, 2)
         first_update((2,), 5, gap[2, 0][0][:].rearrange("p (k j) -> p k j", k=1))
         pick_half(2, 1, "gap20")
@@ -368,10 +394,10 @@ def tile_list_zoning_accessibility_step_kernel(
 
         pick(3, 0, 1)
         make_gap(3, 0, 1, 0)
-        pick_half(3, 1)
-        last_first = first_product((3,), 7, gap[3, 0][0][:].rearrange("p (k j) -> p k j", k=1))
-        quantize_z(z_middle, 1, 2, "gap30")
-        pick_half(3, 2)
+        make_z_on_vector(1, 2, STRIP, STRIP, (second_strip(decay[1, 2]), opp_strip[1][:]))
+        last_first = first_product((3,), 7, gap[3, 0][0][:].rearrange("p (k j) -> p k j", k=1), "picked20")
+        quantize_z(z_middle, 1, 2)
+        pick(3, 1, 3)
         first_sums((3,), last_first)
         put(0, 3)
         make_wide_gap(1)
@@ -397,7 +423,7 @@ def tile_list_zoning_accessibility_step_kernel(
         make_z(0, 3, STRIP, STRIP, late_strip[:])
         make_z(1, 3)
         quantize_z(z_last, 3, 1)
-        make_wide_gap(3, "w1_raw00")
+        make_gap(3, 1, 3, 1, "w1_raw00")
         update(1, 3, 1, 7)
         put(1, 3)
         update(2, 0, 1, 4)

@@ -130,7 +130,7 @@ def tile_list_zoning_accessibility_step_kernel(
         placed = {"v_w1_640": 0, "w1_grouped11": 1024, "z_first": 1536, "z_middle": 1536, "picked31": 1536}
         placed.update({"new03": 4608, "z_last": 5632})
         placed.update({"size02": 12288, "moved00": 15360, "size12": 16384})
-        placed.update({"late_strip": 12288, "moved10": 13824, "size13": 14336, "moved13": 14336, "moved20": 15360})
+        placed.update({"late_strip": 12288, "moved10": 13824, "size13": 14336, "moved20": 14336})
         placed.update({"size03": 20480, "moved02": 24064, "gap01": 24576})
         placed.update({"gap11": 27648, "picked30": 30208, "gap21": 30720})
 
@@ -359,7 +359,7 @@ def tile_list_zoning_accessibility_step_kernel(
             cols = span(u * STRIP, STRIP)
             make_z_on_vector(1, 0, u * STRIP, STRIP, (decay[1, 0][:, :, cols], opp_sb[1, 0][:, :, cols]))
         quantize_z(z_first, 0, 1)
-        make_size(1, 1, (2, 3), now=False)
+        make_size(1, 1, (0, 1), now=False)
         z_middle = open_z("z_middle", 1, 2)
         make_z(0, 1)
 
@@ -376,7 +376,7 @@ def tile_list_zoning_accessibility_step_kernel(
         put(0, 1)
         make_size(0, 2, (0, 1))
         make_z(0, 2)
-        make_size(1, 2, (2, 3), now=False)
+        make_size(1, 2, (0, 1), now=False)
 
         pick(2, 0, 1)
         make_gap(2, 0, 1, 0)
@@ -410,7 +410,7 @@ def tile_list_zoning_accessibility_step_kernel(
         open_update(1, 2, 2, 5, "w1_raw01")
         close_update(1, 0, "w1_raw00")
         put(1, 0)
-        make_size(1, 3, (2, 3), now=False)
+        make_size(1, 3, (0, 1), now=False)
         close_update(1, 1)
         put(1, 1)
         late_strip = spot([P, STRIP // RUN, PACK, RUN], "late_strip")
@@ -421,10 +421,10 @@ def tile_list_zoning_accessibility_step_kernel(
         close_update(1, 2)
         put(1, 2)
         make_z(0, 3, STRIP, STRIP, late_strip[:])
+        make_gap(3, 1, 3, 1, "w1_raw00")
+        update(1, 3, 1, 7, "tab_w0")
         make_z(1, 3)
         quantize_z(z_last, 3, 1)
-        make_gap(3, 1, 3, 1, "w1_raw00")
-        update(1, 3, 1, 7)
         put(1, 3)
         update(2, 0, 1, 4)
         put(2, 0)

@@ -107,13 +107,13 @@ def tile_list_zoning_accessibility_step_kernel(
         load_w1(0, 1)
         load_w1(1, 1)
         load_opp(0, 0)
-        for q in range(4):
-            nc.sync.dma_start(
-                w2_s[32 * q : 32 * q + 4, :, :].bitcast(I32),
-                w2_scales[:, 4 * q : 4 * q + 4, :].rearrange("a r n -> r a n").bitcast(I32),
-            )
         load_state(0)
         load_opp(1, 0)
+        for r in range(4):
+            nc.sync.dma_start(
+                w2_s[r:P:32, :, :].bitcast(I32),
+                w2_scales[:, r:16:4, :].rearrange("a q n -> q a n").bitcast(I32),
+            )
         load_w2(0)
         load_state(1)
         load_opp(0, 1)

@@ -52,8 +52,9 @@ def tile_list_zoning_accessibility_step_kernel(
         tab_w = [held([P, T], I32, f"tab_w{a}") for a in range(2)]
         tab_s = keep.tile([P, T], U8, name="tab_s")
         w1_raw = {(a, b): held([P, PACK, PASS], F32, f"w1_raw{a}{b}") for a in range(2) for b in range(2)}
-        opp_tile = {(b, c): held([P, PACK, CHUNK], F32, f"opp{b}{c}") for b in range(2) for c in range(chunks) if (b, c) != (1, 2)}
+        opp_tile = {(b, c): held([P, PACK, CHUNK], F32, f"opp{b}{c}") for b in range(2) for c in range(chunks) if (b, c) not in ((0, 1), (1, 2))}
         opp_strip = [held([P, PACK, STRIP], F32, f"opp_strip{u}") for u in range(2)]
+        early_strip = [held([P, PACK, STRIP], F32, f"early_strip{u}") for u in range(2)]
         opp_sb = {key: tile[:] for key, tile in opp_tile.items()}
         state = [keep.tile([P, T], F32, name=f"state{n}") for n in range(n_tiles)]
         w2_w = [held([P, 2, N], U8, f"w2_w{pair}") for pair in range(2)]
@@ -86,6 +87,10 @@ def tile_list_zoning_accessibility_step_kernel(
             rows = opp[span(PASS, PASS), span(2 * CHUNK + u * STRIP, STRIP)]
             nc.sync.dma_start(opp_strip[u][:], rows.rearrange("(p i) j -> p i j", i=PACK))
 
+        def load_early_strip(u):
+            rows = opp[span(0, PASS), span(CHUNK + u * STRIP, STRIP)]
+            nc.sync.dma_start(early_strip[u][:], rows.rearrange("(p i) j -> p i j", i=PACK))
+
         def load_w2(pair):
             words = w2_words[:, :, span(pair * N, N)].rearrange("a p c -> p a c")
             nc.sync.dma_start(w2_w[pair][:].bitcast(I32), words.bitcast(I32))
@@ -109,14 +114,15 @@ def tile_list_zoning_accessibility_step_kernel(
         load_opp(0, 0)
         load_state(0)
         load_opp(1, 0)
+        load_state(1)
+        load_early_strip(0)
         for r in range(4):
             nc.sync.dma_start(
                 w2_s[r:P:32, :, :].bitcast(I32),
                 w2_scales[:, r:16:4, :].rearrange("a q n -> q a n").bitcast(I32),
             )
         load_w2(0)
-        load_state(1)
-        load_opp(0, 1)
+        load_early_strip(1)
         load_w2(1)
         load_opp(1, 1)
         load_state(2)
@@ -228,11 +234,11 @@ def tile_list_zoning_accessibility_step_kernel(
                 ALU.mult,
             )
 
-        def make_z(b, c, first=0, count=CHUNK, source=None):
+        def make_z(b, c, first=0, count=CHUNK, source=None, weights=None):
             nc.gpsimd.tensor_tensor(
                 grouped_z[b, c][:, span(first * PACK, count * PACK)].rearrange("p (c e i) -> p c i e", e=RUN, i=PACK),
                 in_runs(decay[b, c])[:, span(first // RUN, count // RUN)] if source is None else source,
-                opp_sb[b, c][:, :, span(first, count)].rearrange("p i (c e) -> p c i e", e=RUN),
+                (opp_sb[b, c][:, :, span(first, count)] if weights is None else weights).rearrange("p i (c e) -> p c i e", e=RUN),
                 ALU.mult,
             )
 
@@ -361,7 +367,8 @@ def tile_list_zoning_accessibility_step_kernel(
         quantize_z(z_first, 0, 1)
         make_size(1, 1, (0, 1), now=False)
         z_middle = open_z("z_middle", 1, 2)
-        make_z(0, 1)
+        for u in range(2):
+            make_z(0, 1, u * STRIP, STRIP, weights=early_strip[u][:])
 
         first_gaps = held([P, 2, CHUNK], F32, "first_gaps")
         difference(first_gaps[:, 0, :], picked[0, 0][:, 0:CHUNK], 0)

@@ -52,9 +52,9 @@ def tile_list_zoning_accessibility_step_kernel(
         tab_w = [held([P, T], I32, f"tab_w{a}") for a in range(2)]
         tab_s = keep.tile([P, T], U8, name="tab_s")
         w1_raw = {(a, b): held([P, PACK, PASS], F32, f"w1_raw{a}{b}") for a in range(2) for b in range(2)}
-        opp_tile = {(b, c): held([P, PACK, CHUNK], F32, f"opp{b}{c}") for b in range(2) for c in range(chunks) if (b, c) not in ((0, 1), (1, 2))}
+        opp_tile = {(b, c): held([P, PACK, CHUNK], F32, f"opp{b}{c}") for b in range(2) for c in range(chunks) if (b, c) not in ((0, 0), (0, 1), (1, 2))}
         opp_strip = [held([P, PACK, STRIP], F32, f"opp_strip{u}") for u in range(2)]
-        early_strip = [held([P, PACK, STRIP], F32, f"early_strip{u}") for u in range(2)]
+        early_strip = [held([P, PACK, STRIP], F32, f"early_strip{u}") for u in range(4)]
         opp_sb = {key: tile[:] for key, tile in opp_tile.items()}
         state = [keep.tile([P, T], F32, name=f"state{n}") for n in range(n_tiles)]
         w2_w = [held([P, 2, N], U8, f"w2_w{pair}") for pair in range(2)]
@@ -88,7 +88,7 @@ def tile_list_zoning_accessibility_step_kernel(
             nc.sync.dma_start(opp_strip[u][:], rows.rearrange("(p i) j -> p i j", i=PACK))
 
         def load_early_strip(u):
-            rows = opp[span(0, PASS), span(CHUNK + u * STRIP, STRIP)]
+            rows = opp[span(0, PASS), span(u * STRIP, STRIP)]
             nc.sync.dma_start(early_strip[u][:], rows.rearrange("(p i) j -> p i j", i=PACK))
 
         def load_w2(pair):
@@ -105,24 +105,25 @@ def tile_list_zoning_accessibility_step_kernel(
                 tab_s[32 * q : 32 * q + 8, :].bitcast(I32),
                 tab_scales[:, 4 * q : 4 * q + 4, :].bitcast(I32),
             )
-        nc.sync.dma_start(plan_rows[0:n_tiles, :], plan.rearrange("(n p) -> n p", p=P))
         load_w1(0, 0)
         load_tab(1)
         load_w1(1, 0)
         load_w1(0, 1)
         load_w1(1, 1)
-        load_opp(0, 0)
-        load_state(0)
-        load_opp(1, 0)
-        load_state(1)
         load_early_strip(0)
+        load_state(0)
+        load_early_strip(1)
+        load_opp(1, 0)
+        nc.sync.dma_start(plan_rows[0:n_tiles, :], plan.rearrange("(n p) -> n p", p=P))
+        load_state(1)
+        load_early_strip(2)
         for r in range(4):
             nc.sync.dma_start(
                 w2_s[r:P:32, :, :].bitcast(I32),
                 w2_scales[:, r:16:4, :].rearrange("a q n -> q a n").bitcast(I32),
             )
         load_w2(0)
-        load_early_strip(1)
+        load_early_strip(3)
         load_w2(1)
         load_opp(1, 1)
         load_state(2)
@@ -359,7 +360,8 @@ def tile_list_zoning_accessibility_step_kernel(
         make_size(1, 0, (0, 1), later="now")
         make_decay(0, 1, "size10")
         z_first = open_z("z_first", 0, 1)
-        make_z(0, 0)
+        for u in range(2):
+            make_z(0, 0, u * STRIP, STRIP, weights=early_strip[u][:])
         pick(0, 0, chunks)
         for u in range(2):
             cols = span(u * STRIP, STRIP)
@@ -368,7 +370,7 @@ def tile_list_zoning_accessibility_step_kernel(
         make_size(1, 1, (0, 1), now=False)
         z_middle = open_z("z_middle", 1, 2)
         for u in range(2):
-            make_z(0, 1, u * STRIP, STRIP, weights=early_strip[u][:])
+            make_z(0, 1, u * STRIP, STRIP, weights=early_strip[2 + u][:])
 
         first_gaps = held([P, 2, CHUNK], F32, "first_gaps")
         difference(first_gaps[:, 0, :], picked[0, 0][:, 0:CHUNK], 0)

@@ -22,17 +22,26 @@ PACK = 4
 PASS = P * PACK
 CHUNK = 256
 STRIP = 128
-SHARE = 84
 RUN = 4
+VECTOR_SHARE = 84
 HALF_REST = (S - CHUNK) // 2
+CHUNKS = S // CHUNK
+ROW_TILES = N // P
+
+PLACED = {
+    "v_w1_640": 0, "w1_grouped11": 1024, "z_first": 1536, "z_middle": 1536,
+    "picked32": 1536, "new03": 4608, "z_last": 5632,
+    "moved00": 15360, "size02": 12288, "size12": 16384,
+    "moved10": 13824, "late_strip": 12288, "size13": 14336, "moved20": 14336,
+    "moved02": 24064, "size03": 20480, "gap01": 24576,
+    "picked30": 30208, "gap11": 27648, "gap21": 30720,
+}
 
 
 def tile_list_zoning_accessibility_step_kernel(
     tc, tab_words, tab_scales, offs, w1, opp, w2_words, w2_scales, gT, plan, out
 ):
     nc = tc.nc
-    n_tiles = N // P
-    chunks = S // CHUNK
 
     with ExitStack() as ctx:
         keep = ctx.enter_context(tc.tile_pool(name="keep", bufs=1))
@@ -42,24 +51,37 @@ def tile_list_zoning_accessibility_step_kernel(
         def held(shape, dtype, name, slot=None):
             return keep.tile(shape, dtype, name=name, tag=slot or name, align_bytes=64)
 
+        def spot(shape, name, slot=None, dtype=F32):
+            if name in PLACED:
+                return shared.tile(shape, dtype, name=name, offset=PLACED[name], align_bytes=64)
+            return held(shape, dtype, name, slot)
+
         def bank(shape, index, name):
             return psum.tile(shape, F32, name=name, tag=f"bank{index}")
 
         def span(first, count):
             return slice(first, first + count)
 
+        by_strips = ((0, 0), (0, 1), (1, 2))
         offsets = keep.tile([P, S // 16], U16, name="offsets")
         tab_w = [held([P, T], I32, f"tab_w{a}") for a in range(2)]
         tab_s = keep.tile([P, T], U8, name="tab_s")
         w1_raw = {(a, b): held([P, PACK, PASS], F32, f"w1_raw{a}{b}") for a in range(2) for b in range(2)}
-        opp_tile = {(b, c): held([P, PACK, CHUNK], F32, f"opp{b}{c}") for b in range(2) for c in range(chunks) if (b, c) not in ((0, 0), (0, 1), (1, 2))}
-        opp_strip = [held([P, PACK, STRIP], F32, f"opp_strip{u}") for u in range(2)]
-        early_strip = [held([P, PACK, STRIP], F32, f"early_strip{u}") for u in range(4)]
-        opp_sb = {key: tile[:] for key, tile in opp_tile.items()}
-        state = [keep.tile([P, T], F32, name=f"state{n}") for n in range(n_tiles)]
+        opp_chunk = {
+            (b, c): held([P, PACK, CHUNK], F32, f"opp{b}{c}")
+            for b in range(2)
+            for c in range(CHUNKS)
+            if (b, c) not in by_strips
+        }
+        opp_strip = {
+            (b, c, u): held([P, PACK, STRIP], F32, f"opp{b}{c}{u}")
+            for b, c in (by_strips[2], by_strips[0], by_strips[1])
+            for u in range(2)
+        }
+        state = [keep.tile([P, T], F32, name=f"state{n}") for n in range(ROW_TILES)]
         w2_w = [held([P, 2, N], U8, f"w2_w{pair}") for pair in range(2)]
         w2_s = held([P, 2, N], U8, "w2_s")
-        plan_sb = keep.tile([P, n_tiles], F32, name="plan_sb")
+        plan_sb = keep.tile([P, ROW_TILES], F32, name="plan_sb")
 
         def entries(first, count):
             return offsets[:, first // 16 : (first + count) // 16]
@@ -81,15 +103,11 @@ def tile_list_zoning_accessibility_step_kernel(
 
         def load_opp(b, c):
             rows = opp[span(b * PASS, PASS), span(c * CHUNK, CHUNK)]
-            nc.sync.dma_start(opp_tile[b, c][:], rows.rearrange("(p i) j -> p i j", i=PACK))
+            nc.sync.dma_start(opp_chunk[b, c][:], rows.rearrange("(p i) j -> p i j", i=PACK))
 
-        def load_opp_strip(u):
-            rows = opp[span(PASS, PASS), span(2 * CHUNK + u * STRIP, STRIP)]
-            nc.sync.dma_start(opp_strip[u][:], rows.rearrange("(p i) j -> p i j", i=PACK))
-
-        def load_early_strip(u):
-            rows = opp[span(0, PASS), span(u * STRIP, STRIP)]
-            nc.sync.dma_start(early_strip[u][:], rows.rearrange("(p i) j -> p i j", i=PACK))
+        def load_opp_strip(b, c, u):
+            rows = opp[span(b * PASS, PASS), span(c * CHUNK + u * STRIP, STRIP)]
+            nc.sync.dma_start(opp_strip[b, c, u][:], rows.rearrange("(p i) j -> p i j", i=PACK))
 
         def load_w2(pair):
             words = w2_words[:, :, span(pair * N, N)].rearrange("a p c -> p a c")
@@ -110,45 +128,33 @@ def tile_list_zoning_accessibility_step_kernel(
         load_w1(1, 0)
         load_w1(0, 1)
         load_w1(1, 1)
-        load_early_strip(0)
+        load_opp_strip(0, 0, 0)
         load_state(0)
-        load_early_strip(1)
+        load_opp_strip(0, 0, 1)
         load_opp(1, 0)
-        nc.sync.dma_start(plan_rows[0:n_tiles, :], plan.rearrange("(n p) -> n p", p=P))
+        nc.sync.dma_start(plan_rows[0:ROW_TILES, :], plan.rearrange("(n p) -> n p", p=P))
         load_state(1)
-        load_early_strip(2)
+        load_opp_strip(0, 1, 0)
         for r in range(4):
             nc.sync.dma_start(
                 w2_s[r:P:32, :, :].bitcast(I32),
                 w2_scales[:, r:16:4, :].rearrange("a q n -> q a n").bitcast(I32),
             )
         load_w2(0)
-        load_early_strip(3)
+        load_opp_strip(0, 1, 1)
         load_w2(1)
         load_opp(1, 1)
         load_state(2)
         load_opp(0, 2)
-        load_opp_strip(0)
+        load_opp_strip(1, 2, 0)
         load_state(3)
-        load_opp_strip(1)
+        load_opp_strip(1, 2, 1)
         load_opp(0, 3)
         load_opp(1, 3)
 
-        placed = {"v_w1_640": 0, "w1_grouped11": 1024, "z_first": 1536, "z_middle": 1536, "picked31": 1536}
-        placed.update({"new03": 4608, "z_last": 5632})
-        placed.update({"size02": 12288, "moved00": 15360, "size12": 16384})
-        placed.update({"late_strip": 12288, "moved10": 13824, "size13": 14336, "moved20": 14336})
-        placed.update({"size03": 20480, "moved02": 24064, "gap01": 24576})
-        placed.update({"gap11": 27648, "picked30": 30208, "gap21": 30720})
-
-        def spot(shape, name, slot=None, dtype=F32):
-            if name in placed:
-                return shared.tile(shape, dtype, name=name, offset=placed[name], align_bytes=64)
-            return held(shape, dtype, name, slot)
-
         plan_turned = bank([P, P], 7, "plan_turned")
         nc.tensor.transpose(plan_turned[:], plan_rows[:], identity[:])
-        nc.scalar.copy(plan_sb[:], plan_turned[:, 0:n_tiles])
+        nc.scalar.copy(plan_sb[:], plan_turned[:, 0:ROW_TILES])
 
         v_s = held([P, S], U8, "v_s")
         v_w = {}
@@ -173,50 +179,56 @@ def tile_list_zoning_accessibility_step_kernel(
             w1_s[a, b] = held([P, PASS], U8, f"w1_s{a}{b}")
             nc.vector.quantize_mx(out=w1_w[a, b][:].bitcast(FP8X4), scales=w1_s[a, b][:], in_=grouped[:])
 
+        def separation(b, c, u, index):
+            sep = bank([P, PACK, STRIP], index, "sep")
+            for a in range(2):
+                for i in range(PACK):
+                    m = span(i * P, P)
+                    nc.tensor.matmul_mx(
+                        out=sep[:, i, :],
+                        lhsT=w1_w[a, b][:, m].bitcast(FP8X4),
+                        lhsT_scale=w1_s[a, b][:, m],
+                        rhs=v_w[a, 2 * c + u].bitcast(FP8X4),
+                        rhs_scale=v_s[4 * a : P, span(c * CHUNK + u * STRIP, STRIP)],
+                        start=a + i == 0,
+                        stop=a + i == PACK,
+                    )
+            return sep
+
         decay = {}
 
         def in_runs(tile):
             return tile[:].rearrange("p i c -> p (i c)").rearrange("p (c i e) -> p c i e", i=PACK, e=RUN)
 
-        def second_strip(tile):
+        def strip_in_runs(tile, u):
+            return in_runs(tile)[:, span(u * STRIP // RUN, STRIP // RUN)]
+
+        def second_strip_in_planes(tile):
             return tile[:].rearrange("p i c -> p (i c)").rearrange("p (u i c) -> p u i c", u=2, i=PACK)[:, 1]
 
-        def make_size(b, c, banks, slot=None, later=None, now=True):
-            size = decay[b, c] = spot([P, PACK, CHUNK], f"size{b}{c}", slot)
-            if (b, c) == (1, 0):
-                decay[b, c] = held([P, PACK, CHUNK], F32, "decay10")
+        def make_size(b, c, banks, last_for_vector=False):
+            size = decay[b, c] = spot([P, PACK, CHUNK], f"size{b}{c}")
             for u in range(2):
-                cols = span(c * CHUNK + u * STRIP, STRIP)
-                sep = bank([P, PACK, STRIP], banks[u], "sep")
-                for a in range(2):
-                    for i in range(PACK):
-                        m = span(i * P, P)
-                        nc.tensor.matmul_mx(
-                            out=sep[:, i, :],
-                            lhsT=w1_w[a, b][:, m].bitcast(FP8X4),
-                            lhsT_scale=w1_s[a, b][:, m],
-                            rhs=v_w[a, 2 * c + u].bitcast(FP8X4),
-                            rhs_scale=v_s[4 * a : P, cols],
-                            start=a + i == 0,
-                            stop=a + i == PACK,
-                        )
-                if (b, c) == (1, 0):
-                    strip = span(u * STRIP, STRIP)
-                    nc.scalar.activation(size[:, :, strip], sep[:], ACT.Abs)
-                    nc.scalar.activation(decay[b, c][:, :, strip], size[:, :, strip], ACT.Exp, scale=-1.0)
-                elif (b, c, u) == (1, 2, 1):
-                    nc.scalar.activation(second_strip(size), sep[:], ACT.Abs)
+                sep = separation(b, c, u, banks[u])
+                if last_for_vector and u == 1:
+                    nc.scalar.activation(second_strip_in_planes(size), sep[:], ACT.Abs)
                 else:
-                    strip = in_runs(size)[:, span(u * STRIP // RUN, STRIP // RUN)]
-                    nc.scalar.activation(strip, sep[:].rearrange("p i (c e) -> p c i e", e=RUN), ACT.Abs)
-            if now and (b, c) != (1, 0):
-                make_decay(b, c)
+                    nc.scalar.activation(strip_in_runs(size, u), sep[:].rearrange("p i (c e) -> p c i e", e=RUN), ACT.Abs)
 
         def make_decay(b, c, slot=None):
             size = decay[b, c]
             if slot is not None:
                 decay[b, c] = held([P, PACK, CHUNK], F32, f"decay{b}{c}", slot)
             nc.scalar.activation(decay[b, c][:], size[:], ACT.Exp, scale=-1.0)
+
+        def make_decay_by_strips(b, c, banks):
+            size = held([P, PACK, CHUNK], F32, f"size{b}{c}")
+            decay[b, c] = held([P, PACK, CHUNK], F32, f"decay{b}{c}")
+            for u in range(2):
+                sep = separation(b, c, u, banks[u])
+                strip = span(u * STRIP, STRIP)
+                nc.scalar.activation(size[:, :, strip], sep[:], ACT.Abs)
+                nc.scalar.activation(decay[b, c][:, :, strip], size[:, :, strip], ACT.Exp, scale=-1.0)
 
         grouped_z, codes, scales = {}, {}, {}
 
@@ -227,34 +239,39 @@ def tile_list_zoning_accessibility_step_kernel(
                     grouped_z[b, first + k] = tile[:, b, span(k * CHUNK * PACK, CHUNK * PACK)]
             return tile
 
-        def make_z_on_vector(b, c, first, count, factors):
+        def z_on_vector(b, c, u, discount, weights):
             nc.vector.tensor_tensor(
-                grouped_z[b, c][:, span(first * PACK, count * PACK)].rearrange("p (c e i) -> p c i e", e=2, i=PACK),
-                factors[0].rearrange("p i (c e) -> p c i e", e=2),
-                factors[1].rearrange("p i (c e) -> p c i e", e=2),
+                grouped_z[b, c][:, span(u * PASS, PASS)].rearrange("p (c e i) -> p c i e", e=2, i=PACK),
+                discount.rearrange("p i (c e) -> p c i e", e=2),
+                weights.rearrange("p i (c e) -> p c i e", e=2),
                 ALU.mult,
             )
 
-        def make_z(b, c, first=0, count=CHUNK, source=None, weights=None):
+        def z_on_gpsimd(into, discount, weights):
             nc.gpsimd.tensor_tensor(
-                grouped_z[b, c][:, span(first * PACK, count * PACK)].rearrange("p (c e i) -> p c i e", e=RUN, i=PACK),
-                in_runs(decay[b, c])[:, span(first // RUN, count // RUN)] if source is None else source,
-                (opp_sb[b, c][:, :, span(first, count)] if weights is None else weights).rearrange("p i (c e) -> p c i e", e=RUN),
+                into.rearrange("p (c e i) -> p c i e", e=RUN, i=PACK),
+                discount,
+                weights.rearrange("p i (c e) -> p c i e", e=RUN),
                 ALU.mult,
             )
 
-        def quantize_z(tile, first, count, slot=None):
-            words = spot([P, 2, count * CHUNK], f"z_w{first}", slot, U32)
-            bytes_of_scale = held([P, 2, count * CHUNK], U8, f"z_s{first}")
+        def z_chunk(b, c):
+            z_on_gpsimd(grouped_z[b, c], in_runs(decay[b, c]), opp_chunk[b, c][:])
+
+        def z_strip(b, c, u):
+            z_on_gpsimd(grouped_z[b, c][:, span(u * PASS, PASS)], strip_in_runs(decay[b, c], u), opp_strip[b, c, u][:])
+
+        def quantize_z(tile, first, count):
+            codes[first] = held([P, 2, count * CHUNK], U32, f"z_w{first}")
+            scales[first] = held([P, 2, count * CHUNK], U8, f"z_s{first}")
             nc.vector.quantize_mx(
-                out=words[:].rearrange("p b j -> p (b j)").bitcast(FP8X4),
-                scales=bytes_of_scale[:].rearrange("p b j -> p (b j)"),
+                out=codes[first][:].rearrange("p b j -> p (b j)").bitcast(FP8X4),
+                scales=scales[first][:].rearrange("p b j -> p (b j)"),
                 in_=tile[:].rearrange("p b x -> p (b x)"),
             )
-            codes[first], scales[first] = words, bytes_of_scale
 
         def second_pass(into, n, b, first, count, start, stop):
-            c = {0: 0, 1: 1, 2: 1, 3: 3}[first // CHUNK]
+            c = max(opened for opened in codes if opened <= first // CHUNK)
             cols = span(first - c * CHUNK, count)
             nc.tensor.matmul_mx(
                 out=into,
@@ -268,16 +285,19 @@ def tile_list_zoning_accessibility_step_kernel(
 
         picked, gap, new = {}, {}, {}
 
-        def pick(n, c, count, slot=None):
-            picked[n, c] = spot([P, count * CHUNK], f"picked{n}{c}", slot)
+        def pick(n, c, count):
+            picked[n, c] = spot([P, count * CHUNK], f"picked{n}{c}")
             nc.vector.tensor_copy(picked[n, c][:], state[n][:].indirect(entries(c * CHUNK, count * CHUNK)))
 
         def pick_half(n, k, slot=None):
-            picked[n, k] = spot([P, HALF_REST], f"picked{n}{k}", slot)
+            picked[n, k] = held([P, HALF_REST], F32, f"picked{n}{k}", slot)
             nc.vector.tensor_copy(picked[n, k][:], state[n][:].indirect(entries(CHUNK + (k - 1) * HALF_REST, HALF_REST)))
 
         def difference(into, values, n):
             nc.scalar.activation(into, values, ACT.Identity, bias=plan_sb[:, n : n + 1], scale=-1.0)
+
+        def add_plan(into, moved, n):
+            nc.scalar.activation(into, moved, ACT.Identity, bias=plan_sb[:, n : n + 1])
 
         def make_gap(n, c, count, source, slot=None):
             tile = spot([P, count * CHUNK], f"gap{n}{c}", slot)
@@ -285,14 +305,11 @@ def tile_list_zoning_accessibility_step_kernel(
             for k in range(count):
                 gap[n, c + k] = (tile, k)
 
-        def add_plan(into, moved, n):
-            nc.scalar.activation(into, moved, ACT.Identity, bias=plan_sb[:, n : n + 1])
-
-        def make_wide_gap(n, slot=None):
-            tile = spot([P, 3 * CHUNK], f"gap{n}1", slot)
+        def make_gap_of_halves(n):
+            tile = spot([P, 2 * HALF_REST], f"gap{n}1")
             difference(tile[:, 0:HALF_REST], picked[n, 1][:], n)
             difference(tile[:, HALF_REST:], picked[n, 2][:], n)
-            for k in range(3):
+            for k in range(CHUNKS - 1):
                 gap[n, 1 + k] = (tile, k)
 
         def first_product(tiles, index, gaps, slot=None):
@@ -312,8 +329,8 @@ def tile_list_zoning_accessibility_step_kernel(
                 new[0, n] = sums[:, k, :]
                 add_plan(sums[:, k, :], moved[:, k, :], n)
 
-        def first_update(tiles, index, gaps):
-            first_sums(tiles, first_product(tiles, index, gaps))
+        def first_gap(n):
+            return gap[n, 0][0][:].rearrange("p (k j) -> p k j", k=1)
 
         def open_update(c, n, count, index, slot=None):
             first, width = c * CHUNK, count * CHUNK
@@ -351,93 +368,98 @@ def tile_list_zoning_accessibility_step_kernel(
         pick_words(1, 0, CHUNK)
         prepare_w1(0, 0, 0)
         pick_words(1, CHUNK, HALF_REST, "w1_grouped00")
-        prepare_w1(1, 0, SHARE)
+        prepare_w1(1, 0, VECTOR_SHARE)
         make_size(0, 0, (0, 1))
+        make_decay(0, 0)
         prepare_w1(0, 1, P)
-        make_size(0, 1, (2, 3), now=False)
+        make_size(0, 1, (2, 3))
         prepare_w1(1, 1, P)
         pick_words(1, CHUNK + HALF_REST, HALF_REST)
-        make_size(1, 0, (0, 1), later="now")
+        make_decay_by_strips(1, 0, (0, 1))
         make_decay(0, 1, "size10")
         z_first = open_z("z_first", 0, 1)
         for u in range(2):
-            make_z(0, 0, u * STRIP, STRIP, weights=early_strip[u][:])
-        pick(0, 0, chunks)
+            z_strip(0, 0, u)
+        pick(0, 0, CHUNKS)
         for u in range(2):
             cols = span(u * STRIP, STRIP)
-            make_z_on_vector(1, 0, u * STRIP, STRIP, (decay[1, 0][:, :, cols], opp_sb[1, 0][:, :, cols]))
+            z_on_vector(1, 0, u, decay[1, 0][:, :, cols], opp_chunk[1, 0][:, :, cols])
         quantize_z(z_first, 0, 1)
-        make_size(1, 1, (0, 1), now=False)
+        make_size(1, 1, (0, 1))
         z_middle = open_z("z_middle", 1, 2)
         for u in range(2):
-            make_z(0, 1, u * STRIP, STRIP, weights=early_strip[2 + u][:])
+            z_strip(0, 1, u)
 
         first_gaps = held([P, 2, CHUNK], F32, "first_gaps")
         difference(first_gaps[:, 0, :], picked[0, 0][:, 0:CHUNK], 0)
         pick(1, 0, 1)
         difference(first_gaps[:, 1, :], picked[1, 0][:], 1)
         make_decay(1, 1, "picked10")
-        make_z(1, 1)
+        z_chunk(1, 1)
         pick_half(1, 2)
-        first_update((0, 1), 4, first_gaps[:])
+        first_sums((0, 1), first_product((0, 1), 4, first_gaps[:]))
         pick_half(1, 1, "first_gaps")
         put(0, 0)
         put(0, 1)
         make_size(0, 2, (0, 1))
-        make_z(0, 2)
-        make_size(1, 2, (0, 1), now=False)
+        make_decay(0, 2)
+        z_chunk(0, 2)
+        make_size(1, 2, (0, 1))
 
         pick(2, 0, 1)
         make_gap(2, 0, 1, 0)
         make_decay(1, 2, "picked20")
-        opp_sb[1, 2] = opp_strip[0][:]
-        make_z(1, 2, 0, STRIP)
+        for u in range(2):
+            z_strip(1, 2, u)
         pick_half(2, 2)
-        first_update((2,), 5, gap[2, 0][0][:].rearrange("p (k j) -> p k j", k=1))
+        first_sums((2,), first_product((2,), 5, first_gap(2)))
         pick_half(2, 1, "gap20")
         put(0, 2)
-        make_size(0, 3, (0, 1), now=False)
-        strips = [in_runs(decay[0, 3])[:, span(u * STRIP // RUN, STRIP // RUN)] for u in range(2)]
-        nc.scalar.activation(strips[0], strips[0], ACT.Exp, scale=-1.0)
+        make_size(0, 3, (0, 1))
+        early, late = (strip_in_runs(decay[0, 3], u) for u in range(2))
+        nc.scalar.activation(early, early, ACT.Exp, scale=-1.0)
         make_gap(0, 1, 3, 0)
 
         pick(3, 0, 1)
         make_gap(3, 0, 1, 0)
-        make_z_on_vector(1, 2, STRIP, STRIP, (second_strip(decay[1, 2]), opp_strip[1][:]))
-        last_first = first_product((3,), 7, gap[3, 0][0][:].rearrange("p (k j) -> p k j", k=1), "picked20")
+        pick(3, 1, 1)
+        last_first = first_product((3,), 7, first_gap(3), "picked20")
         quantize_z(z_middle, 1, 2)
-        pick(3, 1, 3)
+        pick(3, 2, 2)
         first_sums((3,), last_first)
         put(0, 3)
-        make_wide_gap(1)
-        make_wide_gap(2)
+        make_gap_of_halves(1)
+        make_gap_of_halves(2)
         z_last = open_z("z_last", 3, 1)
-        make_z(0, 3, 0, STRIP)
+        z_on_gpsimd(grouped_z[0, 3][:, 0:PASS], early, opp_chunk[0, 3][:, :, 0:STRIP])
 
         open_update(1, 0, 1, 4, "tab_w0")
         open_update(1, 1, 2, 6)
         open_update(1, 2, 2, 5, "w1_raw01")
         close_update(1, 0, "w1_raw00")
         put(1, 0)
-        make_size(1, 3, (0, 1), now=False)
+        make_size(1, 3, (0, 1))
         close_update(1, 1)
         put(1, 1)
         late_strip = spot([P, STRIP // RUN, PACK, RUN], "late_strip")
-        nc.scalar.activation(late_strip[:], strips[1], ACT.Exp, scale=-1.0)
-        last_size = decay[1, 3]
-        decay[1, 3] = held([P, PACK, CHUNK], F32, "decay13", "w1_raw10")
-        nc.scalar.activation(decay[1, 3][:], last_size[:], ACT.Exp, scale=-1.0)
+        nc.scalar.activation(late_strip[:], late, ACT.Exp, scale=-1.0)
+        make_decay(1, 3, "w1_raw10")
         close_update(1, 2)
         put(1, 2)
-        make_z(0, 3, STRIP, STRIP, late_strip[:])
-        make_gap(3, 1, 3, 1, "w1_raw00")
+        z_on_gpsimd(grouped_z[0, 3][:, PASS:], late_strip[:], opp_chunk[0, 3][:, :, STRIP:])
+        last_gaps = held([P, 3 * CHUNK], F32, "gap31", "w1_raw00")
+        difference(last_gaps[:, 0:CHUNK], picked[3, 1][:], 3)
+        difference(last_gaps[:, CHUNK:], picked[3, 2][:], 3)
+        for k in range(CHUNKS - 1):
+            gap[3, 1 + k] = (last_gaps, k)
         update(1, 3, 1, 7, "tab_w0")
-        make_z(1, 3)
+        z_chunk(1, 3)
         quantize_z(z_last, 3, 1)
+
         put(1, 3)
         update(2, 0, 1, 4)
         put(2, 0)
-        for n in range(3):
+        for n in range(ROW_TILES - 1):
             update(3, n, 1, n, "tab_w1" if n == 0 else None)
             put(3, n)
             store(n)

@@ -29,7 +29,7 @@ CHUNKS = S // CHUNK
 ROW_TILES = N // P
 
 PLACED = {
-    "v_w1_640": 0, "w1_grouped11": 1024, "z_first": 1536, "z_middle": 1536,
+    "w1_grouped11": 1024, "z_first": 1536, "z_middle": 1536,
     "picked32": 1536, "new03": 4608, "z_last": 5632,
     "moved00": 15360, "size02": 12288, "size12": 16384,
     "moved10": 13824, "late_strip": 12288, "size13": 14336, "moved20": 14336,
@@ -247,8 +247,8 @@ def tile_list_zoning_accessibility_step_kernel(
                 ALU.mult,
             )
 
-        def z_on_gpsimd(into, discount, weights):
-            nc.gpsimd.tensor_tensor(
+        def z_in_runs(engine, into, discount, weights):
+            engine.tensor_tensor(
                 into.rearrange("p (c e i) -> p c i e", e=RUN, i=PACK),
                 discount,
                 weights.rearrange("p i (c e) -> p c i e", e=RUN),
@@ -256,10 +256,11 @@ def tile_list_zoning_accessibility_step_kernel(
             )
 
         def z_chunk(b, c):
-            z_on_gpsimd(grouped_z[b, c], in_runs(decay[b, c]), opp_chunk[b, c][:])
+            z_in_runs(nc.gpsimd, grouped_z[b, c], in_runs(decay[b, c]), opp_chunk[b, c][:])
 
-        def z_strip(b, c, u):
-            z_on_gpsimd(grouped_z[b, c][:, span(u * PASS, PASS)], strip_in_runs(decay[b, c], u), opp_strip[b, c, u][:])
+        def z_strip(b, c, u, engine=nc.gpsimd):
+            into = grouped_z[b, c][:, span(u * PASS, PASS)]
+            z_in_runs(engine, into, strip_in_runs(decay[b, c], u), opp_strip[b, c, u][:])
 
         def quantize_z(tile, first, count):
             codes[first] = held([P, 2, count * CHUNK], U32, f"z_w{first}")
@@ -367,19 +368,18 @@ def tile_list_zoning_accessibility_step_kernel(
         nc.vector.tensor_copy(v_s[:], tab_s[:].indirect(offsets[:]))
         pick_words(1, 0, CHUNK)
         prepare_w1(0, 0, 0)
-        pick_words(1, CHUNK, HALF_REST, "w1_grouped00")
+        pick_words(1, CHUNK, S - CHUNK, "w1_grouped00")
         prepare_w1(1, 0, VECTOR_SHARE)
         make_size(0, 0, (0, 1))
         make_decay(0, 0)
         prepare_w1(0, 1, P)
         make_size(0, 1, (2, 3))
         prepare_w1(1, 1, P)
-        pick_words(1, CHUNK + HALF_REST, HALF_REST)
         make_decay_by_strips(1, 0, (0, 1))
         make_decay(0, 1, "size10")
         z_first = open_z("z_first", 0, 1)
-        for u in range(2):
-            z_strip(0, 0, u)
+        z_strip(0, 0, 0, nc.vector)
+        z_strip(0, 0, 1)
         pick(0, 0, CHUNKS)
         for u in range(2):
             cols = span(u * STRIP, STRIP)
@@ -431,7 +431,7 @@ def tile_list_zoning_accessibility_step_kernel(
         make_gap_of_halves(1)
         make_gap_of_halves(2)
         z_last = open_z("z_last", 3, 1)
-        z_on_gpsimd(grouped_z[0, 3][:, 0:PASS], early, opp_chunk[0, 3][:, :, 0:STRIP])
+        z_in_runs(nc.gpsimd, grouped_z[0, 3][:, 0:PASS], early, opp_chunk[0, 3][:, :, 0:STRIP])
 
         open_update(1, 0, 1, 4, "tab_w0")
         open_update(1, 1, 2, 6)
@@ -446,7 +446,7 @@ def tile_list_zoning_accessibility_step_kernel(
         make_decay(1, 3, "w1_raw10")
         close_update(1, 2)
         put(1, 2)
-        z_on_gpsimd(grouped_z[0, 3][:, PASS:], late_strip[:], opp_chunk[0, 3][:, :, STRIP:])
+        z_in_runs(nc.gpsimd, grouped_z[0, 3][:, PASS:], late_strip[:], opp_chunk[0, 3][:, :, STRIP:])
         last_gaps = held([P, 3 * CHUNK], F32, "gap31", "w1_raw00")
         difference(last_gaps[:, 0:CHUNK], picked[3, 1][:], 3)
         difference(last_gaps[:, CHUNK:], picked[3, 2][:], 3)

@@ -119,7 +119,8 @@ def tile_list_zoning_accessibility_step_kernel(
         load_tab(0)
         nc.sync.dma_start(offsets[:], offs)
         for q in range(4):
-            nc.sync.dma_start(
+            queue = nc.sync if q < 2 else nc.scalar
+            queue.dma_start(
                 tab_s[32 * q : 32 * q + 8, :].bitcast(I32),
                 tab_scales[:, 4 * q : 4 * q + 4, :].bitcast(I32),
             )

@@ -24,17 +24,20 @@ CHUNK = 256
 STRIP = 128
 RUN = 4
 VECTOR_SHARE = 84
+EARLY = 192
 HALF_REST = (S - CHUNK) // 2
 CHUNKS = S // CHUNK
 ROW_TILES = N // P
 
 PLACED = {
     "w1_grouped11": 1024, "z_first": 1536, "z_middle": 1536,
-    "picked32": 1536, "new03": 4608, "z_last": 5632,
-    "moved00": 15360, "size02": 12288, "size12": 16384,
-    "moved10": 13824, "late_strip": 12288, "size13": 14336, "moved20": 14336,
+    "gap21": 2048, "new03": 5120, "z_last": 6144,
+    "moved11": 10240, "late_strip": 10240,
+    "moved00": 15872, "size02": 12288, "size12": 16384,
+    "moved10": 13824, "size13": 14336, "moved13": 14336,
     "moved02": 24064, "size03": 20480, "gap01": 24576,
-    "picked30": 30208, "gap11": 27648, "gap21": 30720,
+    "picked30": 30208, "gap11": 27648,
+    "picked20": 31744, "new01": 31232, "decay12": 32256,
 }
 
 
@@ -218,8 +221,8 @@ def tile_list_zoning_accessibility_step_kernel(
 
         def make_decay(b, c, slot=None):
             size = decay[b, c]
-            if slot is not None:
-                decay[b, c] = held([P, PACK, CHUNK], F32, f"decay{b}{c}", slot)
+            if slot is not None or f"decay{b}{c}" in PLACED:
+                decay[b, c] = spot([P, PACK, CHUNK], f"decay{b}{c}", slot)
             nc.scalar.activation(decay[b, c][:], size[:], ACT.Exp, scale=-1.0)
 
         def make_decay_by_strips(b, c, banks):
@@ -287,8 +290,8 @@ def tile_list_zoning_accessibility_step_kernel(
 
         picked, gap, new = {}, {}, {}
 
-        def pick(n, c, count):
-            picked[n, c] = spot([P, count * CHUNK], f"picked{n}{c}")
+        def pick(n, c, count, slot=None):
+            picked[n, c] = spot([P, count * CHUNK], f"picked{n}{c}", slot)
             nc.vector.tensor_copy(picked[n, c][:], state[n][:].indirect(entries(c * CHUNK, count * CHUNK)))
 
         def pick_half(n, k, slot=None):
@@ -314,27 +317,26 @@ def tile_list_zoning_accessibility_step_kernel(
             for k in range(CHUNKS - 1):
                 gap[n, 1 + k] = (tile, k)
 
-        def first_product(tiles, index, gaps, slot=None):
+        def first_steps(tiles, index):
             step = bank([P, len(tiles), CHUNK], index, "step")
             for k, n in enumerate(tiles):
                 for u in range(2):
                     for b in range(2):
                         into = step[:, k, span(u * STRIP, STRIP)]
                         second_pass(into, n, b, u * STRIP, STRIP, k + u + b == 0, k + u + b == len(tiles) + 1)
-            moved = spot([P, len(tiles), CHUNK], f"moved0{tiles[0]}", slot)
-            nc.vector.scalar_tensor_tensor(moved[:], step[:], -1.0, gaps, ALU.add, ALU.mult)
-            return moved
+            return step
 
-        def first_sums(tiles, moved):
-            sums = spot([P, len(tiles), CHUNK], f"new0{tiles[0]}")
-            for k, n in enumerate(tiles):
-                new[0, n] = sums[:, k, :]
-                add_plan(sums[:, k, :], moved[:, k, :], n)
+        def product_on_vector(c, n, step, slot=None):
+            tile, k = gap[n, c]
+            moved = spot([P, CHUNK], f"moved{c}{n}", slot)
+            nc.vector.scalar_tensor_tensor(moved[:], step, -1.0, tile[:, span(k * CHUNK, CHUNK)], ALU.add, ALU.mult)
+            return moved[:]
 
-        def first_gap(n):
-            return gap[n, 0][0][:].rearrange("p (k j) -> p k j", k=1)
+        def sum_apart(c, n, moved, slot=None):
+            new[c, n] = spot([P, CHUNK], f"new{c}{n}", slot)[:]
+            add_plan(new[c, n], moved, n)
 
-        def open_update(c, n, count, index, slot=None):
+        def later_step(c, n, count, index):
             first, width = c * CHUNK, count * CHUNK
             step = bank([P, width], index, "step")
             run = PASS if (c, count) == (1, 2) else STRIP
@@ -342,17 +344,22 @@ def tile_list_zoning_accessibility_step_kernel(
                 for b in range(2):
                     last = u == width // run - 1 and b == 1
                     second_pass(step[:, span(u * run, run)], n, b, first + u * run, run, u + b == 0, last)
-            moved = spot([P, width], f"moved{c}{n}", slot)
+            return step
+
+        def open_update(c, n, count, index, slot=None):
+            step = later_step(c, n, count, index)
+            moved = spot([P, count * CHUNK], f"moved{c}{n}", slot)
             nc.scalar.activation(moved[:], step[:], ACT.Copy, bias=-1.0)
             new[c, n] = moved[:]
 
-        def close_update(c, n, slot=None):
+        def multiply(c, n):
             moved = new[c, n]
             tile, k = gap[n, c]
             nc.gpsimd.tensor_tensor(moved, moved, tile[:, span(k * CHUNK, moved.shape[1])], ALU.mult)
-            if slot is not None:
-                new[c, n] = held(list(moved.shape), F32, f"new{c}{n}", slot)[:]
-            add_plan(new[c, n], moved, n)
+
+        def close_update(c, n):
+            multiply(c, n)
+            add_plan(new[c, n], new[c, n], n)
 
         def update(c, n, count, index, slot=None):
             open_update(c, n, count, index, slot)
@@ -391,17 +398,17 @@ def tile_list_zoning_accessibility_step_kernel(
         for u in range(2):
             z_strip(0, 1, u)
 
-        first_gaps = held([P, 2, CHUNK], F32, "first_gaps")
-        difference(first_gaps[:, 0, :], picked[0, 0][:, 0:CHUNK], 0)
+        make_gap(0, 0, 1, 0)
         pick(1, 0, 1)
-        difference(first_gaps[:, 1, :], picked[1, 0][:], 1)
+        make_gap(1, 0, 1, 0)
         make_decay(1, 1, "picked10")
         z_chunk(1, 1)
         pick_half(1, 2)
-        first_sums((0, 1), first_product((0, 1), 4, first_gaps[:]))
-        pick_half(1, 1, "first_gaps")
+        step = first_steps((0, 1), 4)
+        moved = [product_on_vector(0, 0, step[:, 0, :]), product_on_vector(0, 1, step[:, 1, :], "decay10")]
+        sum_apart(0, 0, moved[0])
+        pick_half(1, 1, "gap00")
         put(0, 0)
-        put(0, 1)
         make_size(0, 2, (0, 1))
         make_decay(0, 2)
         z_chunk(0, 2)
@@ -409,57 +416,70 @@ def tile_list_zoning_accessibility_step_kernel(
 
         pick(2, 0, 1)
         make_gap(2, 0, 1, 0)
-        make_decay(1, 2, "picked20")
+        pick(2, 1, CHUNKS - 1, "opp10")
+        moved.append(product_on_vector(0, 2, first_steps((2,), 5)[:, 0, :]))
+        sum_apart(0, 1, moved[1])
+        make_decay(1, 2)
         for u in range(2):
             z_strip(1, 2, u)
-        pick_half(2, 2)
-        first_sums((2,), first_product((2,), 5, first_gap(2)))
-        pick_half(2, 1, "gap20")
+        put(0, 1)
+        sum_apart(0, 2, moved[2])
         put(0, 2)
         make_size(0, 3, (0, 1))
-        early, late = (strip_in_runs(decay[0, 3], u) for u in range(2))
+        early, late = in_runs(decay[0, 3])[:, : EARLY // RUN], in_runs(decay[0, 3])[:, EARLY // RUN :]
         nc.scalar.activation(early, early, ACT.Exp, scale=-1.0)
         make_gap(0, 1, 3, 0)
 
         pick(3, 0, 1)
         make_gap(3, 0, 1, 0)
         pick(3, 1, 1)
-        last_first = first_product((3,), 7, first_gap(3), "picked20")
-        quantize_z(z_middle, 1, 2)
-        pick(3, 2, 2)
-        first_sums((3,), last_first)
-        put(0, 3)
+        moved.append(product_on_vector(0, 3, first_steps((3,), 7)[:, 0, :], "gap20"))
         make_gap_of_halves(1)
-        make_gap_of_halves(2)
+        quantize_z(z_middle, 1, 2)
+        pick(3, 2, 2, "opp121")
+        later_gaps = spot([P, 2 * HALF_REST], "gap21")
+        for k in range(CHUNKS - 1):
+            gap[2, 1 + k] = (later_gaps, k)
+        difference(later_gaps[:, 0:HALF_REST], picked[2, 1][:, 0:HALF_REST], 2)
+        sum_apart(0, 3, moved[3])
+        difference(later_gaps[:, HALF_REST:], picked[2, 1][:, HALF_REST:], 2)
+        second = product_on_vector(1, 0, later_step(1, 0, 1, 4)[:])
+        put(0, 3)
         z_last = open_z("z_last", 3, 1)
-        z_in_runs(nc.gpsimd, grouped_z[0, 3][:, 0:PASS], early, opp_chunk[0, 3][:, :, 0:STRIP])
+        z_in_runs(nc.gpsimd, grouped_z[0, 3][:, : EARLY * PACK], early, opp_chunk[0, 3][:, :, :EARLY])
 
-        open_update(1, 0, 1, 4, "tab_w0")
-        open_update(1, 1, 2, 6)
-        open_update(1, 2, 2, 5, "w1_raw01")
-        close_update(1, 0, "w1_raw00")
+        open_update(1, 1, 1, 6)
+        sum_apart(1, 0, second, "w1_raw00")
         put(1, 0)
-        make_size(1, 3, (0, 1))
-        close_update(1, 1)
+        open_update(2, 0, 1, 2, "gap00")
+        open_update(1, 2, 2, 5, "w1_raw01")
+        multiply(1, 1)
+        sum_apart(1, 1, new[1, 1])
         put(1, 1)
-        late_strip = spot([P, STRIP // RUN, PACK, RUN], "late_strip")
+        close_update(2, 0)
+        put(2, 0)
+        multiply(1, 2)
+        late_strip = spot([P, (CHUNK - EARLY) // RUN, PACK, RUN], "late_strip")
         nc.scalar.activation(late_strip[:], late, ACT.Exp, scale=-1.0)
+        z_in_runs(nc.gpsimd, grouped_z[0, 3][:, EARLY * PACK :], late_strip[:], opp_chunk[0, 3][:, :, EARLY:])
+        make_size(1, 3, (0, 1))
+        open_update(2, 1, 1, 3, "tab_w0")
+        multiply(2, 1)
         make_decay(1, 3, "w1_raw10")
-        close_update(1, 2)
+        add_plan(new[1, 2], new[1, 2], 2)
         put(1, 2)
-        z_in_runs(nc.gpsimd, grouped_z[0, 3][:, PASS:], late_strip[:], opp_chunk[0, 3][:, :, STRIP:])
+        z_chunk(1, 3)
+        quantize_z(z_last, 3, 1)
+
+        sum_apart(2, 1, new[2, 1], "opp13")
+        put(2, 1)
         last_gaps = held([P, 3 * CHUNK], F32, "gap31", "w1_raw00")
         difference(last_gaps[:, 0:CHUNK], picked[3, 1][:], 3)
         difference(last_gaps[:, CHUNK:], picked[3, 2][:], 3)
         for k in range(CHUNKS - 1):
             gap[3, 1 + k] = (last_gaps, k)
-        update(1, 3, 1, 7, "tab_w0")
-        z_chunk(1, 3)
-        quantize_z(z_last, 3, 1)
-
+        update(1, 3, 1, 7)
         put(1, 3)
-        update(2, 0, 1, 4)
-        put(2, 0)
         for n in range(ROW_TILES - 1):
             update(3, n, 1, n, "tab_w1" if n == 0 else None)
             put(3, n)

from contextlib import ExitStack

import concourse.mybir as mybir
from concourse.masks import make_identity

K, H, N, T, S = 1024, 1024, 512, 2048, 1024
FLOPS = 2 * K * H * S + 2 * H * N * S

F32 = mybir.dt.float32
BF16 = mybir.dt.bfloat16
I32 = mybir.dt.int32
U32 = mybir.dt.uint32
U16 = mybir.dt.uint16
U8 = mybir.dt.uint8
FP8X4 = mybir.dt.float8_e4m3fn_x4
FP4X4 = mybir.dt.float4_e2m1fn_x4
ACT = mybir.ActivationFunctionType
ALU = mybir.AluOpType

P = 128
PACK = 4
PASS = P * PACK
CHUNK = 256
STRIP = 128
RUN = 4
VECTOR_SHARE = 84
EARLY = 192
HALF_REST = (S - CHUNK) // 2
CHUNKS = S // CHUNK
ROW_TILES = N // P

PLACED = {
    "w1_grouped11": 1024, "z_first": 1536, "z_middle": 1536,
    "gap21": 2048, "new03": 5120, "z_last": 6144,
    "moved11": 10240, "late_strip": 10240,
    "moved00": 15872, "size02": 12288, "size12": 16384,
    "moved10": 13824, "size13": 14336, "moved13": 14336,
    "moved02": 24064, "size03": 20480, "gap01": 24576,
    "picked30": 30208, "gap11": 27648,
    "picked20": 31744, "new01": 31232, "decay12": 32256,
}


def tile_list_zoning_accessibility_step_kernel(
    tc, tab_words, tab_scales, offs, w1, opp, w2_words, w2_scales, gT, plan, out
):
    nc = tc.nc

    with ExitStack() as ctx:
        keep = ctx.enter_context(tc.tile_pool(name="keep", bufs=1))
        shared = ctx.enter_context(tc.tile_pool(name="shared", bufs=1))
        psum = ctx.enter_context(tc.psum_pool(name="psum", bufs=1))

        def held(shape, dtype, name, slot=None):
            return keep.tile(shape, dtype, name=name, tag=slot or name, align_bytes=64)

        def spot(shape, name, slot=None, dtype=F32):
            if name in PLACED:
                return shared.tile(shape, dtype, name=name, offset=PLACED[name], align_bytes=64)
            return held(shape, dtype, name, slot)

        def bank(shape, index, name):
            return psum.tile(shape, F32, name=name, tag=f"bank{index}")

        def span(first, count):
            return slice(first, first + count)

        by_strips = ((0, 0), (0, 1), (1, 2))
        offsets = keep.tile([P, S // 16], U16, name="offsets")
        tab_w = [held([P, T], I32, f"tab_w{a}") for a in range(2)]
        tab_s = keep.tile([P, T], U8, name="tab_s")
        w1_raw = {(a, b): held([P, PACK, PASS], F32, f"w1_raw{a}{b}") for a in range(2) for b in range(2)}
        opp_chunk = {
            (b, c): held([P, PACK, CHUNK], F32, f"opp{b}{c}")
            for b in range(2)
            for c in range(CHUNKS)
            if (b, c) not in by_strips
        }
        opp_strip = {
            (b, c, u): held([P, PACK, STRIP], F32, f"opp{b}{c}{u}")
            for b, c in (by_strips[2], by_strips[0], by_strips[1])
            for u in range(2)
        }
        state = [keep.tile([P, T], F32, name=f"state{n}") for n in range(ROW_TILES)]
        w2_w = [held([P, 2, N], U8, f"w2_w{pair}") for pair in range(2)]
        w2_s = held([P, 2, N], U8, "w2_s")
        plan_sb = keep.tile([P, ROW_TILES], F32, name="plan_sb")

        def entries(first, count):
            return offsets[:, first // 16 : (first + count) // 16]

        nc.vector.memset(tab_s[:].bitcast(I32), 0)
        nc.vector.memset(w2_s[:].bitcast(I32), 0)

        identity = keep.tile([P, P], F32, name="identity")
        make_identity(nc, identity[:])
        plan_rows = keep.tile([P, P], F32, name="plan_rows")
        nc.gpsimd.memset(plan_rows[:], 0.0)

        def load_tab(a):
            nc.sync.dma_start(tab_w[a][:], tab_words[a].rearrange("p t i -> p (t i)").bitcast(I32))

        def load_w1(a, b):
            rows = w1[span(a * PASS, PASS), span(b * PASS, PASS)]
            nc.sync.dma_start(w1_raw[a, b][:], rows.rearrange("(p i) c -> p i c", i=PACK))

        def load_opp(b, c):
            rows = opp[span(b * PASS, PASS), span(c * CHUNK, CHUNK)]
            nc.sync.dma_start(opp_chunk[b, c][:], rows.rearrange("(p i) j -> p i j", i=PACK))

        def load_opp_strip(b, c, u):
            rows = opp[span(b * PASS, PASS), span(c * CHUNK + u * STRIP, STRIP)]
            nc.sync.dma_start(opp_strip[b, c, u][:], rows.rearrange("(p i) j -> p i j", i=PACK))

        def load_w2(pair):
            words = w2_words[:, :, span(pair * N, N)].rearrange("a p c -> p a c")
            nc.sync.dma_start(w2_w[pair][:].bitcast(I32), words.bitcast(I32))

        def load_state(n):
            nc.sync.dma_start(state[n][:], gT[span(n * P, P), :])

        load_tab(0)
        nc.sync.dma_start(offsets[:], offs)
        for q in range(4):
            queue = nc.sync if q < 2 else nc.scalar
            queue.dma_start(
                tab_s[32 * q : 32 * q + 8, :].bitcast(I32),
                tab_scales[:, 4 * q : 4 * q + 4, :].bitcast(I32),
            )
        load_w1(0, 0)
        load_tab(1)
        load_w1(1, 0)
        load_w1(0, 1)
        load_w1(1, 1)
        load_opp_strip(0, 0, 0)
        load_state(0)
        load_opp_strip(0, 0, 1)
        load_opp(1, 0)
        nc.sync.dma_start(plan_rows[0:ROW_TILES, :], plan.rearrange("(n p) -> n p", p=P))
        load_state(1)
        load_opp_strip(0, 1, 0)
        for r in range(4):
            nc.sync.dma_start(
                w2_s[r:P:32, :, :].bitcast(I32),
                w2_scales[:, r:16:4, :].rearrange("a q n -> q a n").bitcast(I32),
            )
        load_w2(0)
        load_opp_strip(0, 1, 1)
        load_w2(1)
        load_opp(1, 1)
        load_state(2)
        load_opp(0, 2)
        load_opp_strip(1, 2, 0)
        load_state(3)
        load_opp_strip(1, 2, 1)
        load_opp(0, 3)
        load_opp(1, 3)

        plan_turned = bank([P, P], 7, "plan_turned")
        nc.tensor.transpose(plan_turned[:], plan_rows[:], identity[:])
        nc.scalar.copy(plan_sb[:], plan_turned[:, 0:ROW_TILES])

        v_s = held([P, S], U8, "v_s")
        v_w = {}

        def pick_words(a, first, count, slot=None):
            words = spot([P, count], f"v_w{a}_{first}", slot, U32)
            nc.vector.tensor_copy(words[:], tab_w[a][:].bitcast(U32).indirect(entries(first, count)))
            for u in range(count // STRIP):
                v_w[a, first // STRIP + u] = words[:, span(u * STRIP, STRIP)]

        w1_w, w1_s = {}, {}

        def prepare_w1(a, b, on_vector):
            grouped = spot([P, PASS * PACK], f"w1_grouped{a}{b}", None, BF16)
            into = grouped[:].rearrange("p (u e m i) -> p u m i e", u=2, e=2, i=PACK)
            source = w1_raw[a, b][:].rearrange("p i (m u e) -> p u m i e", u=2, e=2)
            if on_vector > 0:
                nc.vector.tensor_copy(into[:, :, :on_vector], source[:, :, :on_vector])
            if on_vector < P:
                nc.scalar.copy(into[:, :, on_vector:], source[:, :, on_vector:])
            w1_w[a, b] = held([P, PASS], U32, f"w1_w{a}{b}")
            w1_s[a, b] = held([P, PASS], U8, f"w1_s{a}{b}")
            nc.vector.quantize_mx(out=w1_w[a, b][:].bitcast(FP8X4), scales=w1_s[a, b][:], in_=grouped[:])

        def separation(b, c, u, index):
            sep = bank([P, PACK, STRIP], index, "sep")
            for a in range(2):
                for i in range(PACK):
                    m = span(i * P, P)
                    nc.tensor.matmul_mx(
                        out=sep[:, i, :],
                        lhsT=w1_w[a, b][:, m].bitcast(FP8X4),
                        lhsT_scale=w1_s[a, b][:, m],
                        rhs=v_w[a, 2 * c + u].bitcast(FP8X4),
                        rhs_scale=v_s[4 * a : P, span(c * CHUNK + u * STRIP, STRIP)],
                        start=a + i == 0,
                        stop=a + i == PACK,
                    )
            return sep

        decay = {}

        def in_runs(tile):
            return tile[:].rearrange("p i c -> p (i c)").rearrange("p (c i e) -> p c i e", i=PACK, e=RUN)

        def strip_in_runs(tile, u):
            return in_runs(tile)[:, span(u * STRIP // RUN, STRIP // RUN)]

        def second_strip_in_planes(tile):
            return tile[:].rearrange("p i c -> p (i c)").rearrange("p (u i c) -> p u i c", u=2, i=PACK)[:, 1]

        def make_size(b, c, banks, last_for_vector=False):
            size = decay[b, c] = spot([P, PACK, CHUNK], f"size{b}{c}")
            for u in range(2):
                sep = separation(b, c, u, banks[u])
                if last_for_vector and u == 1:
                    nc.scalar.activation(second_strip_in_planes(size), sep[:], ACT.Abs)
                else:
                    nc.scalar.activation(strip_in_runs(size, u), sep[:].rearrange("p i (c e) -> p c i e", e=RUN), ACT.Abs)

        def make_decay(b, c, slot=None):
            size = decay[b, c]
            if slot is not None or f"decay{b}{c}" in PLACED:
                decay[b, c] = spot([P, PACK, CHUNK], f"decay{b}{c}", slot)
            nc.scalar.activation(decay[b, c][:], size[:], ACT.Exp, scale=-1.0)

        def make_decay_by_strips(b, c, banks):
            size = held([P, PACK, CHUNK], F32, f"size{b}{c}")
            decay[b, c] = held([P, PACK, CHUNK], F32, f"decay{b}{c}")
            for u in range(2):
                sep = separation(b, c, u, banks[u])
                strip = span(u * STRIP, STRIP)
                nc.scalar.activation(size[:, :, strip], sep[:], ACT.Abs)
                nc.scalar.activation(decay[b, c][:, :, strip], size[:, :, strip], ACT.Exp, scale=-1.0)

        grouped_z, codes, scales = {}, {}, {}

        def open_z(name, first, count):
            tile = spot([P, 2, count * CHUNK * PACK], name, None, BF16)
            for k in range(count):
                for b in range(2):
                    grouped_z[b, first + k] = tile[:, b, span(k * CHUNK * PACK, CHUNK * PACK)]
            return tile

        def z_on_vector(b, c, u, discount, weights):
            nc.vector.tensor_tensor(
                grouped_z[b, c][:, span(u * PASS, PASS)].rearrange("p (c e i) -> p c i e", e=2, i=PACK),
                discount.rearrange("p i (c e) -> p c i e", e=2),
                weights.rearrange("p i (c e) -> p c i e", e=2),
                ALU.mult,
            )

        def z_in_runs(engine, into, discount, weights):
            engine.tensor_tensor(
                into.rearrange("p (c e i) -> p c i e", e=RUN, i=PACK),
                discount,
                weights.rearrange("p i (c e) -> p c i e", e=RUN),
                ALU.mult,
            )

        def z_chunk(b, c):
            z_in_runs(nc.gpsimd, grouped_z[b, c], in_runs(decay[b, c]), opp_chunk[b, c][:])

        def z_strip(b, c, u, engine=nc.gpsimd):
            into = grouped_z[b, c][:, span(u * PASS, PASS)]
            z_in_runs(engine, into, strip_in_runs(decay[b, c], u), opp_strip[b, c, u][:])

        def quantize_z(tile, first, count):
            codes[first] = held([P, 2, count * CHUNK], U32, f"z_w{first}")
            scales[first] = held([P, 2, count * CHUNK], U8, f"z_s{first}")
            nc.vector.quantize_mx(
                out=codes[first][:].rearrange("p b j -> p (b j)").bitcast(FP8X4),
                scales=scales[first][:].rearrange("p b j -> p (b j)"),
                in_=tile[:].rearrange("p b x -> p (b x)"),
            )

        def second_pass(into, n, b, first, count, start, stop):
            c = max(opened for opened in codes if opened <= first // CHUNK)
            cols = span(first - c * CHUNK, count)
            nc.tensor.matmul_mx(
                out=into,
                lhsT=w2_w[n // 2][:, b, span(2 * (n % 2) * P, 2 * P)].bitcast(FP4X4),
                lhsT_scale=w2_s[:, b, span(n * P, P)],
                rhs=codes[c][:, b, cols].bitcast(FP8X4),
                rhs_scale=scales[c][:, b, cols],
                start=start,
                stop=stop,
            )

        picked, gap, new = {}, {}, {}

        def pick(n, c, count, slot=None):
            picked[n, c] = spot([P, count * CHUNK], f"picked{n}{c}", slot)
            nc.vector.tensor_copy(picked[n, c][:], state[n][:].indirect(entries(c * CHUNK, count * CHUNK)))

        def pick_half(n, k, slot=None):
            picked[n, k] = held([P, HALF_REST], F32, f"picked{n}{k}", slot)
            nc.vector.tensor_copy(picked[n, k][:], state[n][:].indirect(entries(CHUNK + (k - 1) * HALF_REST, HALF_REST)))

        def difference(into, values, n):
            nc.scalar.activation(into, values, ACT.Identity, bias=plan_sb[:, n : n + 1], scale=-1.0)

        def add_plan(into, moved, n):
            nc.scalar.activation(into, moved, ACT.Identity, bias=plan_sb[:, n : n + 1])

        def make_gap(n, c, count, source, slot=None):
            tile = spot([P, count * CHUNK], f"gap{n}{c}", slot)
            difference(tile[:], picked[n, source][:, span((c - source) * CHUNK, count * CHUNK)], n)
            for k in range(count):
                gap[n, c + k] = (tile, k)

        def make_gap_of_halves(n):
            tile = spot([P, 2 * HALF_REST], f"gap{n}1")
            difference(tile[:, 0:HALF_REST], picked[n, 1][:], n)
            difference(tile[:, HALF_REST:], picked[n, 2][:], n)
            for k in range(CHUNKS - 1):
                gap[n, 1 + k] = (tile, k)

        def first_steps(tiles, index):
            step = bank([P, len(tiles), CHUNK], index, "step")
            for k, n in enumerate(tiles):
                for u in range(2):
                    for b in range(2):
                        into = step[:, k, span(u * STRIP, STRIP)]
                        second_pass(into, n, b, u * STRIP, STRIP, k + u + b == 0, k + u + b == len(tiles) + 1)
            return step

        def product_on_vector(c, n, step, slot=None):
            tile, k = gap[n, c]
            moved = spot([P, CHUNK], f"moved{c}{n}", slot)
            nc.vector.scalar_tensor_tensor(moved[:], step, -1.0, tile[:, span(k * CHUNK, CHUNK)], ALU.add, ALU.mult)
            return moved[:]

        def sum_apart(c, n, moved, slot=None):
            new[c, n] = spot([P, CHUNK], f"new{c}{n}", slot)[:]
            add_plan(new[c, n], moved, n)

        def later_step(c, n, count, index):
            first, width = c * CHUNK, count * CHUNK
            step = bank([P, width], index, "step")
            run = PASS if (c, count) == (1, 2) else STRIP
            for u in range(width // run):
                for b in range(2):
                    last = u == width // run - 1 and b == 1
                    second_pass(step[:, span(u * run, run)], n, b, first + u * run, run, u + b == 0, last)
            return step

        def open_update(c, n, count, index, slot=None):
            step = later_step(c, n, count, index)
            moved = spot([P, count * CHUNK], f"moved{c}{n}", slot)
            nc.scalar.activation(moved[:], step[:], ACT.Copy, bias=-1.0)
            new[c, n] = moved[:]

        def multiply(c, n):
            moved = new[c, n]
            tile, k = gap[n, c]
            nc.gpsimd.tensor_tensor(moved, moved, tile[:, span(k * CHUNK, moved.shape[1])], ALU.mult)

        def close_update(c, n):
            multiply(c, n)
            add_plan(new[c, n], new[c, n], n)

        def update(c, n, count, index, slot=None):
            open_update(c, n, count, index, slot)
            close_update(c, n)

        def put(c, n):
            count = new[c, n].shape[1]
            nc.vector.tensor_copy(state[n][:].indirect(entries(c * CHUNK, count)), new[c, n])

        def store(n):
            nc.sync.dma_start(out[span(n * P, P), :], state[n][:])

        pick_words(0, 0, S)
        nc.vector.tensor_copy(v_s[:], tab_s[:].indirect(offsets[:]))
        pick_words(1, 0, CHUNK)
        prepare_w1(0, 0, 0)
        pick_words(1, CHUNK, S - CHUNK, "w1_grouped00")
        prepare_w1(1, 0, VECTOR_SHARE)
        make_size(0, 0, (0, 1))
        make_decay(0, 0)
        prepare_w1(0, 1, P)
        make_size(0, 1, (2, 3))
        prepare_w1(1, 1, P)
        make_decay_by_strips(1, 0, (0, 1))
        make_decay(0, 1, "size10")
        z_first = open_z("z_first", 0, 1)
        z_strip(0, 0, 0, nc.vector)
        z_strip(0, 0, 1)
        pick(0, 0, CHUNKS)
        for u in range(2):
            cols = span(u * STRIP, STRIP)
            z_on_vector(1, 0, u, decay[1, 0][:, :, cols], opp_chunk[1, 0][:, :, cols])
        quantize_z(z_first, 0, 1)
        make_size(1, 1, (0, 1))
        z_middle = open_z("z_middle", 1, 2)
        for u in range(2):
            z_strip(0, 1, u)

        make_gap(0, 0, 1, 0)
        pick(1, 0, 1)
        make_gap(1, 0, 1, 0)
        make_decay(1, 1, "picked10")
        z_chunk(1, 1)
        pick_half(1, 2)
        step = first_steps((0, 1), 4)
        moved = [product_on_vector(0, 0, step[:, 0, :]), product_on_vector(0, 1, step[:, 1, :], "decay10")]
        sum_apart(0, 0, moved[0])
        pick_half(1, 1, "gap00")
        put(0, 0)
        make_size(0, 2, (0, 1))
        make_decay(0, 2)
        z_chunk(0, 2)
        make_size(1, 2, (0, 1))

        pick(2, 0, 1)
        make_gap(2, 0, 1, 0)
        pick(2, 1, CHUNKS - 1, "opp10")
        moved.append(product_on_vector(0, 2, first_steps((2,), 5)[:, 0, :]))
        sum_apart(0, 1, moved[1])
        make_decay(1, 2)
        for u in range(2):
            z_strip(1, 2, u)
        put(0, 1)
        sum_apart(0, 2, moved[2])
        put(0, 2)
        make_size(0, 3, (0, 1))
        early, late = in_runs(decay[0, 3])[:, : EARLY // RUN], in_runs(decay[0, 3])[:, EARLY // RUN :]
        nc.scalar.activation(early, early, ACT.Exp, scale=-1.0)
        make_gap(0, 1, 3, 0)

        pick(3, 0, 1)
        make_gap(3, 0, 1, 0)
        pick(3, 1, 1)
        moved.append(product_on_vector(0, 3, first_steps((3,), 7)[:, 0, :], "gap20"))
        make_gap_of_halves(1)
        quantize_z(z_middle, 1, 2)
        pick(3, 2, 2, "opp121")
        later_gaps = spot([P, 2 * HALF_REST], "gap21")
        for k in range(CHUNKS - 1):
            gap[2, 1 + k] = (later_gaps, k)
        difference(later_gaps[:, 0:HALF_REST], picked[2, 1][:, 0:HALF_REST], 2)
        sum_apart(0, 3, moved[3])
        difference(later_gaps[:, HALF_REST:], picked[2, 1][:, HALF_REST:], 2)
        second = product_on_vector(1, 0, later_step(1, 0, 1, 4)[:])
        put(0, 3)
        z_last = open_z("z_last", 3, 1)
        z_in_runs(nc.gpsimd, grouped_z[0, 3][:, : EARLY * PACK], early, opp_chunk[0, 3][:, :, :EARLY])

        open_update(1, 1, 1, 6)
        sum_apart(1, 0, second, "w1_raw00")
        put(1, 0)
        open_update(2, 0, 1, 2, "gap00")
        open_update(1, 2, 2, 5, "w1_raw01")
        multiply(1, 1)
        sum_apart(1, 1, new[1, 1])
        put(1, 1)
        close_update(2, 0)
        put(2, 0)
        multiply(1, 2)
        late_strip = spot([P, (CHUNK - EARLY) // RUN, PACK, RUN], "late_strip")
        nc.scalar.activation(late_strip[:], late, ACT.Exp, scale=-1.0)
        z_in_runs(nc.gpsimd, grouped_z[0, 3][:, EARLY * PACK :], late_strip[:], opp_chunk[0, 3][:, :, EARLY:])
        make_size(1, 3, (0, 1))
        open_update(2, 1, 1, 3, "tab_w0")
        multiply(2, 1)
        make_decay(1, 3, "w1_raw10")
        add_plan(new[1, 2], new[1, 2], 2)
        put(1, 2)
        z_chunk(1, 3)
        quantize_z(z_last, 3, 1)

        sum_apart(2, 1, new[2, 1], "opp13")
        put(2, 1)
        last_gaps = held([P, 3 * CHUNK], F32, "gap31", "w1_raw00")
        difference(last_gaps[:, 0:CHUNK], picked[3, 1][:], 3)
        difference(last_gaps[:, CHUNK:], picked[3, 2][:], 3)
        for k in range(CHUNKS - 1):
            gap[3, 1 + k] = (last_gaps, k)
        update(1, 3, 1, 7)
        put(1, 3)
        for n in range(ROW_TILES - 1):
            update(3, n, 1, n, "tab_w1" if n == 0 else None)
            put(3, n)
            store(n)
        update(2, 3, 2, 3, "w1_raw11")
        put(2, 3)
        store(3)
